import numpy as np, ml_dtypes
CORES = [66,74,82,90,194,202,210,218]
N = 8
BF = ml_dtypes.bfloat16
def gentries(a):
    return np.ascontiguousarray(a.reshape(8, 16, -1).transpose(0, 2, 1)).reshape(8, -1)
def gtable(e):
    e = np.asarray(e); return np.ascontiguousarray(e.reshape(8, -1, 16).transpose(0, 2, 1)).reshape(128, -1).astype(np.int32)
V, GH, RO, DF, TR, FQ = 2048, 256, 7, 20, 7, 4
NS, NU = V // 16, V // 256; S = NS + NU + 1; W = V + (N - 1) * GH
LO, HI = DF + 2, 2 * DF + 1
SMALL = (0, 0, 1, 2, 3, 7, 14, 15, 16)
def parts(rng, share):
    x = rng.integers(LO, HI + 1, (N, 8, 16, V)); xb = rng.integers(LO, HI + 1, (N, 8, 16, V))
    a = np.where(rng.random((N, 8, V)) < share, rng.integers(V, W, (N, 8, V)), rng.integers(0, V, (N, 8, V)))
    return x, xb, a, np.zeros((N, 8, S), np.int64), np.full((N, 8, S), 16, np.int64)
def tame(a):
    k = np.where(a >= V, (a - V) % GH, 0)
    return np.where(a >= V, a - k + k % 14, np.where((a == 14) | (a == 15), 0, a))
def pack(x, xb, a, sg, lm):
    return {"x0": np.ascontiguousarray(x.reshape(N, 128, V)).astype(np.float32).astype(BF), "xi": np.ascontiguousarray(xb.reshape(N, 128, V)).astype(np.float32).astype(BF),
            "ad": np.stack([gtable(e) for e in a]), "sg": np.asarray(sg).astype(np.int32), "lm": np.asarray(lm).astype(np.int32)}
def lows(rng, x, xb, a, n):
    o = rng.permutation(V)[:n]; t = rng.choice(np.array([TR - 1, TR, TR + 1, 16, 16]), n)
    m = np.argsort(rng.random((16, n)), axis=0) < t
    x[:, o] = np.where(m, rng.integers(0, 4, (16, n)), x[:, o]); xb[:, o] = np.where(m, rng.integers(0, 4, (16, n)), xb[:, o])
    h = n // 2; a[o[:h]] = np.where(rng.random(h) < 0.5, o[:h], rng.permutation(o[:h]))
def trigger(rng, x, a, sg, lm):
    s = NS - 1 if rng.random() < 0.5 else int(rng.integers(1, NS))
    lm[:NS] = rng.choice(np.array([13, 14, 16]), NS); lm[s] = rng.integers(0, 5); lm[NS + s // 16] = 0; lm[S - 1] = 0
    for i in range(5):
        v = 16 * s + 3 * i; e = rng.integers(0, 4, 16)
        x[:, v + 2] = e; x[:, v + 1] = e + DF; x[:, v] = e + 2 * DF; a[v] = v + 1; a[v + 1] = v + 2; a[v + 2] = v + 2
    a[16 * s + 15] = 16 * s + 15
def plant(rng, x, xb, a, cr, mode, keep, near):
    x[:, 15] = 2; xb[:, 15] = 2; x[:, 14] = LO; xb[:, 14] = LO; a[14:16] = 15
    if mode == 2: x[:, 15] = LO; x[:, 14] = 1; xb[:, 14] = 1; a[14:16] = 14
    to = 14 if mode == 3 else 15
    o = np.flatnonzero(cr); n = len(o); t = rng.choice(np.array([TR, TR, TR + 1, 16]), n)
    st = np.where(np.argsort(rng.random((16, n)), axis=0) < t, rng.integers(LO + 1, HI + 1, (16, n)), LO)
    x[:, o] = st; xb[:, o] = st if keep else LO; a[o] = to
    o = rng.permutation(np.flatnonzero(~cr[16:]) + 16)[:near]; n = len(o)
    x[:, o] = np.where(np.argsort(rng.random((16, n)), axis=0) < TR - 1, rng.integers(LO + 1, HI + 1, (16, n)), LO); a[o] = to
    if mode == 2: xb[:, o] = x[:, o]
def strike(rng, x, a, lm, s, t):
    n = (1, 1, 2, 3, 5, 8, 13)[t - 1]
    a[(a >> 4) == s] = 0; v = 16 * s + np.arange(16); a[v] = v
    p = 16 * s + rng.permutation(16)[:n + 1]; e = rng.integers(0, 4, 16)
    x[:, p] = (e + DF)[:, None]; x[:, p[0]] = e + 2 * DF; x[:, p[n]] = e; a[p[:n]] = p[1:]
    lm[s] = 0; lm[NS + s // 16] = 0; lm[S - 1] = 0
def setup_inputs(rng):
    x, xb, a, sg, lm = parts(rng, 0.06); order = rng.permutation(N)
    mix = ((0.9, 0.07, 0.03), (0.75, 0.15, 0.1), (0.95, 0.03, 0.02), (0.6, 0.25, 0.15))
    for q in range(N):
        n = FQ if q == order[0] else FQ - 1 if q == order[1] else int(rng.integers(0, FQ - 1))
        weak = rng.permutation(8)[:n]
        for g in range(8):
            sg[q, g] = rng.choice(3, S, p=mix[int(rng.integers(0, 4))])
            lm[q, g, :NS] = rng.choice(np.array([3, 4, 6, 8, 10, 13, 16]), NS); lm[q, g, NS:NS + NU] = rng.choice(np.array([1, 2, 4, 8, 16]), NU)
            lows(rng, x[q, g], xb[q, g], a[q, g], (V // 512, V // 128, V // 64)[int(rng.integers(0, 3))])
            if np.any(weak == g): trigger(rng, x[q, g], a[q, g], sg[q, g], lm[q, g])
    return pack(x, xb, a, sg, lm)
def setup_inputs_spread(rng):
    x, xb, a, sg, lm = parts(rng, 0.12)
    x = np.minimum((np.exp2(6 * rng.random((N, 8, 1, V))) * rng.random((N, 8, 16, V))).astype(np.int64), 63)
    xb = np.minimum((np.exp2(6 * rng.random((N, 8, 1, V))) * rng.random((N, 8, 16, V))).astype(np.int64), 63)
    for q in range(N):
        o = rng.permutation(8); k = rng.permutation(8)[:FQ - 1]
        for i in range(8):
            g = int(o[i])
            if i % 2: a[q, g] = np.where(a[q, g] < V, (V * rng.random(V) ** 3).astype(np.int64), a[q, g])
            if i < 4: sg[q, g] = rng.choice(3, S, p=(0.97, 0.02, 0.01))
            else: sg[q, g] = rng.choice(3, S, p=(0.6, 0.25, 0.15)); lm[q, g, :S - 1] = rng.integers(0, 17, S - 1)
            if np.any(k == g): lm[q, g, S - 1] = rng.integers(0, 4)
    return pack(x, xb, a, sg, lm)
def setup_inputs_ends(rng):
    x, xb, a, sg, lm = parts(rng, 0.15)
    def both():
        t = rng.choice(np.array([0, 0, TR - 1, TR, TR + 1, 16, 16]), (N, 8, V, 1))
        return np.ascontiguousarray((63 * (np.argsort(rng.random((N, 8, V, 16)), axis=3) < t)).transpose(0, 1, 3, 2))
    x = both(); xb = both()
    u = rng.random((N, 8, V)); a = np.where(u < 0.36, 0, np.where(u < 0.72, W - 1, a))
    z = 63 * rng.integers(0, 2, (N, 8, 1)); z[:, 7] = 0; x[..., 0] = z; xb[..., 0] = z
    sg = 2 * (rng.random((N, 8, S)) < rng.choice(np.array([0.1, 0.5]), (N, 8, 1))).astype(np.int64)
    lm = 16 * (rng.random((N, 8, S)) < rng.choice(np.array([0.5, 0.9]), (N, 8, 1))).astype(np.int64)
    lm[..., S - 1] = 16; sg[..., S - 1] = 2 * (rng.random((N, 8)) < 0.25)
    x[:, 7, :, V - 16:] = 63; xb[:, 7, :, V - 16:] = 63; a[:, 7, V - 16:] = 0; a[:, 7, 0] = 0; lm[:, 7, NS - 1] = 16
    for q in range(N):
        k = rng.permutation(7)[:FQ if q == N - 1 else FQ - 1]
        for g in k:
            lm[q, g, S - 1] = 0
            if q == N - 1:
                lm[q, g, NS:NS + NU] = 0; x[q, g, :, 0] = 0; xb[q, g] = 0; xb[q, g, :, V - 16:] = 63
                u = rng.random(V); a[q, g] = np.where(u < 0.86, 0, np.where(u < 0.93, V - 1, rng.integers(0, V, V)))
                a[q, g, 0] = 0; a[q, g, V - 16:] = V - 1
    return pack(x, xb, a, sg, lm)
def pair(rng, die, top):
    if die:
        c = int(rng.integers(0, top)); return c, (top if rng.random() < 0.3 else c + 1)
    c = SMALL[int(rng.integers(0, 9))]; return c, min(c if rng.random() < 0.5 else 0, top)
def setup_inputs_corners(rng):
    x, xb, a, sg, lm = parts(rng, 0.05); a = tame(a); sg = rng.integers(0, 3, (N, 8, S)); order = rng.permutation(N); more = int(rng.integers(FQ + 1, 8))
    for i in range(N):
        q = int(order[i]); mode = (3, 1, 2, 3, 3, 1, 1, 2)[i]; o = rng.permutation(8); dg = o[:(FQ, FQ - 1, more, 0, 7, 8, FQ, FQ - 1)[i]]
        full = int(o[0]) if i in (0, 6) else -1; stay = int(o[FQ - 1]) if i in (1, 7) else -1; late = int(o[FQ]) if i == 1 else -1
        hit = i in (0, 2, 4, 5, 6)
        for k in range(8):
            g = int(o[k]); early = bool(np.any(dg == g)); die = early or g == late; cr = np.zeros(V, bool)
            wild = k in (5, 6); part = not (hit or die or wild or g == stay)
            when = 3 if i in (1, 7) and not early and g != stay else mode
            lm[q, g, S - 1], n = pair(rng, die, NU)
            if g == full: lm[q, g, S - 1] = NU - 1; n = NU
            elif g == stay: lm[q, g, S - 1] = 16 if rng.random() < 0.5 else NU; n = NU
            elif k == 7 and not die: n = 0
            du = rng.permutation(NU)[:n]
            for j in range(NU):
                top = 15 if j == 0 else 16
                lm[q, g, NS + j], n = pair(rng, bool(np.any(du == j)), top); ds = 16 - top + rng.permutation(top)[:n]
                for s in range(16 - top, 16):
                    lm[q, g, 16 * j + s], n = pair(rng, bool(np.any(ds == s)), 16)
                    cr[256 * j + 16 * s + rng.permutation(16)[:n]] = True
            if part and k == 7: cr[:] = False
            if wild: a[q, g] = np.where(a[q, g] == 13, 0, a[q, g])
            plant(rng, x[q, g], xb[q, g], a[q, g], cr, when, k == 5, 0 if part or (i == 1 and when == 1) else V // 32)
            if wild:
                x[q, g, :, 13] = LO if hit else HI; xb[q, g, :, 13] = HI; a[q, g, 13] = 15 if hit else 14
            elif g != stay:
                xb[q, g, :, 14 if when == 2 else 15] = LO
            if part and k < 7:
                m = ~cr & (a[q, g] < V); m[14:16] = False
                e = V + GH * rng.integers(0, N - 1, V) + rng.integers(0, 14, V)
                a[q, g] = np.where(m, np.where(rng.random(V) < 0.5, np.arange(V), e), a[q, g])
    return pack(x, xb, a, sg, lm)
def setup_inputs_crowd(rng):
    x, xb, a, sg, lm = parts(rng, 0.06); a = tame(a)
    for q in range(N):
        o = rng.permutation(8)
        for g in range(8):
            k = int(o[g]); cr = np.zeros(V, bool)
            if k in (0, 1): a[q, g] = V - 1
            if k == 4: a[q, g] = W - 1
            if k == 5: a[q, g] = rng.choice(np.array([0, V - 1, V, W - 1, 7]), V)
            if k in (1, 2, 3, 6):
                for j in range(NU):
                    c = int(rng.integers(0, 4)); lm[q, g, 16 * j:16 * j + 16] = (15, 14, 15, 16)[c]
                    if c == 2: lm[q, g, 16 * j + int(rng.integers(0, 16))] = 16
                lm[q, g, NS:NS + NU] = rng.choice(np.array([14, 15, 16]), NU); lm[q, g, S - 1] = (0, NU // 2, NU - 1)[int(rng.integers(0, 3))]
                sg[q, g] = rng.integers(0, 3, S)
            if k == 1:
                cr[V - 2] = True; sg[q, g, NS - 1] = 2; lm[q, g, NS - 1] = 16
            if k in (2, 3, 6): cr[:] = True; cr[14:16] = False
            if k == 3: s = np.arange(1, NS, 2); cr[16 * s + rng.integers(0, 16, len(s))] = False
            if k == 6: cr[int(rng.integers(16, V))] = False
            if k in (1, 2, 3, 6): plant(rng, x[q, g], xb[q, g], a[q, g], cr, 1 if k in (2, 3) else 3, k == 3, 0)
    return pack(x, xb, a, sg, lm)
def setup_inputs_calm(rng):
    x, xb, a, sg, lm = parts(rng, 0.04); a = tame(a)
    late = (5, min(RO - 1, 7))[:RO - 5]; hit = rng.permutation(N)[:len(late)]
    for q in range(N):
        o = rng.permutation(8); used = np.zeros((8, NS), bool)
        for g in range(8):
            k = int(o[g])
            if k == 0: continue
            sup = 1 + rng.permutation(NS - 2)[:NS // 10]; sup[0] = NS - 1; c1 = np.zeros(V, bool); c3 = np.zeros(V, bool)
            used[g, sup] = True
            for j in range(len(sup)):
                s = int(sup[j]); n = 1 + j % 3; w = 16 * s + rng.permutation(16)[:n]
                if k in (1, 4, 6) or (k == 3 and (j >> 1) & 1): c1[w] = True
                else: c3[w] = True
                sg[q, g, s] = 2 if k == 4 else (2, 1, 0, 2, 1)[j % 5]
                if k in (6, 7): lm[q, g, s] = n - 1 + ((j // 3) & 1)
            if k == 6: lm[q, g, NS:NS + NU] = rng.integers(0, 4, NU); sg[q, g, NS:NS + NU] = rng.integers(0, 3, NU)
            if np.any(c1): plant(rng, x[q, g], xb[q, g], a[q, g], c1, 1, k in (4, 6), 0)
            if np.any(c3): plant(rng, x[q, g], xb[q, g], a[q, g], c3, 3, k == 5, 0)
        for i in range(len(late)):
            if int(hit[i]) != q: continue
            for g in range(8):
                if int(o[g]) >= FQ: continue
                s = int(rng.choice(np.flatnonzero(~used[g, GH // 16:]) + GH // 16))
                strike(rng, x[q, g], a[q, g], lm[q, g], s, late[i])
    return pack(x, xb, a, sg, lm)
def check_inputs(d):
    bad = []
    for k, lo, hi in (("x0", 0, 63), ("xi", 0, 63), ("ad", 0, W - 1), ("sg", 0, 2), ("lm", 0, 16)):
        v = np.asarray(d[k]).astype(np.float64)
        if not np.all((v >= lo) & (v <= hi) & (v == np.rint(v))): bad.append("range of " + k)
    return bad
def judge(c, s, m):
    n = np.add.reduce(c.astype(np.int64), axis=-1); die = n > m
    rest = np.add.accumulate(c.astype(np.int64), axis=-1) > 0
    b = np.where((s == 0)[..., None], c, np.where((s == 1)[..., None], rest, (n > 0)[..., None]))
    return b | die[..., None], die
def reference(x0, xi, ad, sg, lm):
    x = x0.astype(np.float32).astype(np.int16).reshape(N, 8, 16, V); xb = xi.astype(np.float32).astype(np.int16).reshape(N, 8, 16, V)
    a0 = np.stack([gentries(e) for e in ad]).astype(np.int64)
    s = sg.astype(np.int64); m = lm.astype(np.int64)
    a = a0; c = np.zeros_like(a0)
    u = np.full_like(a0, -1); w = np.zeros_like(a0)
    inc = np.ones_like(a0)
    for step in range(RO):
        seen = []
        for r in range(N):
            p = [x[r]]
            for d in range(1, N):
                q = (r - d) % N; p.append(x[q][(np.arange(8) + q - r) & 7][:, :, :GH])
            seen.append(np.concatenate(p, axis=2))
        y = np.take_along_axis(np.stack(seen), a[:, :, None, :], 3)
        own = a < V; ao = np.minimum(a, V - 1)
        ia = np.where(own, np.take_along_axis(inc, ao, 2), 0)
        crash = ((c > 0) & (c != ia)) | (np.add.reduce((y < x - DF).astype(np.int64), axis=2) >= TR)
        ua = np.take_along_axis(u, ao, 2); uc = np.take_along_axis(w, ao, 2); got = own & (ua >= 0)
        na = np.where(got, ua, a); nc = np.where(got, uc, c)
        b1, d1 = judge(crash.reshape(N, 8, NS, 16), s[:, :, :NS], m[:, :, :NS])
        b2, d2 = judge(d1.reshape(N, 8, NU, 16), s[:, :, NS:NS + NU], m[:, :, NS:NS + NU])
        b3, d3 = judge(d2.reshape(N, 8, 1, NU), s[:, :, S - 1:], m[:, :, S - 1:])
        rank = np.add.reduce(d3[:, :, 0].astype(np.int64), axis=1) >= FQ
        born = b1 | b2.reshape(N, 8, NS)[..., None] | np.repeat(b3[:, :, 0], 16, axis=2)[..., None] | rank[:, None, None, None]
        born = born.reshape(N, 8, V)
        x = np.where(born[:, :, None], xb, np.maximum(x, y))
        u = np.where(born, -1, a); w = np.where(born, 0, ia)
        a = np.where(born, a0, na); c = np.where(born, 0, nc)
        inc = inc + born
    return {"yx": np.ascontiguousarray(x.reshape(N, 128, V)).astype(np.float32).astype(BF), "ya": np.stack([gtable(e) for e in 16 * a + c]).astype(np.float32),
            "yu": np.stack([gtable(e) for e in np.where(u < 0, -1, 16 * u + w)]).astype(np.float32), "yi": np.stack([gtable(e) for e in inc]).astype(np.float32)}

@@ -1,0 +1,512 @@
+from concourse.bass import DstId, RemoteDMATransfer
+from concourse.mybir import AluOpType, ActivationFunctionType
+
+N, V, GH, RO = 8, 2048, 256, 7
+WW = V + (N - 1) * GH
+EARLY = False
+NH = 2
+GS = 5
+SEL0 = "s"
+XMS = (0,)
+LTC = [(0, 128)]
+LS = 0
+GTC = [(0, 96), (96, 128)]
+SAME_WAR = False
+INC_ALL = False
+CUTS = [0, 256, 1024, 2048]
+KK = 32768.0
+TH, TL, TW, TB_, TG, TO, TS = 0, 1, 2, 3, 4, 5, 6
+XI = RO
+ORDER = [0, XI] + list(range(1, RO)) if EARLY else list(range(RO))
+
+B, F = "bfloat16", "float32"
+SCRATCH = {
+    "W0": ("sbuf", [128, WW], B), "W1": ("sbuf", [128, WW], B), "W2": ("sbuf", [128, WW], B),
+    "MX": ("sbuf", [128, 2 * V], B), "xm": ("sbuf", [128, V], B), "xc": ("sbuf", [128, V], B), "lt": ("sbuf", [128, V], B), "G": ("sbuf", [128, V], B),
+    "TB": ("sbuf", [128, V + 16], B), "WD": ("sbuf", [128, 512], B),
+    "DI": ("sbuf", [128, 384], "int32"), "HB": ("sbuf", [128, 384], B), "bn": ("sbuf", [128, RO * 128], B),
+    "GG": ("sbuf", [128, 3 * V if EARLY else 16], B),
+    "msg": ("sbuf", [128, RO * 16], "uint16"), "og": ("sbuf", [128, RO * 112], "uint16"),
+    "adi": ("sbuf", [128, 128], "int32"), "adt": ("sbuf", [128, 256], "int32"), "adb": ("sbuf", [128, 256], B),
+    "oa0": ("sbuf", [128, 128], "uint16"), "oa1": ("sbuf", [128, 128], "uint16"),
+    "ot": ("sbuf", [128, 128], "uint16"), "osel": ("sbuf", [128, 128], "uint16"),
+    "sl": ("sbuf", [128, 288], "int32"), "slb": ("sbuf", [128, 288], B), "t1": ("sbuf", [128, 16], B),
+    "v1": ("sbuf", [128, 128], B), "v2": ("sbuf", [128, 128], B), "v3": ("sbuf", [128, 128], B),
+    "vk": ("sbuf", [128, 128], B), "vi": ("sbuf", [128, 128], B),
+    "I1": ("sbuf", [128, 144], B), "I16": ("sbuf", [128, 144], B), "I128": ("sbuf", [128, 128], B),
+    "I1920": ("sbuf", [128, 128], B), "IS0": ("sbuf", [128, 144], B), "IS1": ("sbuf", [128, 144], B), "IF": ("sbuf", [128, 128], F),
+    "BLK": ("sbuf", [128, 128], B), "TRI": ("sbuf", [128, 128], B), "PRE3": ("sbuf", [128, 128], B),
+    "ON16": ("sbuf", [128, 128], B), "E2": ("sbuf", [128, 128], B), "E3": ("sbuf", [128, 128], B),
+    "LE": ("sbuf", [128, 128], B), "GE": ("sbuf", [128, 128], B), "tc1": ("sbuf", [128, 128], B), "tc2": ("sbuf", [128, 128], B),
+    "tc3": ("sbuf", [128, 128], B),
+    "ys": ("sbuf", [128, 512], B), "IN": ("sbuf", [128, 128], B), "SELC": ("sbuf", [128, 16], B), "SELM": ("sbuf", [128, 32], B), "wc": ("sbuf", [128, 8], F),
+    "LIM": ("sbuf", [128, 56], F), "ne": ("sbuf", [128, 32], F), "mul": ("sbuf", [128, 8], F), "nL3": ("sbuf", [128, 8], B),
+    "M1": ("sbuf", [128, 128], B), "M2": ("sbuf", [128, 128], B), "IK": ("sbuf", [128, 128], B), "IK32": ("sbuf", [128, 128], B),
+    "ONK": ("sbuf", [128, 128], B), "d1": ("sbuf", [128, 8], B), "f1": ("sbuf", [128, 8], B), "l2": ("sbuf", [128, 32], B),
+    "d3": ("sbuf", [128, 8], F),
+    "jb": ("sbuf", [128, 128], B), "nb": ("sbuf", [128, 128], B), "qb": ("sbuf", [128, 128], B),
+    "r8": ("sbuf", [128, 8], F), "z8": ("sbuf", [128, 8], F), "ok": ("sbuf", [128, 128], B), "wl": ("sbuf", [128, 128], B),
+    "A0": ("sbuf", [128, 128], "int32"), "A": ("sbuf", [128, 128], "int32"),
+    "D1": ("sbuf", [128, 128], F), "D2": ("sbuf", [128, 128], F), "EB": ("sbuf", [128, 128], F),
+    "fi": ("sbuf", [128, 128], "int32"), "PX": ("sbuf", [128, 128], F), "DW": ("sbuf", [128, 256], F),
+    "YO": ("sbuf", [128, 256], F), "YI": ("sbuf", [128, 128], F), "a0w": ("sbuf", [128, 128], F),
+    "hl": ("sbuf", [128, (RO + 1) * GH if NH else 16], B),
+}
+PSUMS = ("P0", "P1", "P2", "P3", "PC", "PM", "PO", "PL")
+for _p in PSUMS:
+    SCRATCH[_p] = ("psum", [128, 512], F)
+SEMAPHORES = (["qv", "qs", "qt", "qg"] + ["dm%d" % k for k in range(48)]
+              + [a + str(t) for a in ("ar", "ls", "ha", "sm", "lo") for t in range(RO + 1)])
+
+
+def bits(m):
+    return bin(m).count("1")
+
+
+def helper_of(core, T, topo):
+    for c in topo.cores_of(core):
+        if T.rank_of(c) is None and topo.die(c) != topo.die(core) and all(topo.may_write(c, d) for d in T.cores):
+            return c
+    return None
+
+
+def split_dests(r, j, T, topo):
+    me = T.cores[r]
+    others = [(r + d) % N for d in range(1, N)]
+    far = [q for q in others if not topo.same_plane(me, T.cores[q]) and not topo.mates(me, T.cores[q])]
+    far += [q for q in others if topo.mates(me, T.cores[q])]
+    via = far[:0 if EARLY and j == 0 else NH]
+    return [q for q in others if q not in via], via
+
+
+def ghost_slot(T, t, src, dst):
+    d = (dst - src) % N
+    if EARLY and t:
+        a = (V if t == XI else 2 * V * ((t - 1) % 2)) + src * GH
+        return T.GG[:, a:a + GH]
+    return T["W%d" % (t % 3)][:, V + (d - 1) * GH:V + d * GH]
+
+
+def dst_ids(cores, src, topo):
+    return [DstId(rid=a[0], pnc=a[1]) for a in [topo.addr(c, src) for c in cores]]
+
+
+def helper_program(g, core, r, T, topo):
+    off = topo.mask(core, T.cores[(r + 1) % N])
+    on = topo.mask(T.cores[r], core) & ~off
+    todo = [t for t in ORDER if split_dests(r, t, T, topo)[1]]
+    for t in todo:
+        via = split_dests(r, t, T, topo)[1]
+        g.wait_ge(T.sem["ha%d" % t], bits(on))
+        g.remote_dma_fused([RemoteDMATransfer(dst_ids=dst_ids([T.cores[q] for q in via], core, topo), dma_engine_mask=off,
+                                              remote_sem=T.sem["ar%d" % t], srcs=[T.hl[:, t * GH:(t + 1) * GH]],
+                                              dsts=[ghost_slot(T, t, r, q) for q in via])], local_sem=T.sem["ls%d" % t])
+    for t in todo:
+        g.wait_ge(T.sem["ls%d" % t], bits(off))
+
+
+def emit(g, T, ops):
+    queue = {"v": g.vector, "s": g.scalar, "t": g.tensor, "g": g, "y": g.sync}
+    clock = {e: {} for e in queue}
+    seq = {e: 0 for e in queue}
+    lastw, readers, need = {}, {}, set()
+    for o in ops:
+        e = o["eng"]
+        if e is None:
+            for k in o["w"]:
+                lastw[k] = (o["ev"][0], o["ev"][1], {})
+                readers[k] = []
+            continue
+        deps = []
+        for k in o["r"]:
+            if k in lastw and not (e == "t" and lastw[k][0] == e): deps.append(lastw[k])
+        for k in o["w"]:
+            for ev in ([lastw[k]] if k in lastw else []) + readers.get(k, []):
+                if ev[0] == e and (e == "t" or k in PSUMS or not SAME_WAR): continue
+                deps.append(ev)
+        best = {}
+        for ev in deps:
+            if ev[1] > best.get(ev[0], (0, 0))[1]: best[ev[0]] = ev
+        waits = []
+        evs = list(best.values())
+        for ev in evs:
+            if any(x is not ev and x[2].get(ev[0], 0) >= ev[1] for x in evs): continue
+            if clock[e].get(ev[0], 0) < ev[1]:
+                waits.append((ev[0], ev[1]))
+        for ev in evs:
+            for s, v in list(ev[2].items()) + [(ev[0], ev[1])]:
+                if clock[e].get(s, 0) < v: clock[e][s] = v
+        o["waits"] = waits
+        for w in waits: need.add(w)
+        if o["ev"] is None:
+            seq[e] += 1
+            ev = (e, seq[e], dict(clock[e]))
+            o["seq"] = seq[e]
+        else:
+            ev = (o["ev"][0], o["ev"][1], dict(clock[e]))
+        for k in o["r"]: readers.setdefault(k, []).append(ev)
+        for k in o["w"]:
+            lastw[k] = ev
+            readers[k] = []
+    count, value = {e: 0 for e in queue}, {}
+    for o in ops:
+        if o["eng"] is not None and o["ev"] is None and (o["eng"], o["seq"]) in need:
+            count[o["eng"]] += len(o["fn"]) if INC_ALL else 1
+            value[(o["eng"], o["seq"])] = count[o["eng"]]
+    left = {}
+    for o in ops:
+        e = o["eng"]
+        if o["ev"] is not None: left[o["ev"][0]] = (o["ev"][1], e if e in ("s", "y") else "g")
+        if e is None: continue
+        for s, v in o["waits"]:
+            if s in queue: queue[e].wait_ge(T.sem["q" + s], value[(s, v)])
+            else: queue[e].wait_ge(T.sem[s], v)
+        for j, f in enumerate(o["fn"]):
+            ins = f()
+            if o["ev"] is None:
+                if (e, o["seq"]) in need and (INC_ALL or j == len(o["fn"]) - 1): ins.then_inc(T.sem["q" + e], 1)
+            elif o["dma"]:
+                ins.then_inc(T.sem[o["ev"][0]], 16)
+    for s, (v, e) in left.items():
+        if (s, v) not in need: queue[e].wait_ge(T.sem[s], v)
+
+
+def rank_program(g, core, T, topo):
+    r = T.rank_of(core)
+    if r is None:
+        if NH:
+            for q in range(N):
+                if helper_of(T.cores[q], T, topo) == core: helper_program(g, core, q, T, topo)
+        return
+    Op, AF = AluOpType, ActivationFunctionType
+    vec, act, pe = g.vector, g.scalar, g.tensor
+    ops, ndma = [], [0]
+
+    def op(eng, fn, r_=(), w=()):
+        rd = [k for k in r_ if k not in PSUMS]
+        wr = list(w) + [k for k in r_ if k in PSUMS]
+        ops.append({"eng": eng, "fn": fn if isinstance(fn, list) else [fn], "r": rd, "w": wr, "ev": None, "dma": False})
+
+    def dma(eng, pairs, r_=(), w=()):
+        q = {"s": act, "y": g.sync}[eng]
+        s = "dm%d" % ndma[0]
+        ndma[0] += 1
+        ops.append({"eng": eng, "fn": [(lambda o=o, i=i: q.dma_start(o, i)) for o, i in pairs], "r": list(r_), "w": list(w),
+                    "ev": (s, 16 * len(pairs)), "dma": True})
+
+    def rot(sb, dr, cs, cd, unit=16, load=True):
+        n, k = 8 * unit, r * unit
+        parts = [(slice(0, n - k), slice(k, n))] + ([(slice(n - k, n), slice(0, k))] if k else [])
+        return [((sb[a, cs], dr[b, cd]) if load else (dr[b, cd], sb[a, cs])) for a, b in parts]
+
+    def tt(out, a, b, o, r_, w): op("v", lambda: vec.tensor_tensor(out, a, b, o), r_, w)
+    def ts(out, a, s1, o1, r_, w, s2=None, o2=None):
+        if o2 is None: op("v", lambda: vec.tensor_scalar(out, a, s1, None, o1), r_, w)
+        else: op("v", lambda: vec.tensor_scalar(out, a, s1, s2, o1, o2), r_, w)
+    def cp(out, a, r_, w): op("v", lambda: vec.tensor_copy(out, a), r_, w)
+    def ms(out, c, w, r_=()): op("v", lambda: vec.memset(out, c), r_, w)
+    def mm(lst, r_, w): op("t", [(lambda a=a: pe.matmul(*a)) for a in lst], r_, w)
+    def sc(out, a, r_, w, **kw): op("s", lambda: act.activation(out, a, AF.Identity, **kw), r_, w)
+    def scan(out, a, b, init, o0, o1, r_, w): op("v", lambda: vec.tensor_tensor_scan(out, a, b, init, o0, o1), r_, w)
+
+    off = topo.mask(core, T.cores[(r + 1) % N])
+
+    def small(t):
+        tr = RemoteDMATransfer(dst_ids=dst_ids([T.cores[(r + d) % N] for d in range(1, N)], core, topo), dma_engine_mask=off,
+                               remote_sem=T.sem["sm%d" % t], srcs=[T.msg[:, 16 * t:16 * t + 16]],
+                               dsts=[T.og[:, 112 * t + 16 * d:112 * t + 16 * d + 16] for d in range(N - 1)])
+        ops.append({"eng": "g", "fn": [lambda: g.remote_dma_fused([tr], local_sem=T.sem["lo%d" % t])],
+                    "r": ["msg%d" % t], "w": [], "ev": ("lo%d" % t, bits(off)), "dma": False})
+        ops.append({"eng": None, "w": ["og%d" % t], "ev": ("sm%d" % t, (N - 1) * bits(off))})
+
+    def send(t):
+        direct, via = split_dests(r, t, T, topo)
+        src, sk, dk = T["W%d" % (t % 3)][:, 0:GH], "W%d.0" % (t % 3), ["W%d.g" % (t % 3), "W%d.h" % (t % 3)]
+        if EARLY and t == XI: src, sk, dk = T.MX[:, GH:2 * GH], "xi", ["gxi"]
+        elif EARLY and t: src, sk, dk = T.MX[:, 0:GH], "m0", ["gm%d" % ((t - 1) % 2)]
+        trs = [RemoteDMATransfer(dst_ids=dst_ids([T.cores[q] for q in direct], core, topo), dma_engine_mask=off,
+                                 remote_sem=T.sem["ar%d" % t], srcs=[src], dsts=[ghost_slot(T, t, r, q) for q in direct])]
+        n = bits(off)
+        if via:
+            hc = helper_of(core, T, topo)
+            on = topo.mask(core, hc) & ~off
+            trs.append(RemoteDMATransfer(dst_ids=dst_ids([hc], core, topo), dma_engine_mask=on, remote_sem=T.sem["ha%d" % t],
+                                         srcs=[src], dsts=[T.hl[:, t * GH:(t + 1) * GH]]))
+            n += bits(on)
+        ops.append({"eng": "g", "fn": [lambda: g.remote_dma_fused(trs, local_sem=T.sem["ls%d" % t])],
+                    "r": [sk], "w": [], "ev": ("ls%d" % t, n), "dma": False})
+        ops.append({"eng": None, "w": dk, "ev": ("ar%d" % t, (N - 1) * bits(off))})
+
+    def wkeys(t): return ["W%d.%s" % (t % 3, k) for k in ("0", "1", "2", "g", "h")]
+    full = slice(0, 128)
+    wd = lambda k: T.WD[:, 128 * k:128 * k + 128]
+    TBK = ["TBi", "TBg"] + ["TB%d" % k for k in range(16)]
+
+    def rows(pairs):
+        dma("y", [(T.TB[k::16, 0:V], wd(j)) for k, j in pairs], ["TBi"] + ["WD%d" % j for k, j in pairs], ["TB%d" % k for k, j in pairs])
+
+    I1, I16 = T.I1[:, 0:128], T.I16[:, 0:128]
+
+    dma("y", rot(T.W0, T.x0, slice(0, GH), slice(0, GH)), w=["W0.0"])
+    dma("s", rot(T.adi, T.ad, full, full), w=["adi"])
+    dma("y", rot(T.W0, T.x0, slice(GH, V), slice(GH, V)), w=["W0.1", "W0.2"])
+    dma("s", rot(T.sl, T.lm, slice(0, 137), slice(0, 137), 1) + rot(T.sl, T.sg, slice(144, 281), slice(0, 137), 1), w=["sl"])
+    dma("y", sum([rot(T.MX, T.xi, slice(CUTS[k] + CUTS[k + 1], 2 * CUTS[k + 1]), slice(CUTS[k], CUTS[k + 1])) for k in range(3)], []), w=["xi"])
+    io_ = lambda out, pat, cm, k: op("g", lambda: g.iota(out, pat, 0, cm, allow_small_or_imprecise_dtypes=True), (), [k])
+    io_(T.v1[:], [[1, 128]], -1, "v1")
+    io_(T.v2[:], [[16, 8], [0, 16]], -1, "v2")
+    io_(T.v3[:], [[1, 8], [0, 16]], -1, "v3")
+    io_(T.vi[:], [[0, 8], [1, 16]], 0, "vi")
+    send(0)
+    io_(T.vk[:], [[0, 128]], 1, "vk")
+    if EARLY: send(XI)
+    ms(T.ONK[:], KK / 16, ["ONK"])
+    ms(T.ON16[:], 0.0625, ["ON16"]); ms(T.z8[:], 0.0, ["z8"]); ms(T.ok[:], 1.0, ["ok"])
+    for nm, k in (("I1", 1.0), ("I16", 16.0), ("IF", 1.0)):
+        ts(T[nm][:, 0:128], T.v1[:], 0.0, Op.is_equal, ["v1"], [nm], k, Op.mult)
+    ts(T.M1[:], T.vi[:], 1.0, Op.is_ge, ["vi"], ["M1"])
+    ts(T.LE[:], T.v2[:], 0.0, Op.is_le, ["v2"], ["LE"])
+    ts(T.GE[:], T.v2[:], -15.0, Op.is_ge, ["v2"], ["GE"])
+    ts(T.PRE3[:], T.v2[:], -15.0, Op.is_ge, ["v2"], ["PRE3"], 2 * KK, Op.mult)
+    ts(T.tc1[:], T.v1[:], 0.0, Op.is_ge, ["v1"], ["tc1"])
+    ts(T.E2[:], T.v3[:], 0.0, Op.is_equal, ["v3"], ["E2"])
+    ts(T.E3[:], T.ON16[:], T.IF[:, 8:9], Op.mult, ["ON16", "IF"], ["E3"], 16.0, Op.mult)
+    cp(T.oa0[:], T.adi[:], ["adi"], ["oa0"])
+    ts(T.adt[:, 0:128], T.adi[:], 4, Op.arith_shift_right, ["adi"], ["adt0"])
+    ts(T.adt[:, 128:256], T.adi[:], 15, Op.bitwise_and, ["adi"], ["adt1"])
+    tt(T.BLK[:], T.LE[:], T.GE[:], Op.mult, ["LE", "GE"], ["BLK"])
+    cp(T.adb[:], T.adt[:], ["adt0", "adt1"], ["adb"])
+    cp(T.slb[0:8, 0:137], T.sl[0:8, 0:137], ["sl"], ["slb0"])
+    cp(T.slb[0:8, 144:281], T.sl[0:8, 144:281], ["sl"], ["slb1"])
+    sc(T.xm[:], T.W0[:, 0:V], ["W0.0", "W0.1", "W0.2"], ["xm0", "xm1", "xm2"], bias=-20.0)
+    mm([(T.PC[:, 0:1], T.vi[:], T.I1[:, 0:1], True, True)], ["vi", "I1"], ["PC"])
+    mm([(T.PM[:, 0:128], T.adb[:, 0:128], I1, True, True), (T.PM[:, 128:256], T.adb[:, 128:256], I1, True, True),
+        (T.PM[:, 256:384], T.adb[:, 0:128], I16, True, False), (T.PM[:, 256:384], T.adb[:, 128:256], I1, False, True)],
+       ["adb", "I1", "I16"], ["PM"])
+    mm([(T.PL[:, 0:8], T.slb[0:8, 0:128], T.I1[0:8, 0:8], True, True), (T.PL[:, 24:32], T.slb[0:8, 144:272], T.I1[0:8, 0:8], True, True),
+        (T.PL[0:9, 64:72], T.slb[0:8, 128:137], T.I1[0:8, 0:8], True, True), (T.PL[0:9, 72:80], T.slb[0:8, 272:281], T.I1[0:8, 0:8], True, True)],
+       ["slb0", "slb1", "I1"], ["PL"])
+    tt(T.TRI[:], T.LE[:], T.tc1[:], Op.mult, ["LE", "tc1"], ["TRI"])
+    ts(T.SELC[:, 0:8], T.BLK[:, 0::16], 0.15625, Op.mult, ["BLK"], ["SELC"])
+    if LS:
+        sc(T.SELC[:, 8:16], T.BLK[:, 0::16], ["BLK"], ["SELD"], scale=0.078125)
+        sc(T.IN[:], I1, ["I1"], ["IN"], scale=-1.0)
+        ms(T.wc[:, 6:7], -20.5, ["wc6"])
+        ms(T.ok[LS:128, :], -0.25, ["ok"], ["ok"])
+    cp(T.t1[0:9, :], T.PL[0:9, 64:80], ["PL"], ["t1"])
+    mm([(T.PL[:, 8:16], T.E2[0:9, :], T.t1[0:9, 0:8], True, True), (T.PL[:, 16:24], T.E3[0:9, :], T.t1[0:9, 0:8], True, True),
+        (T.PL[:, 32:40], T.E2[0:9, :], T.t1[0:9, 8:16], True, True), (T.PL[:, 40:48], T.E3[0:9, :], T.t1[0:9, 8:16], True, True)],
+       ["t1", "E2", "E3"], ["PL"])
+    ts(T.A0[:], T.PM[:, 256:384], 16.0, Op.mult, ["PM"], ["A0"], 15.0, Op.add)
+    ts(T.wl[:], T.adb[:, 0:128], 128.0, Op.is_ge, ["adb"], ["wl"], 14.0, Op.mult)
+    ts(T.wc[:, 7:8], T.PC[:, 0:1], float(TO), Op.is_equal, ["PC"], ["wc7"])
+    sc(wd(0), T.adb[:, 0:128], ["adb"], ["WD0"], scale=256.0)
+    sc(wd(1), T.adb[:, 128:256], ["adb"], ["WD1"], scale=16.0)
+    sc(wd(2), T.wl[:], ["wl"], ["WD2"], bias=1.0)
+    ts(T.TB[:, 0:V], T.W0[:, 0:V], 0.0, Op.mult, ["W0.0", "W0.1", "W0.2", "wc7"], ["TBi"], T.wc[:, 7:8], Op.add)
+    rows([(TH, 0), (TL, 1), (TW, 2)])
+    for j, (k, o) in enumerate(((TB_, Op.is_ge), (TB_, Op.is_equal), (TW, Op.is_le), (TO, Op.is_ge), (TO, Op.is_equal))):
+        ts(T.wc[:, j:j + 1], T.PC[:, 0:1], float(k), o, ["PC"], ["wc%d" % j])
+    ts(T.wc[:, 5:6], T.PC[:, 0:1], float(TG), Op.is_equal, ["PC"], ["wc5"], 240.0, Op.mult)
+    ts(T.ne[:, 0:16], T.PL[:, 24:40], 2.0, Op.not_equal, ["PL"], ["ne"])
+    ts(T.ne[:, 16:24], T.PL[:, 40:48], 2.0, Op.not_equal, ["PL"], ["ne3"], -1.0, Op.mult)
+    ts(T.ne[:, 24:32], T.PL[:, 40:48], 0.0, Op.is_equal, ["PL"], ["z3"], 99.0, Op.mult)
+    ts(T.LIM[:, 40:48], T.PL[:, 32:40], 0.0, Op.is_equal, ["PL"], ["LIM5"], 99.0, Op.mult)
+    ts(T.mul[:], T.PL[:, 24:32], 0.0, Op.is_equal, ["PL"], ["mul"], -0.5, Op.mult)
+    tt(T.wc[:, 4:5], T.wc[:, 1:2], T.wc[:, 4:5], Op.subtract, ["wc1", "wc4"], ["wc4"])
+    tt(T.wc[:, 3:4], T.wc[:, 3:4], T.wc[:, 1:2], Op.add, ["wc1", "wc3"], ["wc3"])
+    tt(T.LIM[:, 8:16], T.PL[:, 0:8], T.ne[:, 0:8], Op.mult, ["PL", "ne"], ["LIM1"])
+    tt(T.LIM[:, 32:40], T.PL[:, 8:16], T.ne[:, 8:16], Op.mult, ["PL", "ne"], ["LIM4"])
+    tt(T.nL3[:], T.PL[:, 16:24], T.ne[:, 16:24], Op.mult, ["PL", "ne3"], ["nL3"])
+    tt(T.LIM[:, 24:32], T.PL[:, 8:16], T.ne[:, 24:32], Op.add, ["PL", "z3"], ["LIM3"])
+    ts(T.TB[:, V:V + 16], T.ON16[:, 0:16], T.wc[:, 5:6], Op.mult, ["ON16", "wc4", "wc5"], ["TBg"], T.wc[:, 4:5], Op.add)
+    for a, b, k in ((0, 0, 0), (16, 8, 2), (48, 16, 6)):
+        sc(T.LIM[:, a:a + 8], T.PL[:, b:b + 8], ["PL"], ["LIM%d" % k])
+    for b in range(8):
+        sc(T.M2[:, 16 * b + 1:16 * b + 16], T.M1[:, 1:16], ["M1", "mul"], ["M2c%d" % b], bias=1.0, scale=T.mul[:, b:b + 1])
+    sc(T.M2[:, 0::16], T.M1[:, 0::16], ["M1"], ["M2"])
+    sc(T.IK[:], I1, ["I1"], ["IK"], scale=KK)
+    sc(T.IK32[:], I1, ["I1"], ["IK32"], scale=32 * KK)
+    for j in range(4):
+        sc(T.SELM[:, 8 * j:8 * j + 8], T.BLK[:, 0::16], ["BLK", "wc%d" % j], ["SELM%d" % j], scale=T.wc[:, j:j + 1])
+    for k in range(3):
+        a, b = CUTS[k] // 16, CUTS[k + 1] // 16
+        for nm in (("IS0", "IS1") if EARLY else ("IS0",)):
+            sc(T[nm][:, a:b], T.I1[:, a:b], ["I1"], [nm + "_%d" % k], scale=float(CUTS[k + 1] - CUTS[k]))
+    sc(T.I128[:], I1, ["I1"], ["I128"], scale=128.0)
+    sc(T.I1920[:], I1, ["I1"], ["I1920"], scale=1920.0)
+    if EARLY:
+        for nm, k in (("I1", 1.0), ("I16", 16.0), ("IS0", float(V)), ("IS1", -float(V))):
+            sc(T[nm][:, 128:144], T.I1[:, 0:16], ["I1"], [nm + "x"], scale=k)
+        for k in range(3): sc(T.GG[:, k * V + r * GH:k * V + (r + 1) * GH], T.W0[:, 0:GH], ["W0.0"], ["GGo%d" % k])
+    ts(T.tc2[:], T.vk[:], float(CUTS[1] // 16), Op.is_ge, ["vk"], ["tc2"], -float(CUTS[1] // 16), Op.mult)
+    ts(T.tc3[:], T.vk[:], float(CUTS[2] // 16), Op.is_ge, ["vk"], ["tc3"], float(CUTS[1] // 16 - CUTS[2] // 16), Op.mult)
+    ts(T.a0w[:], T.adi[:], 16.0, Op.mult, ["adi"], ["a0w"])
+    M2K = ["M2"] + ["M2c%d" % b for b in range(8)]
+    SELK = ["SELM%d" % j for j in range(4)]
+    h, l, gh = [T.HB[:, 128 * k:128 * k + 128] for k in range(3)]
+    cc = T.DI[:, 256:384]
+    F0, F1, F2, F3 = [T.PM[:, 128 * k:128 * k + 128] for k in range(4)]
+    nA, EE = T.PC[:, 128:256], T.PC[:, 256:384]
+
+    def base(n):
+        mm([(T.PO[:, 0:n], T.vk[:], T.I16[:, 0:n], True, False), (T.PO[:, 0:128], T.tc2[:], I16, False, False),
+            (T.PO[:, 0:128], T.tc3[:], I16, False, False), (T.PO[:, 0:n], T.vi[:], T.I1[:, 0:n], False, False)],
+           ["vk", "vi", "tc2", "tc3", "I16", "I1", "I16x", "I1x"], ["PO"])
+
+    for t in range(RO):
+        last = t == RO - 1
+        p = t % 2
+        q = 1 - p
+        Wt, Wn = T["W%d" % (t % 3)], T["W%d" % ((t + 1) % 3)]
+        wn = "W%d." % ((t + 1) % 3)
+        oa, oak = T["oa%d" % p], "oa%d" % p
+        born, bk = T.bn[:, 128 * t:128 * t + 128], "bn%d" % t
+
+        def maxg(k):
+            a, b = CUTS[k], CUTS[k + 1]
+            tt(T.MX[:, 2 * a:a + b], Wt[:, 0:WW].indirect(oa[:, a // 16:b // 16]), T.xc[:, a:b], Op.max,
+               wkeys(t) + [oak, "xc%d" % min(k, 1)], ["m%d" % k])
+
+        def select(eng, k):
+            a, b = CUTS[k], CUTS[k + 1]
+            src = T.MX[:, 2 * a:2 * b].indirect(T.osel[:, a // 16:b // 16])
+            (cp if eng == "v" else sc)(Wn[:, a:b], src, ["m%d" % k, "xi", "osel"], [wn + str(k)])
+
+        def minus(k):
+            a, b = CUTS[k], min(CUTS[k + 1], 16 * (LS or 128))
+            if k in XMS: sc(T.xm[:, a:b], Wn[:, a:b], [wn + str(k)], ["xm%d" % k], bias=-20.0)
+            else: ts(T.xm[:, a:b], Wn[:, a:b], -20.0, Op.add, [wn + str(k)], ["xm%d" % k])
+
+        NO = 144 if EARLY and not last else 128
+        if EARLY: cp(T.xc[:, 0:GH], Wt[:, 0:GH], wkeys(t)[:1], ["xc0"])
+        else: dma("y", [(T.xc[:, 0:GH], Wt[:, 0:GH])], wkeys(t), ["xc0"])
+        dma("y", [(T.xc[:, GH:V], Wt[:, GH:V])], wkeys(t), ["xc1"])
+        if EARLY and not last:
+            maxg(0)
+            send(t + 1)
+        if t == 0: base(NO)
+        if LS:
+            c0 = 16 * LS
+            sc(T.ys[:], Wt[:, 0:WW].indirect(oa[:, LS:128]), wkeys(t) + [oak], ["ys"])
+            mm([(T.P2[:], T.IN[:], Wt[:, c0:V], True, False)], wkeys(t)[:3] + ["IN"], ["P2"])
+            mm([(T.P2[:], I1, T.ys[:], False, True)], ["ys"], ["P2"])
+            op("s", lambda: act.activation(T.lt[:, 16 * LS:V], T.P2[:], AF.Sign, bias=T.wc[:, 6:7], scale=-1.0), ["P2", "wc6"], ["lts"])
+        for j, (a, b) in enumerate(LTC):
+            if LS and j == len(LTC) - 1:
+                mm([(T.PC[LS:128, i:128:16], T.lt[:, 16 * LS + i:V:16], T.SELC[:, 8:16], True, True) for i in range(16)], ["lts", "SELD"], ["PC"])
+            tt(T.lt[:, 16 * a:16 * b], Wt[:, 0:WW].indirect(oa[:, a:b]), T.xm[:, 16 * a:16 * b], Op.is_lt,
+               wkeys(t) + [oak, "xm0", "xm1", "xm2"], ["lt%d" % j])
+            mm([(T.PC[a:b, i:128:16], T.lt[:, 16 * a + i:16 * b:16], T.SELC[:, 0:8], True, True) for i in range(16)], ["lt%d" % j, "SELC"], ["PC"])
+        if last or not EARLY: maxg(0)
+        if 0 < t and not last: rows([(TH, 0), (TL, 1), (TS + t - 1, 3)])
+        if t > 0:
+            tt(T.ok[:], F0, cc, Op.is_le, ["PM", "DI2"], ["ok"])
+            tt(T.D1[:], T.A[:], F2, Op.subtract, ["PM", "A"], ["D1"])
+            if LS: ts(T.ok[LS:128, :], T.ok[LS:128, :], -1.25, Op.add, ["ok"], ["ok"])
+            tt(T.D2[:], F1, T.D1[:], Op.mult, ["PM", "D1"], ["D2"])
+            if not last: sc(T.wl[:], F0, ["PM"], ["wl"])
+            if last:
+                tt(T.fi[:], F2, T.D2[:], Op.add, ["PM", "D2"], ["fi"])
+                sc(T.wl[:], F3, ["PM"], ["wl"])
+                ts(T.DI[:, 0:128], T.fi[:], 15, Op.bitwise_and, ["fi"], ["DI0"])
+        if last:
+            ts(T.D2[:], T.DI[:, 0:128], 15.0, Op.is_equal, ["DI0"], ["D2"], -15.0, Op.mult)
+            tt(T.PX[:], T.fi[:], T.D2[:], Op.add, ["fi", "D2"], ["PX"])
+        tt(T.jb[:], T.PC[:, 0:128], T.ok[:], Op.is_ge, ["PC", "ok"], ["cr"])
+        scan(T.nb[:], T.M1[:], T.jb[:], 0.0, Op.mult, Op.add, ["M1", "cr"], ["nb"])
+        tt(T.d1[:], T.nb[:, 15::16], T.LIM[:, 0:8], Op.is_gt, ["nb", "LIM0"], ["d1"])
+        mm([(T.PL[:, 8 * k:8 * k + 8], (T.TRI if k == 3 else T.BLK)[:], T.d1[:], True, True) for k in range(4)], ["d1", "BLK", "TRI"], ["PL"])
+        tt(T.f1[:], T.nb[:, 15::16], T.LIM[:, 8:16], Op.is_gt, ["nb", "LIM1"], ["f1"])
+        mm([(T.P3[:, 0:8], T.IK[:], T.nL3[:], True, False), (T.P3[:, 0:8], T.IK32[:], T.f1[:], False, False)], ["IK", "IK32", "nL3", "f1"], ["P3"])
+        if 0 < t and not last:
+            tt(nA, F2, T.D2[:], Op.add, ["PM", "PC", "D2"], ["nA"])
+        tt(T.l2[:], T.PL[:, 0:32], T.LIM[:, 16:48], Op.is_gt, ["PL", "LIM2", "LIM3", "LIM4", "LIM5"], ["l2"])
+        mm([(T.PL[:, 32:40], T.ON16[:], T.l2[:, 0:8], True, True)], ["l2", "ON16"], ["PL"])
+        mm([(T.P3[:, 0:8], T.ONK[:], T.l2[:, 0:8], False, False), (T.P3[:, 0:8], T.PRE3[:], T.l2[:, 8:16], False, False),
+            (T.P3[:, 0:8], T.IK32[:], T.l2[:, 16:24], False, False), (T.P3[:, 0:8], T.IK32[:], T.l2[:, 24:32], False, True)],
+           ["l2", "ONK", "PRE3"], ["P3"])
+        if 0 < t and not last:
+            mm([(T.P0[:, 256:384], T.wl[:], I1, True, True)], ["wl"], ["P0"])
+            sc(wd(2), T.P0[:, 256:384], ["P0"], ["WD2"])
+            rows([(TW, 2)])
+            tt(EE, T.A0[:], nA, Op.subtract, ["A0", "nA", "PC"], ["EE"])
+        tt(T.d3[:], T.PL[:, 32:40], T.LIM[:, 48:56], Op.is_gt, ["PL", "LIM6"], ["d3"])
+        tt(T.jb[:, 0::16], T.P3[:, 0:8], T.jb[:, 0::16], Op.max, ["P3", "cr"], ["cr"])
+        scan(T.r8[:], T.d3[:], T.z8[:], -3.0, Op.add, Op.add, ["d3", "z8"], ["r8"])
+        scan(T.qb[:], T.M2[:], T.jb[:], 0.0, Op.mult, Op.max, M2K + ["cr"], ["qb"])
+        ts(born, T.qb[:], T.r8[:, 7:8], Op.max, ["qb", "r8"], [bk], 0.75, Op.is_ge)
+        isn = "IS%d" % (p if EARLY else 0)
+        mm([(T.PO[:, 0:NO], born, T[isn][:, 0:NO], False, True)], [bk, isn + "x"] + [isn + "_%d" % k for k in range(3)], ["PO"])
+        if not last:
+            mm([(T.P0[:, 384:512], born, I1, True, True)], [bk], ["P0"])
+            if t > 0: tt(T.EB[:], EE, born, Op.mult, ["EE", "PC", bk], ["EB"])
+        if NO > 128:
+            ts(T.msg[:, 16 * t:16 * t + 16], T.PO[:, 128:144], float(GH * r + V * p), Op.add, ["PO"], ["msg%d" % t])
+            small(t)
+        cp(T.osel[:], T.PO[:, 0:128], ["PO"], ["osel"])
+        if not last:
+            select(SEL0, 0)
+            if not EARLY: send(t + 1)
+            sc(wd(3), T.P0[:, 384:512], ["P0"], ["WD3"])
+            rows([(TB_, 3)])
+            if 0 in XMS: minus(0)
+            maxg(2)
+            select("s", 2)
+            if t > 0: tt(T.A[:], nA, T.EB[:], Op.add, ["nA", "PC", "EB"], ["A"])
+            else: cp(T.A[:], T.A0[:], ["A0"], ["A"])
+            maxg(1)
+            select("s", 1)
+            ts(T.DI[:, 0:128], T.A[:], 8, Op.arith_shift_right, ["A"], ["DI0"])
+            ts(T.DI[:, 128:256], T.A[:], 4, Op.arith_shift_right, ["A"], ["DI1"], 15, Op.bitwise_and)
+            ts(cc, T.A[:], 15, Op.bitwise_and, ["A"], ["DI2"])
+            cp(T.HB[:, 0:256], T.DI[:, 0:256], ["DI0", "DI1"], ["HB"])
+            ts(gh, h, 128.0, Op.is_ge, ["HB"], ["HBg"])
+            mm([(T.PO[:, 144:272], h, I16, True, False), (T.PO[:, 144:272], l, I1, False, True),
+                (T.PO[:, 272:400], h, I1, True, False), (T.PO[:, 272:400], l, T.I128[:], False, False),
+                (T.PO[:, 272:400], gh, T.I1920[:], False, True)], ["HB", "HBg", "I128", "I1920"], ["PO"])
+            if t < RO - 2:
+                mm([(T.P0[:, 0:128], h, T.I128[:], True, False), (T.P0[:, 0:128], h, T.I128[:], False, True),
+                    (T.P0[:, 128:256], l, I16, True, True)], ["HB"], ["P0"])
+            else:
+                mm([(T.P1[:, 0:128], T.bn[:, 128 * s:128 * s + 128], I1, s == 0, False) for s in range(t + 1)], [bk], ["P1"])
+            if 0 not in XMS: minus(0)
+            minus(2)
+            ts(T.ot[:], T.PO[:, 272:400], float(V), Op.min, ["PO"], ["ot"])
+            cp(T["oa%d" % q][:], T.PO[:, 144:272], ["PO"], ["oa%d" % q])
+            base(144 if EARLY and t < RO - 2 else 128)
+            minus(1)
+            if EARLY:
+                win, rd = T.GG[:, p * V:(p + 2) * V], ["gm%d" % p, "gxi", "GGo0", "GGo1", "GGo2", "og%d" % t]
+                o0 = 112 * t
+                if GS: sc(Wn[:, V:V + GS * GH], win.indirect(T.og[:, o0:o0 + 16 * GS]), rd, [wn + "g"])
+                if GS < N - 1: cp(Wn[:, V + GS * GH:WW], win.indirect(T.og[:, o0 + 16 * GS:o0 + 112]), rd, [wn + "h"])
+            nf = 4 if t == RO - 2 else 3
+            for j, (a, b) in enumerate(GTC):
+                sc(T.G[:, 16 * a:16 * b], T.TB[:, 0:V + 16].indirect(T.ot[:, a:b]), TBK + ["ot"], ["G%d" % j])
+                mm([(T.PM[a:b, i:128 * nf:16], T.G[:, 16 * a + i:16 * b:16], T.SELM[:, 0:8 * nf], True, True) for i in range(16)],
+                   ["G%d" % j] + SELK, ["PM"])
+            if t < RO - 2: sc(T.WD[:, 0:256], T.P0[:, 0:256], ["P0"], ["WD0", "WD1"])
+        else:
+            mm([(T.P1[:, 0:128], born, I1, False, True)], [bk], ["P1"])
+            op("t", [lambda: pe.transpose(T.P0[:, 0:128], T.PX[:], T.IF[:])]
+               + [(lambda a=a: pe.matmul(*a)) for a in ((T.P0[:, 128:256], h, T.I128[:], True, False), (T.P0[:, 128:256], h, T.I128[:], False, False),
+                                                        (T.P0[:, 128:256], l, I16, False, False), (T.P0[:, 128:256], T.wl[:], I1, False, True))],
+               ["PX", "IF", "HB", "wl"], ["P0"])
+            mm([(T.P0[:, 256:384], born, I1, True, True)], [bk], ["P0"])
+            select("s", 0)
+            sc(T.YI[:], T.P1[:, 0:128], ["P1"], ["YI"], bias=1.0)
+            dma("s", rot(T.YI, T.yi, full, full, load=False), r_=["YI"])
+            maxg(2)
+            select("s", 2)
+            maxg(1)
+            dma("y", rot(Wn, T.yx, slice(1024, V), slice(1024, V), load=False), r_=[wn + "2"])
+            select("s", 1)
+            dma("y", rot(Wn, T.yx, slice(0, 1024), slice(0, 1024), load=False), r_=[wn + "0", wn + "1"])
+            tt(T.DW[:, 0:128], T.a0w[:], T.P0[:, 0:128], Op.subtract, ["a0w", "P0"], ["DW0"])
+            ts(T.DW[:, 128:256], T.P0[:, 128:256], -1.0, Op.mult, ["P0"], ["DW1"], -1.0, Op.add)
+            tt(T.DW[:, 0:128], T.P0[:, 256:384], T.DW[:, 0:128], Op.mult, ["P0", "DW0"], ["DW0"])
+            tt(T.DW[:, 128:256], T.P0[:, 256:384], T.DW[:, 128:256], Op.mult, ["P0", "DW1"], ["DW1"])
+            tt(T.YO[:], T.P0[:, 0:256], T.DW[:], Op.add, ["P0", "DW0", "DW1"], ["YO"])
+            dma("s", rot(T.YO, T.ya, slice(0, 128), full, load=False) + rot(T.YO, T.yu, slice(128, 256), full, load=False), r_=["YO"])
+    emit(g, T, ops)

@@ -3,87 +3,72 @@ from concourse.mybir import AluOpType, ActivationFunctionType
 
 N, V, GH, RO = 8, 2048, 256, 7
 WW = V + (N - 1) * GH
-EARLY = False
-NH = 2
-GS = 5
-SEL0 = "s"
-XMS = (0,)
-LTC = [(0, 128)]
-LS = 0
-GTC = [(0, 96), (96, 128)]
-SAME_WAR = False
-INC_ALL = False
-CUTS = [0, 256, 1024, 2048]
+ROUTE = [(True, 2, 0)]
+CUTS = [0, 256, 640, 1344, 2048]
+SQ = CUTS[2] // 16
+EM = CUTS[2]
+FIRST = CUTS[3]
+SECOND = CUTS[3] + 256
+LATE = (96, 112)
+T0S = True
+LS = 1536
+GT = [("s", 0, 36), ("v", 36, 84), ("s", 84, 128)]
+FR = [(0, 64), (64, 128)]
 KK = 32768.0
-TH, TL, TW, TB_, TG, TO, TS = 0, 1, 2, 3, 4, 5, 6
-XI = RO
-ORDER = [0, XI] + list(range(1, RO)) if EARLY else list(range(RO))
+BIG = 32 * KK
+TH, TL, TW, TB_, TO, TS = 0, 1, 2, 3, 4, 5
 
 B, F = "bfloat16", "float32"
+SQUARE = ("v1", "v2", "v3", "vk", "vi", "I1", "I16", "I128", "I256", "IN15", "I1920", "IS", "IN", "IK", "IB", "INB", "BLK", "TRI", "PRE3", "ON16",
+          "ONK", "E2", "E3", "LE", "GE", "tc1", "tc2", "sr", "M1", "M2", "jb", "nb", "qb", "ok", "cc", "wl", "gh", "cz", "fb", "one")
 SCRATCH = {
     "W0": ("sbuf", [128, WW], B), "W1": ("sbuf", [128, WW], B), "W2": ("sbuf", [128, WW], B),
     "MX": ("sbuf", [128, 2 * V], B), "xm": ("sbuf", [128, V], B), "xc": ("sbuf", [128, V], B), "lt": ("sbuf", [128, V], B), "G": ("sbuf", [128, V], B),
-    "TB": ("sbuf", [128, V + 16], B), "WD": ("sbuf", [128, 512], B),
-    "DI": ("sbuf", [128, 384], "int32"), "HB": ("sbuf", [128, 384], B), "bn": ("sbuf", [128, RO * 128], B),
-    "GG": ("sbuf", [128, 3 * V if EARLY else 16], B),
-    "msg": ("sbuf", [128, RO * 16], "uint16"), "og": ("sbuf", [128, RO * 112], "uint16"),
+    "ltb": ("sbuf", [128, V], B), "ys": ("sbuf", [128, CUTS[2]], B), "rl": ("sbuf", [128, CUTS[2]], B),
+    "TB": ("sbuf", [128, V + 16], B), "WD": ("sbuf", [128, 640], B), "bn": ("sbuf", [128, RO * 128], B),
+    "HB": ("sbuf", [128, 256], B), "A0": ("sbuf", [128, 256], B), "nA": ("sbuf", [128, 256], B), "t0": ("sbuf", [128, 256], B), "t1": ("sbuf", [128, 256], B),
     "adi": ("sbuf", [128, 128], "int32"), "adt": ("sbuf", [128, 256], "int32"), "adb": ("sbuf", [128, 256], B),
     "oa0": ("sbuf", [128, 128], "uint16"), "oa1": ("sbuf", [128, 128], "uint16"),
     "ot": ("sbuf", [128, 128], "uint16"), "osel": ("sbuf", [128, 128], "uint16"),
-    "sl": ("sbuf", [128, 288], "int32"), "slb": ("sbuf", [128, 288], B), "t1": ("sbuf", [128, 16], B),
-    "v1": ("sbuf", [128, 128], B), "v2": ("sbuf", [128, 128], B), "v3": ("sbuf", [128, 128], B),
-    "vk": ("sbuf", [128, 128], B), "vi": ("sbuf", [128, 128], B),
-    "I1": ("sbuf", [128, 144], B), "I16": ("sbuf", [128, 144], B), "I128": ("sbuf", [128, 128], B),
-    "I1920": ("sbuf", [128, 128], B), "IS0": ("sbuf", [128, 144], B), "IS1": ("sbuf", [128, 144], B), "IF": ("sbuf", [128, 128], F),
-    "BLK": ("sbuf", [128, 128], B), "TRI": ("sbuf", [128, 128], B), "PRE3": ("sbuf", [128, 128], B),
-    "ON16": ("sbuf", [128, 128], B), "E2": ("sbuf", [128, 128], B), "E3": ("sbuf", [128, 128], B),
-    "LE": ("sbuf", [128, 128], B), "GE": ("sbuf", [128, 128], B), "tc1": ("sbuf", [128, 128], B), "tc2": ("sbuf", [128, 128], B),
-    "tc3": ("sbuf", [128, 128], B),
-    "ys": ("sbuf", [128, 512], B), "IN": ("sbuf", [128, 128], B), "SELC": ("sbuf", [128, 16], B), "SELM": ("sbuf", [128, 32], B), "wc": ("sbuf", [128, 8], F),
-    "LIM": ("sbuf", [128, 56], F), "ne": ("sbuf", [128, 32], F), "mul": ("sbuf", [128, 8], F), "nL3": ("sbuf", [128, 8], B),
-    "M1": ("sbuf", [128, 128], B), "M2": ("sbuf", [128, 128], B), "IK": ("sbuf", [128, 128], B), "IK32": ("sbuf", [128, 128], B),
-    "ONK": ("sbuf", [128, 128], B), "d1": ("sbuf", [128, 8], B), "f1": ("sbuf", [128, 8], B), "l2": ("sbuf", [128, 32], B),
-    "d3": ("sbuf", [128, 8], F),
-    "jb": ("sbuf", [128, 128], B), "nb": ("sbuf", [128, 128], B), "qb": ("sbuf", [128, 128], B),
-    "r8": ("sbuf", [128, 8], F), "z8": ("sbuf", [128, 8], F), "ok": ("sbuf", [128, 128], B), "wl": ("sbuf", [128, 128], B),
-    "A0": ("sbuf", [128, 128], "int32"), "A": ("sbuf", [128, 128], "int32"),
-    "D1": ("sbuf", [128, 128], F), "D2": ("sbuf", [128, 128], F), "EB": ("sbuf", [128, 128], F),
-    "fi": ("sbuf", [128, 128], "int32"), "PX": ("sbuf", [128, 128], F), "DW": ("sbuf", [128, 256], F),
-    "YO": ("sbuf", [128, 256], F), "YI": ("sbuf", [128, 128], F), "a0w": ("sbuf", [128, 128], F),
-    "hl": ("sbuf", [128, (RO + 1) * GH if NH else 16], B),
+    "sl": ("sbuf", [128, 288], "int32"), "slb": ("sbuf", [128, 288], B), "tu": ("sbuf", [128, 16], B),
+    "SELC": ("sbuf", [128, 8], B), "SELM": ("sbuf", [128, 32], B), "wc": ("sbuf", [128, 16], F), "EK": ("sbuf", [128, 16], F),
+    "LIM": ("sbuf", [128, 48], F), "ne": ("sbuf", [128, 32], F), "mul": ("sbuf", [128, 8], F), "nL3": ("sbuf", [128, 8], B), "nl3": ("sbuf", [128, 16], B),
+    "d1": ("sbuf", [128, 8], B), "f1": ("sbuf", [128, 8], B), "l2": ("sbuf", [128, 32], B),
+    "sgn": ("sbuf", [128, 16], F), "rk": ("sbuf", [128, 8], F),
+    "YO": ("sbuf", [128, 256], F), "YI": ("sbuf", [128, 128], F), "a0w": ("sbuf", [128, 128], F), "tw": ("sbuf", [128, 128], F),
+    "hl": ("sbuf", [128, RO * GH], B),
 }
-PSUMS = ("P0", "P1", "P2", "P3", "PC", "PM", "PO", "PL")
+for _n in SQUARE:
+    SCRATCH[_n] = ("sbuf", [128, 128], B)
+PSUMS = ("PA", "PB", "P0", "P1", "PC", "PM", "PN", "PO")
 for _p in PSUMS:
     SCRATCH[_p] = ("psum", [128, 512], F)
 SEMAPHORES = (["qv", "qs", "qt", "qg"] + ["dm%d" % k for k in range(48)]
-              + [a + str(t) for a in ("ar", "ls", "ha", "sm", "lo") for t in range(RO + 1)])
+              + [a + str(t) for a in ("ar", "ls", "ha") for t in range(RO)])
 
 
 def bits(m):
     return bin(m).count("1")
 
 
-def helper_of(core, T, topo):
-    for c in topo.cores_of(core):
-        if T.rank_of(c) is None and topo.die(c) != topo.die(core) and all(topo.may_write(c, d) for d in T.cores):
-            return c
-    return None
-
-
-def split_dests(r, j, T, topo):
+def routes(r, T, topo):
     me = T.cores[r]
     others = [(r + d) % N for d in range(1, N)]
-    far = [q for q in others if not topo.same_plane(me, T.cores[q]) and not topo.mates(me, T.cores[q])]
-    far += [q for q in others if topo.mates(me, T.cores[q])]
-    via = far[:0 if EARLY and j == 0 else NH]
-    return [q for q in others if q not in via], via
+    plane = [q for q in others if topo.same_plane(me, T.cores[q])]
+    far = [q for q in others if q not in plane and not topo.mates(me, T.cores[q])]
+    free = [c for c in topo.cores_of(me) if T.rank_of(c) is None]
+    hands = []
+    for other_die, nf, np_ in ROUTE:
+        via, far, plane = far[:nf] + plane[:np_], far[nf:], plane[np_:]
+        c = [c for c in free if (topo.die(c) != topo.die(me)) == other_die and all(topo.may_write(c, T.cores[q]) for q in via)][0]
+        free.remove(c)
+        hands.append((c, via))
+    mate = [q for q in others if topo.mates(me, T.cores[q])]
+    return far + plane + mate, hands
 
 
 def ghost_slot(T, t, src, dst):
     d = (dst - src) % N
-    if EARLY and t:
-        a = (V if t == XI else 2 * V * ((t - 1) % 2)) + src * GH
-        return T.GG[:, a:a + GH]
     return T["W%d" % (t % 3)][:, V + (d - 1) * GH:V + d * GH]
 
 
@@ -91,17 +76,15 @@ def dst_ids(cores, src, topo):
     return [DstId(rid=a[0], pnc=a[1]) for a in [topo.addr(c, src) for c in cores]]
 
 
-def helper_program(g, core, r, T, topo):
-    off = topo.mask(core, T.cores[(r + 1) % N])
+def helper_program(g, core, r, via, T, topo):
+    off = topo.mask(core, T.cores[via[0]])
     on = topo.mask(T.cores[r], core) & ~off
-    todo = [t for t in ORDER if split_dests(r, t, T, topo)[1]]
-    for t in todo:
-        via = split_dests(r, t, T, topo)[1]
+    for t in range(RO):
         g.wait_ge(T.sem["ha%d" % t], bits(on))
         g.remote_dma_fused([RemoteDMATransfer(dst_ids=dst_ids([T.cores[q] for q in via], core, topo), dma_engine_mask=off,
                                               remote_sem=T.sem["ar%d" % t], srcs=[T.hl[:, t * GH:(t + 1) * GH]],
                                               dsts=[ghost_slot(T, t, r, q) for q in via])], local_sem=T.sem["ls%d" % t])
-    for t in todo:
+    for t in range(RO):
         g.wait_ge(T.sem["ls%d" % t], bits(off))
 
 
@@ -122,8 +105,7 @@ def emit(g, T, ops):
             if k in lastw and not (e == "t" and lastw[k][0] == e): deps.append(lastw[k])
         for k in o["w"]:
             for ev in ([lastw[k]] if k in lastw else []) + readers.get(k, []):
-                if ev[0] == e and (e == "t" or k in PSUMS or not SAME_WAR): continue
-                deps.append(ev)
+                if ev[0] != e or not (e == "t" or k in PSUMS): deps.append(ev)
         best = {}
         for ev in deps:
             if ev[1] > best.get(ev[0], (0, 0))[1]: best[ev[0]] = ev
@@ -151,7 +133,7 @@ def emit(g, T, ops):
     count, value = {e: 0 for e in queue}, {}
     for o in ops:
         if o["eng"] is not None and o["ev"] is None and (o["eng"], o["seq"]) in need:
-            count[o["eng"]] += len(o["fn"]) if INC_ALL else 1
+            count[o["eng"]] += 1
             value[(o["eng"], o["seq"])] = count[o["eng"]]
     left = {}
     for o in ops:
@@ -164,7 +146,7 @@ def emit(g, T, ops):
         for j, f in enumerate(o["fn"]):
             ins = f()
             if o["ev"] is None:
-                if (e, o["seq"]) in need and (INC_ALL or j == len(o["fn"]) - 1): ins.then_inc(T.sem["q" + e], 1)
+                if (e, o["seq"]) in need and j == len(o["fn"]) - 1: ins.then_inc(T.sem["q" + e], 1)
             elif o["dma"]:
                 ins.then_inc(T.sem[o["ev"][0]], 16)
     for s, (v, e) in left.items():
@@ -174,9 +156,9 @@ def emit(g, T, ops):
 def rank_program(g, core, T, topo):
     r = T.rank_of(core)
     if r is None:
-        if NH:
-            for q in range(N):
-                if helper_of(T.cores[q], T, topo) == core: helper_program(g, core, q, T, topo)
+        for q in range(N):
+            for c, via in routes(q, T, topo)[1]:
+                if c == core: helper_program(g, core, q, via, T, topo)
         return
     Op, AF = AluOpType, ActivationFunctionType
     vec, act, pe = g.vector, g.scalar, g.tensor
@@ -206,38 +188,28 @@ def rank_program(g, core, T, topo):
     def cp(out, a, r_, w): op("v", lambda: vec.tensor_copy(out, a), r_, w)
     def ms(out, c, w, r_=()): op("v", lambda: vec.memset(out, c), r_, w)
     def mm(lst, r_, w): op("t", [(lambda a=a: pe.matmul(*a)) for a in lst], r_, w)
-    def sc(out, a, r_, w, **kw): op("s", lambda: act.activation(out, a, AF.Identity, **kw), r_, w)
+    def sc(out, a, r_, w, f=AF.Identity, **kw): op("s", lambda: act.activation(out, a, f, **kw), r_, w)
+    def move(eng, out, a, r_, w): (cp if eng == "v" else sc)(out, a, r_, w)
     def scan(out, a, b, init, o0, o1, r_, w): op("v", lambda: vec.tensor_tensor_scan(out, a, b, init, o0, o1), r_, w)
+    def group(out, terms):
+        return [(out, a, b, j == 0, j == len(terms) - 1) for j, (a, b) in enumerate(terms)]
 
     off = topo.mask(core, T.cores[(r + 1) % N])
 
-    def small(t):
-        tr = RemoteDMATransfer(dst_ids=dst_ids([T.cores[(r + d) % N] for d in range(1, N)], core, topo), dma_engine_mask=off,
-                               remote_sem=T.sem["sm%d" % t], srcs=[T.msg[:, 16 * t:16 * t + 16]],
-                               dsts=[T.og[:, 112 * t + 16 * d:112 * t + 16 * d + 16] for d in range(N - 1)])
-        ops.append({"eng": "g", "fn": [lambda: g.remote_dma_fused([tr], local_sem=T.sem["lo%d" % t])],
-                    "r": ["msg%d" % t], "w": [], "ev": ("lo%d" % t, bits(off)), "dma": False})
-        ops.append({"eng": None, "w": ["og%d" % t], "ev": ("sm%d" % t, (N - 1) * bits(off))})
-
     def send(t):
-        direct, via = split_dests(r, t, T, topo)
-        src, sk, dk = T["W%d" % (t % 3)][:, 0:GH], "W%d.0" % (t % 3), ["W%d.g" % (t % 3), "W%d.h" % (t % 3)]
-        if EARLY and t == XI: src, sk, dk = T.MX[:, GH:2 * GH], "xi", ["gxi"]
-        elif EARLY and t: src, sk, dk = T.MX[:, 0:GH], "m0", ["gm%d" % ((t - 1) % 2)]
+        direct, hands = routes(r, T, topo)
+        src, wn = T["W%d" % (t % 3)][:, 0:GH], "W%d." % (t % 3)
+        on = topo.mask(core, hands[0][0]) & ~off
         trs = [RemoteDMATransfer(dst_ids=dst_ids([T.cores[q] for q in direct], core, topo), dma_engine_mask=off,
-                                 remote_sem=T.sem["ar%d" % t], srcs=[src], dsts=[ghost_slot(T, t, r, q) for q in direct])]
-        n = bits(off)
-        if via:
-            hc = helper_of(core, T, topo)
-            on = topo.mask(core, hc) & ~off
-            trs.append(RemoteDMATransfer(dst_ids=dst_ids([hc], core, topo), dma_engine_mask=on, remote_sem=T.sem["ha%d" % t],
-                                         srcs=[src], dsts=[T.hl[:, t * GH:(t + 1) * GH]]))
-            n += bits(on)
+                                 remote_sem=T.sem["ar%d" % t], srcs=[src], dsts=[ghost_slot(T, t, r, q) for q in direct]),
+               RemoteDMATransfer(dst_ids=dst_ids([c for c, via in hands], core, topo), dma_engine_mask=on, remote_sem=T.sem["ha%d" % t],
+                                 srcs=[src], dsts=[T.hl[:, t * GH:(t + 1) * GH] for c in hands])]
         ops.append({"eng": "g", "fn": [lambda: g.remote_dma_fused(trs, local_sem=T.sem["ls%d" % t])],
-                    "r": [sk], "w": [], "ev": ("ls%d" % t, n), "dma": False})
-        ops.append({"eng": None, "w": dk, "ev": ("ar%d" % t, (N - 1) * bits(off))})
+                    "r": [wn + "a", wn + "0"], "w": ["sent"], "ev": ("ls%d" % t, bits(off) + bits(on)), "dma": False})
+        ops.append({"eng": None, "w": [wn + "g"], "ev": ("ar%d" % t, (N - 1) * bits(off))})
 
-    def wkeys(t): return ["W%d.%s" % (t % 3, k) for k in ("0", "1", "2", "g", "h")]
+    def okeys(t, ks=range(4)): return ["W%d.%s" % (t % 3, k) for k in ks] + (["W%d.a" % (t % 3)] if 0 in ks else [])
+    def wkeys(t): return okeys(t) + ["W%d.g" % (t % 3)]
     full = slice(0, 128)
     wd = lambda k: T.WD[:, 128 * k:128 * k + 128]
     TBK = ["TBi", "TBg"] + ["TB%d" % k for k in range(16)]
@@ -245,268 +217,285 @@ def rank_program(g, core, T, topo):
     def rows(pairs):
         dma("y", [(T.TB[k::16, 0:V], wd(j)) for k, j in pairs], ["TBi"] + ["WD%d" % j for k, j in pairs], ["TB%d" % k for k, j in pairs])
 
-    I1, I16 = T.I1[:, 0:128], T.I16[:, 0:128]
+    I1, I16 = T.I1[:], T.I16[:]
+    c2 = CUTS[2]
+    xi_pieces = lambda ks: sum([rot(T.MX, T.xi, slice(CUTS[k] + CUTS[k + 1], 2 * CUTS[k + 1]), slice(CUTS[k], CUTS[k + 1])) for k in ks], [])
 
-    dma("y", rot(T.W0, T.x0, slice(0, GH), slice(0, GH)), w=["W0.0"])
+    dma("y", rot(T.W0, T.x0, slice(0, GH), slice(0, GH)), w=okeys(0, [0]))
     dma("s", rot(T.adi, T.ad, full, full), w=["adi"])
-    dma("y", rot(T.W0, T.x0, slice(GH, V), slice(GH, V)), w=["W0.1", "W0.2"])
+    dma("y", rot(T.W0, T.x0, slice(GH, V), slice(GH, V)), w=okeys(0, [1, 2, 3]))
     dma("s", rot(T.sl, T.lm, slice(0, 137), slice(0, 137), 1) + rot(T.sl, T.sg, slice(144, 281), slice(0, 137), 1), w=["sl"])
-    dma("y", sum([rot(T.MX, T.xi, slice(CUTS[k] + CUTS[k + 1], 2 * CUTS[k + 1]), slice(CUTS[k], CUTS[k + 1])) for k in range(3)], []), w=["xi"])
     io_ = lambda out, pat, cm, k: op("g", lambda: g.iota(out, pat, 0, cm, allow_small_or_imprecise_dtypes=True), (), [k])
     io_(T.v1[:], [[1, 128]], -1, "v1")
-    io_(T.v2[:], [[16, 8], [0, 16]], -1, "v2")
-    io_(T.v3[:], [[1, 8], [0, 16]], -1, "v3")
     io_(T.vi[:], [[0, 8], [1, 16]], 0, "vi")
-    send(0)
+    io_(T.v2[:], [[16, 8], [0, 16]], -1, "v2")
     io_(T.vk[:], [[0, 128]], 1, "vk")
-    if EARLY: send(XI)
-    ms(T.ONK[:], KK / 16, ["ONK"])
-    ms(T.ON16[:], 0.0625, ["ON16"]); ms(T.z8[:], 0.0, ["z8"]); ms(T.ok[:], 1.0, ["ok"])
-    for nm, k in (("I1", 1.0), ("I16", 16.0), ("IF", 1.0)):
-        ts(T[nm][:, 0:128], T.v1[:], 0.0, Op.is_equal, ["v1"], [nm], k, Op.mult)
+    send(0)
+    io_(T.v3[:], [[1, 8], [0, 16]], -1, "v3")
+    dma("y", xi_pieces([0, 1]), ["sent"], ["xi0", "xi1"])
+    dma("y", rot(T.xc, T.x0, slice(c2, V), slice(c2, V)), ["sent"], ["xc2", "xc3"])
+    dma("y", xi_pieces([2, 3]), ["sent"], ["xi2", "xi3"])
+    ms(T.ONK[:], KK / 16, ["ONK"]); ms(T.ON16[:], 0.0625, ["ON16"]); ms(T.one[:], 1.0, ["one"])
+    ms(T.wc[:, 8:9], -20.5 * 256, ["wc8"]); ms(T.wc[:, 9:10], 128.0, ["wc9"]); ms(T.nl3[:, 8:9], 1.0, ["nl3b"])
+    ms(T.wc[:, 10:11], -14.5 * 256, ["wc10"]); ms(T.wc[:, 11:12], -BIG, ["wc11"])
+    ms(T.lt[:, 0:GH], 0.0, ["lty"]); ms(T.lt[:, 16 * LATE[0]:16 * LATE[1]], 0.0, ["ltz"], ["lty"])
+    for nm, k in (("I1", 1.0), ("I16", 16.0), ("IN", -1.0)):
+        ts(T[nm][:], T.v1[:], 0.0, Op.is_equal, ["v1"], [nm], k, Op.mult)
+    sc(T.tc1[:], T.v1[:], ["v1", "wc9"], ["tc1"], AF.Sigmoid, bias=T.wc[:, 9:10], scale=256.0)
+    for nm, k in (("IK", KK), ("IB", BIG), ("INB", -BIG), ("I128", 128.0), ("I1920", 1920.0), ("I256", 256.0), ("IN15", -15.0)):
+        sc(T[nm][:], I1, ["I1"], [nm], scale=k)
     ts(T.M1[:], T.vi[:], 1.0, Op.is_ge, ["vi"], ["M1"])
+    mm([(T.PC[:, 0:1], T.vi[:], T.I1[:, 0:1], True, True)], ["vi", "I1"], ["PC"])
     ts(T.LE[:], T.v2[:], 0.0, Op.is_le, ["v2"], ["LE"])
     ts(T.GE[:], T.v2[:], -15.0, Op.is_ge, ["v2"], ["GE"])
     ts(T.PRE3[:], T.v2[:], -15.0, Op.is_ge, ["v2"], ["PRE3"], 2 * KK, Op.mult)
-    ts(T.tc1[:], T.v1[:], 0.0, Op.is_ge, ["v1"], ["tc1"])
-    ts(T.E2[:], T.v3[:], 0.0, Op.is_equal, ["v3"], ["E2"])
-    ts(T.E3[:], T.ON16[:], T.IF[:, 8:9], Op.mult, ["ON16", "IF"], ["E3"], 16.0, Op.mult)
-    cp(T.oa0[:], T.adi[:], ["adi"], ["oa0"])
+    ts(T.EK[:], T.vi[:, 0:16], T.PC[:, 0:1], Op.is_equal, ["vi", "PC"], ["EK"])
+    ts(T.wc[:, 0:1], T.PC[:, 0:1], float(TB_), Op.is_ge, ["PC"], ["wc0"], 0.0625, Op.mult)
+    cp(T.oa1[:], T.adi[:], ["adi"], ["oa1"])
     ts(T.adt[:, 0:128], T.adi[:], 4, Op.arith_shift_right, ["adi"], ["adt0"])
     ts(T.adt[:, 128:256], T.adi[:], 15, Op.bitwise_and, ["adi"], ["adt1"])
     tt(T.BLK[:], T.LE[:], T.GE[:], Op.mult, ["LE", "GE"], ["BLK"])
-    cp(T.adb[:], T.adt[:], ["adt0", "adt1"], ["adb"])
+    cp(T.WD[:, 0:256], T.adt[:], ["adt0", "adt1"], ["WD0", "WD1"])
     cp(T.slb[0:8, 0:137], T.sl[0:8, 0:137], ["sl"], ["slb0"])
     cp(T.slb[0:8, 144:281], T.sl[0:8, 144:281], ["sl"], ["slb1"])
-    sc(T.xm[:], T.W0[:, 0:V], ["W0.0", "W0.1", "W0.2"], ["xm0", "xm1", "xm2"], bias=-20.0)
-    mm([(T.PC[:, 0:1], T.vi[:], T.I1[:, 0:1], True, True)], ["vi", "I1"], ["PC"])
-    mm([(T.PM[:, 0:128], T.adb[:, 0:128], I1, True, True), (T.PM[:, 128:256], T.adb[:, 128:256], I1, True, True),
-        (T.PM[:, 256:384], T.adb[:, 0:128], I16, True, False), (T.PM[:, 256:384], T.adb[:, 128:256], I1, False, True)],
-       ["adb", "I1", "I16"], ["PM"])
-    mm([(T.PL[:, 0:8], T.slb[0:8, 0:128], T.I1[0:8, 0:8], True, True), (T.PL[:, 24:32], T.slb[0:8, 144:272], T.I1[0:8, 0:8], True, True),
-        (T.PL[0:9, 64:72], T.slb[0:8, 128:137], T.I1[0:8, 0:8], True, True), (T.PL[0:9, 72:80], T.slb[0:8, 272:281], T.I1[0:8, 0:8], True, True)],
-       ["slb0", "slb1", "I1"], ["PL"])
+    mm([(T.PM[:, 0:128], wd(0), I1, True, True), (T.PM[:, 128:256], wd(1), I1, True, True)], ["WD0", "WD1", "I1"], ["PM"])
+    mm([(T.PN[:, 0:8], T.slb[0:8, 0:128], T.I1[0:8, 0:8], True, True), (T.PN[:, 24:32], T.slb[0:8, 144:272], T.I1[0:8, 0:8], True, True),
+        (T.PN[0:9, 64:72], T.slb[0:8, 128:137], T.I1[0:8, 0:8], True, True), (T.PN[0:9, 72:80], T.slb[0:8, 272:281], T.I1[0:8, 0:8], True, True)],
+       ["slb0", "slb1", "I1"], ["PN"])
+    sc(T.A0[:], T.PM[:, 0:256], ["PM"], ["A0"])
+    ts(T.E2[:], T.v3[:], 0.0, Op.is_equal, ["v3"], ["E2"])
+    ts(T.E3[:], T.vk[:], 8.0, Op.is_equal, ["vk"], ["E3"])
+    cp(T.tu[0:9, :], T.PN[0:9, 64:80], ["PN"], ["tu"])
+    mm([(T.PN[:, 8:16], T.E2[0:9, :], T.tu[0:9, 0:8], True, True), (T.PN[:, 16:24], T.E3[0:9, :], T.tu[0:9, 0:8], True, True),
+        (T.PN[:, 32:40], T.E2[0:9, :], T.tu[0:9, 8:16], True, True), (T.PN[:, 40:48], T.E3[0:9, :], T.tu[0:9, 8:16], True, True)],
+       ["tu", "E2", "E3"], ["PN"])
+    ts(T.xm[:, c2:V], T.W0[:, c2:V], -20.0, Op.add, okeys(0), ["xm2", "xm3"])
     tt(T.TRI[:], T.LE[:], T.tc1[:], Op.mult, ["LE", "tc1"], ["TRI"])
-    ts(T.SELC[:, 0:8], T.BLK[:, 0::16], 0.15625, Op.mult, ["BLK"], ["SELC"])
-    if LS:
-        sc(T.SELC[:, 8:16], T.BLK[:, 0::16], ["BLK"], ["SELD"], scale=0.078125)
-        sc(T.IN[:], I1, ["I1"], ["IN"], scale=-1.0)
-        ms(T.wc[:, 6:7], -20.5, ["wc6"])
-        ms(T.ok[LS:128, :], -0.25, ["ok"], ["ok"])
-    cp(T.t1[0:9, :], T.PL[0:9, 64:80], ["PL"], ["t1"])
-    mm([(T.PL[:, 8:16], T.E2[0:9, :], T.t1[0:9, 0:8], True, True), (T.PL[:, 16:24], T.E3[0:9, :], T.t1[0:9, 0:8], True, True),
-        (T.PL[:, 32:40], T.E2[0:9, :], T.t1[0:9, 8:16], True, True), (T.PL[:, 40:48], T.E3[0:9, :], T.t1[0:9, 8:16], True, True)],
-       ["t1", "E2", "E3"], ["PL"])
-    ts(T.A0[:], T.PM[:, 256:384], 16.0, Op.mult, ["PM"], ["A0"], 15.0, Op.add)
-    ts(T.wl[:], T.adb[:, 0:128], 128.0, Op.is_ge, ["adb"], ["wl"], 14.0, Op.mult)
-    ts(T.wc[:, 7:8], T.PC[:, 0:1], float(TO), Op.is_equal, ["PC"], ["wc7"])
-    sc(wd(0), T.adb[:, 0:128], ["adb"], ["WD0"], scale=256.0)
-    sc(wd(1), T.adb[:, 128:256], ["adb"], ["WD1"], scale=16.0)
-    sc(wd(2), T.wl[:], ["wl"], ["WD2"], bias=1.0)
-    ts(T.TB[:, 0:V], T.W0[:, 0:V], 0.0, Op.mult, ["W0.0", "W0.1", "W0.2", "wc7"], ["TBi"], T.wc[:, 7:8], Op.add)
-    rows([(TH, 0), (TL, 1), (TW, 2)])
-    for j, (k, o) in enumerate(((TB_, Op.is_ge), (TB_, Op.is_equal), (TW, Op.is_le), (TO, Op.is_ge), (TO, Op.is_equal))):
-        ts(T.wc[:, j:j + 1], T.PC[:, 0:1], float(k), o, ["PC"], ["wc%d" % j])
-    ts(T.wc[:, 5:6], T.PC[:, 0:1], float(TG), Op.is_equal, ["PC"], ["wc5"], 240.0, Op.mult)
-    ts(T.ne[:, 0:16], T.PL[:, 24:40], 2.0, Op.not_equal, ["PL"], ["ne"])
-    ts(T.ne[:, 16:24], T.PL[:, 40:48], 2.0, Op.not_equal, ["PL"], ["ne3"], -1.0, Op.mult)
-    ts(T.ne[:, 24:32], T.PL[:, 40:48], 0.0, Op.is_equal, ["PL"], ["z3"], 99.0, Op.mult)
-    ts(T.LIM[:, 40:48], T.PL[:, 32:40], 0.0, Op.is_equal, ["PL"], ["LIM5"], 99.0, Op.mult)
-    ts(T.mul[:], T.PL[:, 24:32], 0.0, Op.is_equal, ["PL"], ["mul"], -0.5, Op.mult)
-    tt(T.wc[:, 4:5], T.wc[:, 1:2], T.wc[:, 4:5], Op.subtract, ["wc1", "wc4"], ["wc4"])
-    tt(T.wc[:, 3:4], T.wc[:, 3:4], T.wc[:, 1:2], Op.add, ["wc1", "wc3"], ["wc3"])
-    tt(T.LIM[:, 8:16], T.PL[:, 0:8], T.ne[:, 0:8], Op.mult, ["PL", "ne"], ["LIM1"])
-    tt(T.LIM[:, 32:40], T.PL[:, 8:16], T.ne[:, 8:16], Op.mult, ["PL", "ne"], ["LIM4"])
-    tt(T.nL3[:], T.PL[:, 16:24], T.ne[:, 16:24], Op.mult, ["PL", "ne3"], ["nL3"])
-    tt(T.LIM[:, 24:32], T.PL[:, 8:16], T.ne[:, 24:32], Op.add, ["PL", "z3"], ["LIM3"])
-    ts(T.TB[:, V:V + 16], T.ON16[:, 0:16], T.wc[:, 5:6], Op.mult, ["ON16", "wc4", "wc5"], ["TBg"], T.wc[:, 4:5], Op.add)
-    for a, b, k in ((0, 0, 0), (16, 8, 2), (48, 16, 6)):
-        sc(T.LIM[:, a:a + 8], T.PL[:, b:b + 8], ["PL"], ["LIM%d" % k])
+    ts(T.SELC[:], T.BLK[:, 0::16], 0.15625, Op.mult, ["BLK"], ["SELC"])
+    ts(T.ne[:, 0:16], T.PN[:, 24:40], 2.0, Op.not_equal, ["PN"], ["ne"])
+    ts(T.ne[:, 16:24], T.PN[:, 40:48], 2.0, Op.not_equal, ["PN"], ["ne3"], -1.0, Op.mult)
+    ts(T.ne[:, 24:32], T.PN[:, 40:48], 0.0, Op.is_equal, ["PN"], ["z3"], 99.0, Op.mult)
+    ts(T.LIM[:, 40:48], T.PN[:, 32:40], 0.0, Op.is_equal, ["PN"], ["LIM5"], 99.0, Op.mult)
+    ts(T.mul[:], T.PN[:, 24:32], 0.0, Op.is_equal, ["PN"], ["mul"], -0.5, Op.mult)
+    ts(T.nl3[:, 0:8], T.PN[:, 16:24], -1.0, Op.mult, ["PN"], ["nl3"], -0.5, Op.add)
+    tt(T.LIM[:, 8:16], T.PN[:, 0:8], T.ne[:, 0:8], Op.mult, ["PN", "ne"], ["LIM1"])
+    tt(T.LIM[:, 32:40], T.PN[:, 8:16], T.ne[:, 8:16], Op.mult, ["PN", "ne"], ["LIM4"])
+    tt(T.nL3[:], T.PN[:, 16:24], T.ne[:, 16:24], Op.mult, ["PN", "ne3"], ["nL3"])
+    tt(T.LIM[:, 24:32], T.PN[:, 8:16], T.ne[:, 24:32], Op.add, ["PN", "z3"], ["LIM3"])
+    for a, b, k in ((0, 0, 0), (16, 8, 2)):
+        sc(T.LIM[:, a:a + 8], T.PN[:, b:b + 8], ["PN"], ["LIM%d" % k])
     for b in range(8):
         sc(T.M2[:, 16 * b + 1:16 * b + 16], T.M1[:, 1:16], ["M1", "mul"], ["M2c%d" % b], bias=1.0, scale=T.mul[:, b:b + 1])
     sc(T.M2[:, 0::16], T.M1[:, 0::16], ["M1"], ["M2"])
-    sc(T.IK[:], I1, ["I1"], ["IK"], scale=KK)
-    sc(T.IK32[:], I1, ["I1"], ["IK32"], scale=32 * KK)
+    for k in range(4):
+        a, b = CUTS[k] // 16, CUTS[k + 1] // 16
+        sc(T.IS[:, a:b], T.I1[:, a:b], ["I1"], ["IS%d" % k], scale=float(CUTS[k + 1] - CUTS[k]))
+    for k in range(1, 4):
+        ts(T.tc2[:], T.vk[:], float(CUTS[k] // 16), Op.is_ge, ["vk"], ["tc2"], float(CUTS[k - 1] // 16 - CUTS[k] // 16), Op.mult)
+        tt(T.sr[:], T.vk[:] if k == 1 else T.sr[:], T.tc2[:], Op.add, ["vk", "sr", "tc2"], ["sr"])
+    ek = lambda k: T.EK[:, k:k + 1]
+    ts(wd(2), wd(0), 128.0, Op.is_ge, ["WD0"], ["WD2a"], 14.0, Op.mult)
+    ts(T.TB[:, 0:V], T.W0[:, 0:V], 0.0, Op.mult, okeys(0) + ["EK"], ["TBi"], ek(TO), Op.add)
+    sc(wd(2), wd(2), ["WD2a"], ["WD2"], bias=1.0)
+    rows([(TH, 0), (TL, 1), (TW, 2)])
+    ts(T.wc[:, 6:7], ek(TO), 14.0, Op.mult, ["EK"], ["wc6"], ek(TB_), Op.add)
+    ts(T.wc[:, 4:5], ek(TB_), BIG, Op.mult, ["EK"], ["wc4"])
+    ts(T.wc[:, 3:4], ek(TW), 0.0625, Op.mult, ["EK"], ["wc3"], ek(TB_), Op.add)
+    ts(T.gh[:], T.A0[:, 0:128], 128.0, Op.is_ge, ["A0"], ["gh"])
+    ts(T.wc[:, 1:3], T.EK[:, TH:TL + 1], T.wc[:, 4:5], Op.subtract, ["EK", "wc4"], ["wc1", "wc2"])
+    ts(T.TB[:, V:V + 16], T.one[:, 0:16], T.wc[:, 6:7], Op.mult, ["one", "wc6"], ["TBg"])
     for j in range(4):
         sc(T.SELM[:, 8 * j:8 * j + 8], T.BLK[:, 0::16], ["BLK", "wc%d" % j], ["SELM%d" % j], scale=T.wc[:, j:j + 1])
-    for k in range(3):
-        a, b = CUTS[k] // 16, CUTS[k + 1] // 16
-        for nm in (("IS0", "IS1") if EARLY else ("IS0",)):
-            sc(T[nm][:, a:b], T.I1[:, a:b], ["I1"], [nm + "_%d" % k], scale=float(CUTS[k + 1] - CUTS[k]))
-    sc(T.I128[:], I1, ["I1"], ["I128"], scale=128.0)
-    sc(T.I1920[:], I1, ["I1"], ["I1920"], scale=1920.0)
-    if EARLY:
-        for nm, k in (("I1", 1.0), ("I16", 16.0), ("IS0", float(V)), ("IS1", -float(V))):
-            sc(T[nm][:, 128:144], T.I1[:, 0:16], ["I1"], [nm + "x"], scale=k)
-        for k in range(3): sc(T.GG[:, k * V + r * GH:k * V + (r + 1) * GH], T.W0[:, 0:GH], ["W0.0"], ["GGo%d" % k])
-    ts(T.tc2[:], T.vk[:], float(CUTS[1] // 16), Op.is_ge, ["vk"], ["tc2"], -float(CUTS[1] // 16), Op.mult)
-    ts(T.tc3[:], T.vk[:], float(CUTS[2] // 16), Op.is_ge, ["vk"], ["tc3"], float(CUTS[1] // 16 - CUTS[2] // 16), Op.mult)
     ts(T.a0w[:], T.adi[:], 16.0, Op.mult, ["adi"], ["a0w"])
     M2K = ["M2"] + ["M2c%d" % b for b in range(8)]
     SELK = ["SELM%d" % j for j in range(4)]
-    h, l, gh = [T.HB[:, 128 * k:128 * k + 128] for k in range(3)]
-    cc = T.DI[:, 256:384]
-    F0, F1, F2, F3 = [T.PM[:, 128 * k:128 * k + 128] for k in range(4)]
-    nA, EE = T.PC[:, 128:256], T.PC[:, 256:384]
+    F0, FU, F3, FB, X = T.PM[:, 0:128], T.PM[:, 128:384], T.PM[:, 384:512], T.PN[:, 0:256], T.PN[:, 256:512]
+    PL, N3, UP, BT, Z = T.PC[:, 128:160], T.PC[:, 160:169], T.P1[:, 384:392], T.P1[:, 256:384], T.P0[:, 0:256]
+    PU, PI = T.P0[:, 0:128], T.PA[:, 384:512]
+    PD = [(T.PA[:, 0:CUTS[1]], "PA"), (T.PB[:, 0:CUTS[2] - CUTS[1]], "PB")]
 
-    def base(n):
-        mm([(T.PO[:, 0:n], T.vk[:], T.I16[:, 0:n], True, False), (T.PO[:, 0:128], T.tc2[:], I16, False, False),
-            (T.PO[:, 0:128], T.tc3[:], I16, False, False), (T.PO[:, 0:n], T.vi[:], T.I1[:, 0:n], False, False)],
-           ["vk", "vi", "tc2", "tc3", "I16", "I1", "I16x", "I1x"], ["PO"])
+    def offsets(hb, hk, oa, oak):
+        h, l = hb[:, 0:128], hb[:, 128:256]
+        mm(group(T.PO[:, 256:384], [(h, I1), (l, T.I128[:]), (T.gh[:], T.I1920[:])])
+           + (group(T.PO[:, 128:256], [(h, I16), (l, I1)]) if oak else []), [hk, "gh", "I128", "I1920", "I16"], ["PO"])
+        ts(T.ot[:], T.PO[:, 256:384], float(V), Op.min, ["PO"], ["ot"])
+        if oak: cp(oa[:], T.PO[:, 128:256], ["PO"], [oak])
+
+    def base():
+        mm([(T.PO[:, 0:128], T.sr[:], I16, True, False), (T.PO[:, 0:128], T.vi[:], I1, False, False)], ["sr", "vi", "I16", "I1"], ["PO"])
+
+    def own(W, t):
+        for k in (1, 0):
+            mm([(PD[k][0], T.IN[:], W[:, CUTS[k]:CUTS[k + 1]], True, False)], okeys(t, [k]) + ["IN"], [PD[k][1]])
+
+    offsets(T.A0, "A0", None, None)
+    base()
 
     for t in range(RO):
         last = t == RO - 1
-        p = t % 2
-        q = 1 - p
         Wt, Wn = T["W%d" % (t % 3)], T["W%d" % ((t + 1) % 3)]
         wn = "W%d." % ((t + 1) % 3)
-        oa, oak = T["oa%d" % p], "oa%d" % p
+        oak, onk = "oa%d" % (t % 2 if t else 1), "oa%d" % ((t + 1) % 2)
+        oa = T[oak]
+        hb, hk = (T.HB, "HB") if t > 1 else (T.A0, "A0")
+        cc, ck = (T.cc, "cc") if t > 1 else (T.one, "one")
         born, bk = T.bn[:, 128 * t:128 * t + 128], "bn%d" % t
+        wb = 3 + t % 2
 
-        def maxg(k):
-            a, b = CUTS[k], CUTS[k + 1]
-            tt(T.MX[:, 2 * a:a + b], Wt[:, 0:WW].indirect(oa[:, a // 16:b // 16]), T.xc[:, a:b], Op.max,
-               wkeys(t) + [oak, "xc%d" % min(k, 1)], ["m%d" % k])
+        def maxg(k, a=None, b=None, j=0):
+            a, b = a or CUTS[k], b or CUTS[k + 1]
+            if a < b:
+                tt(T.MX[:, CUTS[k] + a:CUTS[k] + b], Wt[:, 0:WW].indirect(oa[:, a // 16:b // 16]), T.xc[:, a:b], Op.max,
+                   wkeys(t) + [oak, "xc%d" % k], ["m%d.%d" % (k, j)])
 
-        def select(eng, k):
-            a, b = CUTS[k], CUTS[k + 1]
-            src = T.MX[:, 2 * a:2 * b].indirect(T.osel[:, a // 16:b // 16])
-            (cp if eng == "v" else sc)(Wn[:, a:b], src, ["m%d" % k, "xi", "osel"], [wn + str(k)])
+        def select(eng, k, a=None, b=None, key=None):
+            a, b = a or CUTS[k], b or CUTS[k + 1]
+            src = T.MX[:, 2 * CUTS[k]:2 * CUTS[k + 1]].indirect(T.osel[:, a // 16:b // 16])
+            move(eng, Wn[:, a:b], src, ["m%d.%d" % (k, j) for j in range(3)] + ["xi%d" % k, "os%d" % min(k, 1)], [key or wn + str(k)])
 
         def minus(k):
-            a, b = CUTS[k], min(CUTS[k + 1], 16 * (LS or 128))
-            if k in XMS: sc(T.xm[:, a:b], Wn[:, a:b], [wn + str(k)], ["xm%d" % k], bias=-20.0)
-            else: ts(T.xm[:, a:b], Wn[:, a:b], -20.0, Op.add, [wn + str(k)], ["xm%d" % k])
+            a, b = CUTS[k], CUTS[k + 1]
+            ts(T.xm[:, a:b], Wn[:, a:b], -20.0, Op.add, [wn + str(k)], ["xm%d" % k])
 
-        NO = 144 if EARLY and not last else 128
-        if EARLY: cp(T.xc[:, 0:GH], Wt[:, 0:GH], wkeys(t)[:1], ["xc0"])
-        else: dma("y", [(T.xc[:, 0:GH], Wt[:, 0:GH])], wkeys(t), ["xc0"])
-        dma("y", [(T.xc[:, GH:V], Wt[:, GH:V])], wkeys(t), ["xc1"])
-        if EARLY and not last:
-            maxg(0)
-            send(t + 1)
-        if t == 0: base(NO)
-        if LS:
-            c0 = 16 * LS
-            sc(T.ys[:], Wt[:, 0:WW].indirect(oa[:, LS:128]), wkeys(t) + [oak], ["ys"])
-            mm([(T.P2[:], T.IN[:], Wt[:, c0:V], True, False)], wkeys(t)[:3] + ["IN"], ["P2"])
-            mm([(T.P2[:], I1, T.ys[:], False, True)], ["ys"], ["P2"])
-            op("s", lambda: act.activation(T.lt[:, 16 * LS:V], T.P2[:], AF.Sign, bias=T.wc[:, 6:7], scale=-1.0), ["P2", "wc6"], ["lts"])
-        for j, (a, b) in enumerate(LTC):
-            if LS and j == len(LTC) - 1:
-                mm([(T.PC[LS:128, i:128:16], T.lt[:, 16 * LS + i:V:16], T.SELC[:, 8:16], True, True) for i in range(16)], ["lts", "SELD"], ["PC"])
-            tt(T.lt[:, 16 * a:16 * b], Wt[:, 0:WW].indirect(oa[:, a:b]), T.xm[:, 16 * a:16 * b], Op.is_lt,
-               wkeys(t) + [oak, "xm0", "xm1", "xm2"], ["lt%d" % j])
-            mm([(T.PC[a:b, i:128:16], T.lt[:, 16 * a + i:16 * b:16], T.SELC[:, 0:8], True, True) for i in range(16)], ["lt%d" % j, "SELC"], ["PC"])
-        if last or not EARLY: maxg(0)
-        if 0 < t and not last: rows([(TH, 0), (TL, 1), (TS + t - 1, 3)])
+        def count(a, b, r_, lt=T.lt):
+            mm([(T.PC[a:b, i:128:16], lt[:, 16 * a + i:16 * b:16], T.SELC[:], True, True) for i in range(16)], r_ + ["SELC"], ["PC"])
+
+        def low(a, b, key, lt=T.lt):
+            tt(lt[:, 16 * a:16 * b], Wt[:, 0:WW].indirect(oa[:, a:b]), T.xm[:, 16 * a:16 * b], Op.is_lt, wkeys(t) + [oak, "xm2", "xm3"], [key])
+
+        def table(pieces):
+            for e, a, b in pieces:
+                move(e, T.G[:, 16 * a:16 * b], T.TB[:, 0:V + 16].indirect(T.ot[:, a:b]), TBK + ["ot"], ["G%d" % a])
+
+        def fields(a, b):
+            gk = ["G%d" % c for e, c, d in GT if c < b and d > a] + SELK
+            mm([(T.PM[a:b, i:512:16], T.G[:, 16 * a + i:16 * b:16], T.SELM[:], True, True) for i in range(16)], gk, ["PM"])
+
+        def pair(out, a, flag, scale, r_, w):
+            if a is not None: mm([(out, I1, a[:], True, False)], r_, w)
+            else: mm([(out[:, 0:128], scale, flag, False, False), (out[:, 128:256], scale, flag, False, True)], r_, w)
+
+        new = [(TH, hb[:, 0:128]), (TL, hb[:, 128:256]), (TW, T.wl[:])][0 if t > 1 else 2:]
+
+        def digits():
+            a = 128 * new[0][0]
+            mm([(T.P0[:, 128 * k:128 * k + 128], d, I1, True, True) for k, d in new], [hk, "wl"], ["P0"])
+            sc(T.WD[:, a:384], T.P0[:, a:384], ["P0"], ["WD%d" % k for k, _ in new])
+            rows([(k, k) for k, _ in new] + [(TS + t - 1, 7 - wb)])
+
+        most = lambda k: mm(group(PD[k][0], [(I1, Wt[:, CUTS[k]:CUTS[k + 1]]), (I1, T.rl[:, CUTS[k]:CUTS[k + 1]])]), okeys(t, [k]) + ["rl%d" % k], [PD[k][1]])
+        keep1 = lambda: sc(T.MX[:, 2 * CUTS[1]:CUTS[1] + CUTS[2]], PD[1][0], ["PB"], ["m1.0"])
+
+        if t == 0: own(Wt, t)
+        else: pair(FB, hb, None, None, [hk], ["PN"])
+        for k in (1, 0):
+            a, b = CUTS[k], CUTS[k + 1]
+            sc(T.ys[:, a:b], Wt[:, 0:WW].indirect(oa[:, a // 16:b // 16]), wkeys(t) + [oak], ["ys%d" % k])
+            mm([(PD[k][0], I1, T.ys[:, a:b], False, True)], ["ys%d" % k], [PD[k][1]])
+        low(SQ, LATE[0], "ltv")
+        low(LATE[1], 128, "ltw")
+        low(LATE[0], LATE[1], "ltb", T.ltb)
+        for k in (1, 0):
+            sc(T.lt[:, CUTS[1]:c2] if k else T.ltb[:, 0:GH], PD[k][0], [PD[k][1], "wc8"], ["lt%d" % k], AF.Sigmoid, bias=T.wc[:, 8:9], scale=-256.0)
+        count(0, 128, ["ltz", "lt1", "ltv", "ltw"])
+        count(LATE[0], LATE[1], ["ltb"], T.ltb)
+        count(0, GH // 16, ["lt0"], T.ltb)
         if t > 0:
-            tt(T.ok[:], F0, cc, Op.is_le, ["PM", "DI2"], ["ok"])
-            tt(T.D1[:], T.A[:], F2, Op.subtract, ["PM", "A"], ["D1"])
-            if LS: ts(T.ok[LS:128, :], T.ok[LS:128, :], -1.25, Op.add, ["ok"], ["ok"])
-            tt(T.D2[:], F1, T.D1[:], Op.mult, ["PM", "D1"], ["D2"])
-            if not last: sc(T.wl[:], F0, ["PM"], ["wl"])
-            if last:
-                tt(T.fi[:], F2, T.D2[:], Op.add, ["PM", "D2"], ["fi"])
-                sc(T.wl[:], F3, ["PM"], ["wl"])
-                ts(T.DI[:, 0:128], T.fi[:], 15, Op.bitwise_and, ["fi"], ["DI0"])
-        if last:
-            ts(T.D2[:], T.DI[:, 0:128], 15.0, Op.is_equal, ["DI0"], ["D2"], -15.0, Op.mult)
-            tt(T.PX[:], T.fi[:], T.D2[:], Op.add, ["fi", "D2"], ["PX"])
-        tt(T.jb[:], T.PC[:, 0:128], T.ok[:], Op.is_ge, ["PC", "ok"], ["cr"])
+            ts(T.fb[:], F3, 1.0, Op.is_ge, ["PM"], ["fb"])
+            tt(T.ok[:], F0, cc[:], Op.is_le, ["PM", ck], ["ok"])
+            ts(T.wl[:], F0, 16.0, Op.mult, ["PM"], ["wl"])
+            if last: ts(T.cz[:], F3, 16.0, Op.mult, ["PM"], ["cz"], 15.0, Op.min)
+            pair(FB, None, T.fb[:], T.IB[:], ["fb"], ["PN"])
+        for k in (0, 1):
+            a, b = CUTS[k], CUTS[k + 1]
+            sc(T.rl[:, a:b], PD[k][0], [PD[k][1]], ["rl%d" % k], AF.Relu)
+        most(0)
+        if t > 0: sc(T.t1[:], FB, ["PN", "wc11"], ["t1"], AF.Relu, bias=T.wc[:, 11:12])
+        sc(T.MX[:, 0:CUTS[1]], PD[0][0], ["PA"], ["m0.0"])
+        if 0 < t and not last: digits()
+        tt(T.jb[:], T.PC[:, 0:128], (T.ok if t else T.one)[:], Op.is_ge, ["PC", "ok", "one"], ["cr"])
         scan(T.nb[:], T.M1[:], T.jb[:], 0.0, Op.mult, Op.add, ["M1", "cr"], ["nb"])
         tt(T.d1[:], T.nb[:, 15::16], T.LIM[:, 0:8], Op.is_gt, ["nb", "LIM0"], ["d1"])
-        mm([(T.PL[:, 8 * k:8 * k + 8], (T.TRI if k == 3 else T.BLK)[:], T.d1[:], True, True) for k in range(4)], ["d1", "BLK", "TRI"], ["PL"])
+        mm([(PL[:, 8 * k:8 * k + 8], (T.TRI if k == 3 else T.BLK)[:], T.d1[:], True, True) for k in range(4)]
+           + [(N3, I1, T.nl3[:, 0:9], True, False)], ["d1", "BLK", "TRI", "nl3", "nl3b"], ["PC"])
         tt(T.f1[:], T.nb[:, 15::16], T.LIM[:, 8:16], Op.is_gt, ["nb", "LIM1"], ["f1"])
-        mm([(T.P3[:, 0:8], T.IK[:], T.nL3[:], True, False), (T.P3[:, 0:8], T.IK32[:], T.f1[:], False, False)], ["IK", "IK32", "nL3", "f1"], ["P3"])
-        if 0 < t and not last:
-            tt(nA, F2, T.D2[:], Op.add, ["PM", "PC", "D2"], ["nA"])
-        tt(T.l2[:], T.PL[:, 0:32], T.LIM[:, 16:48], Op.is_gt, ["PL", "LIM2", "LIM3", "LIM4", "LIM5"], ["l2"])
-        mm([(T.PL[:, 32:40], T.ON16[:], T.l2[:, 0:8], True, True)], ["l2", "ON16"], ["PL"])
-        mm([(T.P3[:, 0:8], T.ONK[:], T.l2[:, 0:8], False, False), (T.P3[:, 0:8], T.PRE3[:], T.l2[:, 8:16], False, False),
-            (T.P3[:, 0:8], T.IK32[:], T.l2[:, 16:24], False, False), (T.P3[:, 0:8], T.IK32[:], T.l2[:, 24:32], False, True)],
-           ["l2", "ONK", "PRE3"], ["P3"])
-        if 0 < t and not last:
-            mm([(T.P0[:, 256:384], T.wl[:], I1, True, True)], ["wl"], ["P0"])
-            sc(wd(2), T.P0[:, 256:384], ["P0"], ["WD2"])
-            rows([(TW, 2)])
-            tt(EE, T.A0[:], nA, Op.subtract, ["A0", "nA", "PC"], ["EE"])
-        tt(T.d3[:], T.PL[:, 32:40], T.LIM[:, 48:56], Op.is_gt, ["PL", "LIM6"], ["d3"])
-        tt(T.jb[:, 0::16], T.P3[:, 0:8], T.jb[:, 0::16], Op.max, ["P3", "cr"], ["cr"])
-        scan(T.r8[:], T.d3[:], T.z8[:], -3.0, Op.add, Op.add, ["d3", "z8"], ["r8"])
+        mm([(UP, T.IK[:], T.nL3[:], True, False), (UP, T.IB[:], T.f1[:], False, False)], ["IK", "IB", "nL3", "f1"], ["P1"])
+        if last:
+            sc(T.tc2[:], F3, ["PM", "wc10"], ["tc2"], AF.Sigmoid, bias=T.wc[:, 10:11], scale=4096.0)
+        tt(T.l2[:], PL, T.LIM[:, 16:48], Op.is_gt, ["PC", "LIM2", "LIM3", "LIM4", "LIM5"], ["l2"])
+        mm([(N3[:, 0:8], T.ON16[:], T.l2[:, 0:8], False, True)], ["l2", "ON16"], ["PC"])
+        mm([(UP, T.ONK[:], T.l2[:, 0:8], False, False), (UP, T.PRE3[:], T.l2[:, 8:16], False, False),
+            (UP, T.IB[:], T.l2[:, 16:24], False, False), (UP, T.IB[:], T.l2[:, 24:32], False, True)], ["l2", "ONK", "PRE3"], ["P1"])
+        most(1)
+        sc(T.sgn[:, 0:9], N3, ["PC"], ["rk"], AF.Sign, accum_out=T.rk[:, 0:1])
+        if t > 0: tt(T.nA[:], FU, T.t1[:], Op.max, ["PM", "t1"], ["nA"])
+        else: maxg(2, c2, EM)
+        if last: keep1()
+        tt(T.jb[:, 0::16], UP, T.jb[:, 0::16], Op.max, ["P1", "cr"], ["cr"])
         scan(T.qb[:], T.M2[:], T.jb[:], 0.0, Op.mult, Op.max, M2K + ["cr"], ["qb"])
-        ts(born, T.qb[:], T.r8[:, 7:8], Op.max, ["qb", "r8"], [bk], 0.75, Op.is_ge)
-        isn = "IS%d" % (p if EARLY else 0)
-        mm([(T.PO[:, 0:NO], born, T[isn][:, 0:NO], False, True)], [bk, isn + "x"] + [isn + "_%d" % k for k in range(3)], ["PO"])
+        ts(born, T.qb[:], T.rk[:, 0:1], Op.max, ["qb", "rk"], [bk], 0.75, Op.is_ge)
+        mm([(T.PO[:, 0:128], born, T.IS[:], False, True)], [bk] + ["IS%d" % k for k in range(4)], ["PO"])
         if not last:
-            mm([(T.P0[:, 384:512], born, I1, True, True)], [bk], ["P0"])
-            if t > 0: tt(T.EB[:], EE, born, Op.mult, ["EE", "PC", bk], ["EB"])
-        if NO > 128:
-            ts(T.msg[:, 16 * t:16 * t + 16], T.PO[:, 128:144], float(GH * r + V * p), Op.add, ["PO"], ["msg%d" % t])
-            small(t)
-        cp(T.osel[:], T.PO[:, 0:128], ["PO"], ["osel"])
-        if not last:
-            select(SEL0, 0)
-            if not EARLY: send(t + 1)
-            sc(wd(3), T.P0[:, 384:512], ["P0"], ["WD3"])
-            rows([(TB_, 3)])
-            if 0 in XMS: minus(0)
-            maxg(2)
-            select("s", 2)
-            if t > 0: tt(T.A[:], nA, T.EB[:], Op.add, ["nA", "PC", "EB"], ["A"])
-            else: cp(T.A[:], T.A0[:], ["A0"], ["A"])
-            maxg(1)
+            mm([(BT, born, I1, True, True)], [bk], ["P1"])
+            cp(T.osel[:, 0:16], T.PO[:, 0:16], ["PO"], ["os0"])
+            sc(wd(wb), BT, ["P1"], ["WD%d" % wb])
+            rows([(TB_, wb)])
+            select("v", 0, 0, GH // 2, wn + "a")
+            select("s", 0, GH // 2, GH)
+            send(t + 1)
+            cp(T.osel[:, 16:128], T.PO[:, 16:128], ["PO"], ["os1"])
+            if t > 0:
+                pair(Z, T.A0, None, None, ["A0"], ["P0"])
+                pair(Z, None, born, T.IB[:], [bk], ["P0"])
+                pair(X, T.nA, None, None, ["nA"], ["PN"])
+                pair(X, None, born, T.INB[:], [bk, "INB"], ["PN"])
+                if T0S: sc(T.t0[:], Z, ["P0", "wc11"], ["t0"], AF.Relu, bias=T.wc[:, 11:12])
+                else: ts(T.t0[:], Z, -BIG, Op.add, ["P0"], ["t0"], 0.0, Op.max)
+            keep1()
             select("s", 1)
-            ts(T.DI[:, 0:128], T.A[:], 8, Op.arith_shift_right, ["A"], ["DI0"])
-            ts(T.DI[:, 128:256], T.A[:], 4, Op.arith_shift_right, ["A"], ["DI1"], 15, Op.bitwise_and)
-            ts(cc, T.A[:], 15, Op.bitwise_and, ["A"], ["DI2"])
-            cp(T.HB[:, 0:256], T.DI[:, 0:256], ["DI0", "DI1"], ["HB"])
-            ts(gh, h, 128.0, Op.is_ge, ["HB"], ["HBg"])
-            mm([(T.PO[:, 144:272], h, I16, True, False), (T.PO[:, 144:272], l, I1, False, True),
-                (T.PO[:, 272:400], h, I1, True, False), (T.PO[:, 272:400], l, T.I128[:], False, False),
-                (T.PO[:, 272:400], gh, T.I1920[:], False, True)], ["HB", "HBg", "I128", "I1920"], ["PO"])
-            if t < RO - 2:
-                mm([(T.P0[:, 0:128], h, T.I128[:], True, False), (T.P0[:, 0:128], h, T.I128[:], False, True),
-                    (T.P0[:, 128:256], l, I16, True, True)], ["HB"], ["P0"])
-            else:
-                mm([(T.P1[:, 0:128], T.bn[:, 128 * s:128 * s + 128], I1, s == 0, False) for s in range(t + 1)], [bk], ["P1"])
-            if 0 not in XMS: minus(0)
+            first = FIRST if t else c2
+            maxg(2, EM if t == 0 else c2, first, 1)
+            if t > 0:
+                tt(T.HB[:], X, T.t0[:], Op.max, ["PN", "t0"], ["HB"])
+                ts(T.gh[:], T.HB[:, 0:128], 128.0, Op.is_ge, ["HB"], ["gh"])
+            maxg(2, max(first, EM if t == 0 else c2), None, 2)
+            select("s", 2)
+            maxg(3, None, SECOND)
+            if t > 0: offsets(T.HB, "HB", T[onk], onk)
+            base()
+            own(Wn, t + 1)
+            table([p for p in GT[:1] if p[0] == "s"])
+            maxg(3, SECOND, None, 1)
+            select("s", 3)
+            dma("y", [(T.xc[:, c2:V], Wn[:, c2:V])], ["sent", wn + "2", wn + "3"], ["xc2", "xc3"])
+            if t > 0: tt(T.cc[:], F3, born, Op.max, ["PM", bk], ["cc"])
+            table([p for j, p in enumerate(GT) if j or p[0] != "s"])
             minus(2)
-            ts(T.ot[:], T.PO[:, 272:400], float(V), Op.min, ["PO"], ["ot"])
-            cp(T["oa%d" % q][:], T.PO[:, 144:272], ["PO"], ["oa%d" % q])
-            base(144 if EARLY and t < RO - 2 else 128)
-            minus(1)
-            if EARLY:
-                win, rd = T.GG[:, p * V:(p + 2) * V], ["gm%d" % p, "gxi", "GGo0", "GGo1", "GGo2", "og%d" % t]
-                o0 = 112 * t
-                if GS: sc(Wn[:, V:V + GS * GH], win.indirect(T.og[:, o0:o0 + 16 * GS]), rd, [wn + "g"])
-                if GS < N - 1: cp(Wn[:, V + GS * GH:WW], win.indirect(T.og[:, o0 + 16 * GS:o0 + 112]), rd, [wn + "h"])
-            nf = 4 if t == RO - 2 else 3
-            for j, (a, b) in enumerate(GTC):
-                sc(T.G[:, 16 * a:16 * b], T.TB[:, 0:V + 16].indirect(T.ot[:, a:b]), TBK + ["ot"], ["G%d" % j])
-                mm([(T.PM[a:b, i:128 * nf:16], T.G[:, 16 * a + i:16 * b:16], T.SELM[:, 0:8 * nf], True, True) for i in range(16)],
-                   ["G%d" % j] + SELK, ["PM"])
-            if t < RO - 2: sc(T.WD[:, 0:256], T.P0[:, 0:256], ["P0"], ["WD0", "WD1"])
+            minus(3)
+            for a, b in FR: fields(a, b)
         else:
-            mm([(T.P1[:, 0:128], born, I1, False, True)], [bk], ["P1"])
-            op("t", [lambda: pe.transpose(T.P0[:, 0:128], T.PX[:], T.IF[:])]
-               + [(lambda a=a: pe.matmul(*a)) for a in ((T.P0[:, 128:256], h, T.I128[:], True, False), (T.P0[:, 128:256], h, T.I128[:], False, False),
-                                                        (T.P0[:, 128:256], l, I16, False, False), (T.P0[:, 128:256], T.wl[:], I1, False, True))],
-               ["PX", "IF", "HB", "wl"], ["P0"])
-            mm([(T.P0[:, 256:384], born, I1, True, True)], [bk], ["P0"])
+            out = lambda a, b, r_: dma("y", rot(Wn, T.yx, slice(a, b), slice(a, b), load=False), r_=r_)
+            mm([(BT, born, T.IB[:], True, True)], [bk], ["P1"])
+            mm(group(PU, [(hb[:, 0:128], T.I256[:]), (hb[:, 128:256], I16), (T.wl[:], I1), (T.gh[:], T.IN15[:]), (born, T.INB[:])]),
+               [hk, "wl", "gh", "I256", "IN15", "INB"], ["P0"])
+            mm(group(X[:, 0:128], [(T.nA[:, 0:128], T.I256[:]), (T.nA[:, 128:256], I16), (T.cz[:], I1), (T.tc2[:], T.IN15[:]), (born, T.INB[:])]),
+               ["nA", "cz", "tc2", bk], ["PN"])
+            mm(group(PI, [(T.bn[:, 128 * s:128 * s + 128], I1) for s in range(RO)]), [], ["PA"])
+            cp(T.osel[:], T.PO[:, 0:128], ["PO"], ["os0", "os1"])
             select("s", 0)
-            sc(T.YI[:], T.P1[:, 0:128], ["P1"], ["YI"], bias=1.0)
-            dma("s", rot(T.YI, T.yi, full, full, load=False), r_=["YI"])
+            select("s", 1)
+            out(0, c2, okeys(t + 1, [0, 1]))
             maxg(2)
             select("s", 2)
-            maxg(1)
-            dma("y", rot(Wn, T.yx, slice(1024, V), slice(1024, V), load=False), r_=[wn + "2"])
-            select("s", 1)
-            dma("y", rot(Wn, T.yx, slice(0, 1024), slice(0, 1024), load=False), r_=[wn + "0", wn + "1"])
-            tt(T.DW[:, 0:128], T.a0w[:], T.P0[:, 0:128], Op.subtract, ["a0w", "P0"], ["DW0"])
-            ts(T.DW[:, 128:256], T.P0[:, 128:256], -1.0, Op.mult, ["P0"], ["DW1"], -1.0, Op.add)
-            tt(T.DW[:, 0:128], T.P0[:, 256:384], T.DW[:, 0:128], Op.mult, ["P0", "DW0"], ["DW0"])
-            tt(T.DW[:, 128:256], T.P0[:, 256:384], T.DW[:, 128:256], Op.mult, ["P0", "DW1"], ["DW1"])
-            tt(T.YO[:], T.P0[:, 0:256], T.DW[:], Op.add, ["P0", "DW0", "DW1"], ["YO"])
-            dma("s", rot(T.YO, T.ya, slice(0, 128), full, load=False) + rot(T.YO, T.yu, slice(128, 256), full, load=False), r_=["YO"])
+            sc(T.YI[:], PI, ["PA"], ["YI"], bias=1.0)
+            out(c2, CUTS[3], okeys(t + 1, [2]))
+            maxg(3)
+            select("s", 3, LS, V)
+            tt(T.tw[:], BT, T.a0w[:], Op.min, ["P1", "a0w"], ["tw"])
+            ts(T.YO[:, 128:256], PU, -1.0, Op.max, ["P0"], ["YU"])
+            tt(T.YO[:, 0:128], X[:, 0:128], T.tw[:], Op.max, ["PN", "tw"], ["YA"])
+            dma("y", rot(T.YI, T.yi, full, full, load=False) + rot(T.YO, T.ya, slice(0, 128), full, load=False)
+                + rot(T.YO, T.yu, slice(128, 256), full, load=False), r_=["YI", "YA", "YU"])
+            select("v", 3, CUTS[3], LS, wn + "b")
+            out(CUTS[3], V, okeys(t + 1, [3, "b"]))
     emit(g, T, ops)

@@ -3,39 +3,40 @@ from concourse.mybir import AluOpType, ActivationFunctionType
 
 N, V, GH, RO = 8, 2048, 256, 7
 WW = V + (N - 1) * GH
-ROUTE = [(True, 2, 0)]
-CUTS = [0, 256, 640, 1344, 2048]
-SQ = CUTS[2] // 16
-EM = CUTS[2]
-FIRST = CUTS[3]
-SECOND = CUTS[3] + 256
-LATE = (96, 112)
-T0S = True
-LS = 1536
-GT = [("s", 0, 36), ("v", 36, 84), ("s", 84, 128)]
-FR = [(0, 64), (64, 128)]
-KK = 32768.0
-BIG = 32 * KK
-TH, TL, TW, TB_, TO, TS = 0, 1, 2, 3, 4, 5
+TS = WW // 16
+MO = V - GH
+ROUTE = [(True, 1, 1)]
+A = 1280
+MID = 1536
+END = 1792
+GM = 800
+G2 = 1024
+S0 = 96
+C1 = 896
+SL = 1792
+GT = 62
+SCA = [(A, MID, "PA", "lt"), (END, V, "PB", "lt"), (MID, END, "PN", "ltb")]
+BIG = 1048576.0
+MAGIC = 12582912.0
+TH, TL, TW, TO, TB0 = 0, 1, 2, 3, 4
 
-B, F = "bfloat16", "float32"
-SQUARE = ("v1", "v2", "v3", "vk", "vi", "I1", "I16", "I128", "I256", "IN15", "I1920", "IS", "IN", "IK", "IB", "INB", "BLK", "TRI", "PRE3", "ON16",
-          "ONK", "E2", "E3", "LE", "GE", "tc1", "tc2", "sr", "M1", "M2", "jb", "nb", "qb", "ok", "cc", "wl", "gh", "cz", "fb", "one")
+B, F, U = "bfloat16", "float32", "uint16"
+SQUARE = ("v1", "v2", "v3", "vi", "vc", "I1", "IN", "I16", "IN16", "ITS", "IB", "INB", "I256", "INO", "IT2", "I17", "IN256", "INK", "IK17",
+          "BLK", "TRI", "LE", "GE", "tc1", "E2", "EM", "BC", "BCS", "ON9", "M1", "MQ", "jb", "nb", "qb", "ok", "got", "wq", "one", "b12", "pre", "sgn")
 SCRATCH = {
     "W0": ("sbuf", [128, WW], B), "W1": ("sbuf", [128, WW], B), "W2": ("sbuf", [128, WW], B),
-    "MX": ("sbuf", [128, 2 * V], B), "xm": ("sbuf", [128, V], B), "xc": ("sbuf", [128, V], B), "lt": ("sbuf", [128, V], B), "G": ("sbuf", [128, V], B),
-    "ltb": ("sbuf", [128, V], B), "ys": ("sbuf", [128, CUTS[2]], B), "rl": ("sbuf", [128, CUTS[2]], B),
-    "TB": ("sbuf", [128, V + 16], B), "WD": ("sbuf", [128, 640], B), "bn": ("sbuf", [128, RO * 128], B),
-    "HB": ("sbuf", [128, 256], B), "A0": ("sbuf", [128, 256], B), "nA": ("sbuf", [128, 256], B), "t0": ("sbuf", [128, 256], B), "t1": ("sbuf", [128, 256], B),
-    "adi": ("sbuf", [128, 128], "int32"), "adt": ("sbuf", [128, 256], "int32"), "adb": ("sbuf", [128, 256], B),
-    "oa0": ("sbuf", [128, 128], "uint16"), "oa1": ("sbuf", [128, 128], "uint16"),
-    "ot": ("sbuf", [128, 128], "uint16"), "osel": ("sbuf", [128, 128], "uint16"),
-    "sl": ("sbuf", [128, 288], "int32"), "slb": ("sbuf", [128, 288], B), "tu": ("sbuf", [128, 16], B),
-    "SELC": ("sbuf", [128, 8], B), "SELM": ("sbuf", [128, 32], B), "wc": ("sbuf", [128, 16], F), "EK": ("sbuf", [128, 16], F),
-    "LIM": ("sbuf", [128, 48], F), "ne": ("sbuf", [128, 32], F), "mul": ("sbuf", [128, 8], F), "nL3": ("sbuf", [128, 8], B), "nl3": ("sbuf", [128, 16], B),
-    "d1": ("sbuf", [128, 8], B), "f1": ("sbuf", [128, 8], B), "l2": ("sbuf", [128, 32], B),
-    "sgn": ("sbuf", [128, 16], F), "rk": ("sbuf", [128, 8], F),
-    "YO": ("sbuf", [128, 256], F), "YI": ("sbuf", [128, 128], F), "a0w": ("sbuf", [128, 128], F), "tw": ("sbuf", [128, 128], F),
+    "M0": ("sbuf", [128, 8 * GH], B), "MX": ("sbuf", [128, MO + V], B), "xm": ("sbuf", [128, A], B), "xc": ("sbuf", [128, A], B),
+    "lt": ("sbuf", [128, V], B), "ltb": ("sbuf", [128, V], B), "ys": ("sbuf", [128, V], B), "G": ("sbuf", [128, V], B),
+    "TB": ("sbuf", [128, WW], B), "bn": ("sbuf", [128, RO * TS], B), "HB": ("sbuf", [128, 2 * TS], B), "A0": ("sbuf", [128, 2 * TS], B),
+    "WR": ("sbuf", [128, TS], B), "OW": ("sbuf", [128, TS], B), "t0": ("sbuf", [128, 256], B), "pr": ("sbuf", [128, 256], B),
+    "adi": ("sbuf", [128, 128], "int32"), "adt": ("sbuf", [128, 256], "int32"),
+    "of0": ("sbuf", [128, 256], U), "of1": ("sbuf", [128, 256], U), "osel": ("sbuf", [128, 128], U),
+    "sl": ("sbuf", [128, 288], "int32"), "slb": ("sbuf", [128, 288], B), "lp": ("sbuf", [128, 144], B), "ne": ("sbuf", [128, 144], B),
+    "e1": ("sbuf", [128, 144], B), "tu": ("sbuf", [128, 32], B), "T3": ("sbuf", [128, 8], F), "r3": ("sbuf", [128, 8], B),
+    "SELC": ("sbuf", [128, 8], B), "SELM": ("sbuf", [128, 32 * (RO - 1)], B), "CO": ("sbuf", [128, 32], F),
+    "wc": ("sbuf", [128, 16], F), "EK": ("sbuf", [128, 16], F), "pk": ("sbuf", [128, 32], F), "LIM": ("sbuf", [128, 24], F),
+    "d1": ("sbuf", [128, 24], B), "B0": ("sbuf", [128, 16], B), "MG": ("sbuf", [128, 16], B), "J512": ("sbuf", [128, 16], B),
+    "acc": ("sbuf", [128, 8], F), "YO": ("sbuf", [128, 384], F), "a0w": ("sbuf", [128, 128], F), "tw": ("sbuf", [128, 128], F),
     "hl": ("sbuf", [128, RO * GH], B),
 }
 for _n in SQUARE:
@@ -92,47 +93,40 @@ def emit(g, T, ops):
     queue = {"v": g.vector, "s": g.scalar, "t": g.tensor, "g": g, "y": g.sync}
     clock = {e: {} for e in queue}
     seq = {e: 0 for e in queue}
-    lastw, readers, need = {}, {}, set()
+    wrote, read, need = {}, {}, set()
+    meets = lambda a, b: a[0] & b[0] and a[1] < b[2] and b[1] < a[2] and (a[3] != b[3] or (a[1] - b[1]) % a[3] == 0)
+    inside = lambda a, b: not a[0] & ~b[0] and b[1] <= a[1] and a[2] <= b[2] and (b[3] == 1 or a[1:] == b[1:])
     for o in ops:
         e = o["eng"]
-        if e is None:
-            for k in o["w"]:
-                lastw[k] = (o["ev"][0], o["ev"][1], {})
-                readers[k] = []
-            continue
         deps = []
-        for k in o["r"]:
-            if k in lastw and not (e == "t" and lastw[k][0] == e): deps.append(lastw[k])
-        for k in o["w"]:
-            for ev in ([lastw[k]] if k in lastw else []) + readers.get(k, []):
-                if ev[0] != e or not (e == "t" or k in PSUMS): deps.append(ev)
-        best = {}
-        for ev in deps:
-            if ev[1] > best.get(ev[0], (0, 0))[1]: best[ev[0]] = ev
-        waits = []
-        evs = list(best.values())
-        for ev in evs:
-            if any(x is not ev and x[2].get(ev[0], 0) >= ev[1] for x in evs): continue
-            if clock[e].get(ev[0], 0) < ev[1]:
-                waits.append((ev[0], ev[1]))
-        for ev in evs:
-            for s, v in list(ev[2].items()) + [(ev[0], ev[1])]:
-                if clock[e].get(s, 0) < v: clock[e][s] = v
-        o["waits"] = waits
-        for w in waits: need.add(w)
+        for k, reg in o["r"]:
+            deps += [ev for x, ev in wrote.get(k, []) if meets(x, reg)]
+        for k, reg in o["w"]:
+            deps += [ev for x, ev in wrote.get(k, []) + read.get(k, []) if meets(x, reg) and (ev[0] != e or k not in PSUMS)]
+        if e is not None:
+            best = {}
+            for ev in deps:
+                if ev[1] > best.get(ev[0], (0, 0))[1]: best[ev[0]] = ev
+            evs = list(best.values())
+            o["waits"] = [(ev[0], ev[1]) for ev in evs if clock[e].get(ev[0], 0) < ev[1]
+                          and not any(x is not ev and x[2].get(ev[0], 0) >= ev[1] for x in evs)]
+            for ev in evs:
+                for s, n in list(ev[2].items()) + [(ev[0], ev[1])]:
+                    if clock[e].get(s, 0) < n: clock[e][s] = n
+            need.update(o["waits"])
         if o["ev"] is None:
             seq[e] += 1
-            ev = (e, seq[e], dict(clock[e]))
             o["seq"] = seq[e]
+            ev = (e, seq[e], dict(clock[e]))
         else:
-            ev = (o["ev"][0], o["ev"][1], dict(clock[e]))
-        for k in o["r"]: readers.setdefault(k, []).append(ev)
-        for k in o["w"]:
-            lastw[k] = ev
-            readers[k] = []
+            ev = (o["ev"][0], o["ev"][1], dict(clock[e]) if e else {})
+        for k, reg in o["r"]: read.setdefault(k, []).append((reg, ev))
+        for k, reg in o["w"]:
+            wrote[k] = [x for x in wrote.get(k, []) if not inside(x[0], reg)] + [(reg, ev)]
+            read[k] = [x for x in read.get(k, []) if not inside(x[0], reg)]
     count, value = {e: 0 for e in queue}, {}
     for o in ops:
-        if o["eng"] is not None and o["ev"] is None and (o["eng"], o["seq"]) in need:
+        if o["ev"] is None and (o["eng"], o["seq"]) in need:
             count[o["eng"]] += 1
             value[(o["eng"], o["seq"])] = count[o["eng"]]
     left = {}
@@ -140,17 +134,17 @@ def emit(g, T, ops):
         e = o["eng"]
         if o["ev"] is not None: left[o["ev"][0]] = (o["ev"][1], e if e in ("s", "y") else "g")
         if e is None: continue
-        for s, v in o["waits"]:
-            if s in queue: queue[e].wait_ge(T.sem["q" + s], value[(s, v)])
-            else: queue[e].wait_ge(T.sem[s], v)
+        for s, n in o["waits"]:
+            if s in queue: queue[e].wait_ge(T.sem["q" + s], value[(s, n)])
+            else: queue[e].wait_ge(T.sem[s], n)
         for j, f in enumerate(o["fn"]):
             ins = f()
             if o["ev"] is None:
                 if (e, o["seq"]) in need and j == len(o["fn"]) - 1: ins.then_inc(T.sem["q" + e], 1)
             elif o["dma"]:
                 ins.then_inc(T.sem[o["ev"][0]], 16)
-    for s, (v, e) in left.items():
-        if (s, v) not in need: queue[e].wait_ge(T.sem[s], v)
+    for s, (n, e) in left.items():
+        if (s, n) not in need: queue[e].wait_ge(T.sem[s], n)
 
 
 def rank_program(g, core, T, topo):
@@ -163,339 +157,282 @@ def rank_program(g, core, T, topo):
     Op, AF = AluOpType, ActivationFunctionType
     vec, act, pe = g.vector, g.scalar, g.tensor
     ops, ndma = [], [0]
+    ALL = (1 << 128) - 1
 
-    def op(eng, fn, r_=(), w=()):
-        rd = [k for k in r_ if k not in PSUMS]
-        wr = list(w) + [k for k in r_ if k in PSUMS]
-        ops.append({"eng": eng, "fn": fn if isinstance(fn, list) else [fn], "r": rd, "w": wr, "ev": None, "dma": False})
+    def R(name, a=0, b=None, step=1, p=(0, 128, 1)):
+        b = SCRATCH[name][1][1] if b is None else b
+        p = p if len(p) == 3 else (p[0], p[1], 1)
+        reg = (ALL, 0, 512, 1) if name in PSUMS else (sum(1 << k for k in range(*p)), a, b, step)
+        return T[name][p[0]:p[1]:p[2], a:b:step], [(name, reg)]
 
-    def dma(eng, pairs, r_=(), w=()):
-        q = {"s": act, "y": g.sync}[eng]
-        s = "dm%d" % ndma[0]
+    def pick(win, off): return win[0].indirect(off[0]), win[1] + off[1]
+    ap = lambda x: x[0] if isinstance(x, tuple) else x
+    SENT = [("sent", (1, 0, 1, 1))]
+
+    def op(eng, fn, ins, outs):
+        rd = sum([x[1] for x in ins if isinstance(x, tuple)], [])
+        wr = sum([x[1] for x in outs], []) + [k for k in rd if k[0] in PSUMS]
+        ops.append({"eng": eng, "fn": fn, "r": [k for k in rd if k[0] not in PSUMS], "w": wr, "ev": None, "dma": False})
+
+    def dma(eng, pairs, after=(), **kw):
+        q = {"s": act, "y": g.sync, "g": g}[eng]
         ndma[0] += 1
-        ops.append({"eng": eng, "fn": [(lambda o=o, i=i: q.dma_start(o, i)) for o, i in pairs], "r": list(r_), "w": list(w),
-                    "ev": (s, 16 * len(pairs)), "dma": True})
+        ops.append({"eng": eng, "fn": [(lambda o=o, i=i: q.dma_start(o[0], i[0], **kw)) for o, i in pairs], "r": sum([i[1] for o, i in pairs], list(after)),
+                    "w": sum([o[1] for o, i in pairs], []), "ev": ("dm%d" % (ndma[0] - 1), 16 * len(pairs)), "dma": True})
 
-    def rot(sb, dr, cs, cd, unit=16, load=True):
+    def rot(sb, a, b, dr, c, unit=16, load=True):
         n, k = 8 * unit, r * unit
-        parts = [(slice(0, n - k), slice(k, n))] + ([(slice(n - k, n), slice(0, k))] if k else [])
-        return [((sb[a, cs], dr[b, cd]) if load else (dr[b, cd], sb[a, cs])) for a, b in parts]
+        parts = [((0, n - k), slice(k, n))] + ([((n - k, n), slice(0, k))] if k else [])
+        pairs = [(R(sb, a, b, 1, p), (dr[q, c:c + b - a], [])) for p, q in parts]
+        return pairs if load else [(y, x) for x, y in pairs]
 
-    def tt(out, a, b, o, r_, w): op("v", lambda: vec.tensor_tensor(out, a, b, o), r_, w)
-    def ts(out, a, s1, o1, r_, w, s2=None, o2=None):
-        if o2 is None: op("v", lambda: vec.tensor_scalar(out, a, s1, None, o1), r_, w)
-        else: op("v", lambda: vec.tensor_scalar(out, a, s1, s2, o1, o2), r_, w)
-    def cp(out, a, r_, w): op("v", lambda: vec.tensor_copy(out, a), r_, w)
-    def ms(out, c, w, r_=()): op("v", lambda: vec.memset(out, c), r_, w)
-    def mm(lst, r_, w): op("t", [(lambda a=a: pe.matmul(*a)) for a in lst], r_, w)
-    def sc(out, a, r_, w, f=AF.Identity, **kw): op("s", lambda: act.activation(out, a, f, **kw), r_, w)
-    def move(eng, out, a, r_, w): (cp if eng == "v" else sc)(out, a, r_, w)
-    def scan(out, a, b, init, o0, o1, r_, w): op("v", lambda: vec.tensor_tensor_scan(out, a, b, init, o0, o1), r_, w)
-    def group(out, terms):
-        return [(out, a, b, j == 0, j == len(terms) - 1) for j, (a, b) in enumerate(terms)]
+    def tt(out, a, b, o): op("v", [lambda: vec.tensor_tensor(out[0], a[0], b[0], o)], [a, b], [out])
+    def ts(out, a, s1, o1, s2=None, o2=None):
+        if o2 is None: op("v", [lambda: vec.tensor_scalar(out[0], a[0], ap(s1), None, o1)], [a, s1], [out])
+        else: op("v", [lambda: vec.tensor_scalar(out[0], a[0], ap(s1), ap(s2), o1, o2)], [a, s1, s2], [out])
+    def cp(out, a): op("v", [lambda: vec.tensor_copy(out[0], a[0])], [a], [out])
+    def ms(out, c): op("v", [lambda: vec.memset(out[0], c)], [], [out])
+    def sc(out, a, f=AF.Identity, bias=0.0, scale=1.0, acc=None):
+        if acc: op("s", [lambda: act.activation(out[0], a[0], f, accum_out=acc[0])], [a], [out, acc])
+        else: op("s", [lambda: act.activation(out[0], a[0], f, bias=ap(bias), scale=ap(scale))], [a, bias, scale], [out])
+    def move(eng, out, a): (cp if eng == "v" else sc)(out, a)
+    def scan(out, a, b, o1): op("v", [lambda: vec.tensor_tensor_scan(out[0], a[0], b[0], 0.0, Op.mult, o1)], [a, b], [out])
+    def mm(terms, start=True, stop=True):
+        n = len(terms) - 1
+        op("t", [(lambda x=x, j=j: pe.matmul(x[0][0], x[1][0], x[2][0], start and j == 0, stop and j == n)) for j, x in enumerate(terms)],
+           [y for x in terms for y in x[1:]], [terms[0][0]])
+    def each(terms):
+        op("t", [(lambda x=x: pe.matmul(x[0][0], x[1][0], x[2][0], True, True)) for x in terms], [y for x in terms for y in x[1:]], [terms[0][0]])
 
     off = topo.mask(core, T.cores[(r + 1) % N])
 
     def send(t):
         direct, hands = routes(r, T, topo)
-        src, wn = T["W%d" % (t % 3)][:, 0:GH], "W%d." % (t % 3)
+        src = R("W%d" % (t % 3), 0, GH)
         on = topo.mask(core, hands[0][0]) & ~off
         trs = [RemoteDMATransfer(dst_ids=dst_ids([T.cores[q] for q in direct], core, topo), dma_engine_mask=off,
-                                 remote_sem=T.sem["ar%d" % t], srcs=[src], dsts=[ghost_slot(T, t, r, q) for q in direct]),
+                                 remote_sem=T.sem["ar%d" % t], srcs=[src[0]], dsts=[ghost_slot(T, t, r, q) for q in direct]),
                RemoteDMATransfer(dst_ids=dst_ids([c for c, via in hands], core, topo), dma_engine_mask=on, remote_sem=T.sem["ha%d" % t],
-                                 srcs=[src], dsts=[T.hl[:, t * GH:(t + 1) * GH] for c in hands])]
+                                 srcs=[src[0]], dsts=[T.hl[:, t * GH:(t + 1) * GH] for c in hands])]
         ops.append({"eng": "g", "fn": [lambda: g.remote_dma_fused(trs, local_sem=T.sem["ls%d" % t])],
-                    "r": [wn + "a", wn + "0"], "w": ["sent"], "ev": ("ls%d" % t, bits(off) + bits(on)), "dma": False})
-        ops.append({"eng": None, "w": [wn + "g"], "ev": ("ar%d" % t, (N - 1) * bits(off))})
-
-    def okeys(t, ks=range(4)): return ["W%d.%s" % (t % 3, k) for k in ks] + (["W%d.a" % (t % 3)] if 0 in ks else [])
-    def wkeys(t): return okeys(t) + ["W%d.g" % (t % 3)]
-    full = slice(0, 128)
-    wd = lambda k: T.WD[:, 128 * k:128 * k + 128]
-    TBK = ["TBi", "TBg"] + ["TB%d" % k for k in range(16)]
+                    "r": src[1], "w": SENT, "ev": ("ls%d" % t, bits(off) + bits(on)), "dma": False})
+        ops.append({"eng": None, "r": [], "w": R("W%d" % (t % 3), V, WW)[1], "ev": ("ar%d" % t, (N - 1) * bits(off))})
 
     def rows(pairs):
-        dma("y", [(T.TB[k::16, 0:V], wd(j)) for k, j in pairs], ["TBi"] + ["WD%d" % j for k, j in pairs], ["TB%d" % k for k, j in pairs])
+        dma("y", [(R("TB", 0, WW, 1, (k, 128, 16)), src) for k, src in pairs])
 
-    I1, I16 = T.I1[:], T.I16[:]
-    c2 = CUTS[2]
-    xi_pieces = lambda ks: sum([rot(T.MX, T.xi, slice(CUTS[k] + CUTS[k + 1], 2 * CUTS[k + 1]), slice(CUTS[k], CUTS[k + 1])) for k in ks], [])
+    g8, s16 = (0, 8), (0, 16)
+    I1, I8, pm = R("I1"), R("I1", 0, 8, 1, g8), R("wc", 4, 5)
+    dig = lambda nm, j, n=128: R(nm, TS * j, TS * j + n)
+    pad = lambda nm, j: R(nm, TS * j + 128, TS * j + TS)
+    half = lambda nm, j: R(nm, 128 * j, 128 * j + 128)
+    born = lambda t, n=128: dig("bn", t, n)
+    col = lambda nm, k, p=(0, 128): R(nm, k, k + 1, 1, p)
+    eye = lambda nm, k: ts(R(nm), R("v1"), 0.0, Op.is_equal, float(k), Op.mult)
+    F0, FH, FL, FQ = [half("PM", j) for j in range(4)]
+    PF, PK, PS, PX = R("PO", 0, 16), R("PO", 16, 17), R("P1", 16, 128), R("PC", 0, 128)
+    P2, P3 = R("P1", 0, 128, 1, g8), R("P0", 0, 128, 1, g8)
+    X = [half("PN", 0), half("PN", 1)]
 
-    dma("y", rot(T.W0, T.x0, slice(0, GH), slice(0, GH)), w=okeys(0, [0]))
-    dma("s", rot(T.adi, T.ad, full, full), w=["adi"])
-    dma("y", rot(T.W0, T.x0, slice(GH, V), slice(GH, V)), w=okeys(0, [1, 2, 3]))
-    dma("s", rot(T.sl, T.lm, slice(0, 137), slice(0, 137), 1) + rot(T.sl, T.sg, slice(144, 281), slice(0, 137), 1), w=["sl"])
-    io_ = lambda out, pat, cm, k: op("g", lambda: g.iota(out, pat, 0, cm, allow_small_or_imprecise_dtypes=True), (), [k])
-    io_(T.v1[:], [[1, 128]], -1, "v1")
-    io_(T.vi[:], [[0, 8], [1, 16]], 0, "vi")
-    io_(T.v2[:], [[16, 8], [0, 16]], -1, "v2")
-    io_(T.vk[:], [[0, 128]], 1, "vk")
+    def opens(W):
+        for a, b, bank, lt in SCA: mm([(R(bank, 0, b - a), R("IN"), R(W, a, b))], stop=False)
+        mm([(PF, I1, R("B0")), (PF, I1, R("MG"))], stop=False)
+        for j, out in enumerate((P2, P3)): mm([(out, R("tu", 8 * j, 8 * j + 8, 1, g8), R("E2", p=g8))], stop=False)
+
+    dma("y", rot("W0", 0, GH, T.x0, 0))
+    dma("s", rot("adi", 0, 128, T.ad, 0))
+    dma("y", rot("W0", GH, V, T.x0, GH))
+    dma("s", rot("sl", 0, 137, T.lm, 0, 1) + rot("sl", 144, 281, T.sg, 0, 1))
+    dma("s", rot("MX", 0, GH, T.xi, 0))
+    io_ = lambda nm, pat, cm: op("g", [lambda: g.iota(T[nm][:], pat, 0, cm, allow_small_or_imprecise_dtypes=True)], [], [R(nm)])
+    io_("v1", [[1, 128]], -1)
+    io_("vi", [[0, 8], [1, 16]], 0)
+    io_("v2", [[16, 8], [0, 16]], -1)
+    io_("v3", [[1, 8], [0, 16]], -1)
+    io_("vc", [[1, 128]], 0)
     send(0)
-    io_(T.v3[:], [[1, 8], [0, 16]], -1, "v3")
-    dma("y", xi_pieces([0, 1]), ["sent"], ["xi0", "xi1"])
-    dma("y", rot(T.xc, T.x0, slice(c2, V), slice(c2, V)), ["sent"], ["xc2", "xc3"])
-    dma("y", xi_pieces([2, 3]), ["sent"], ["xi2", "xi3"])
-    ms(T.ONK[:], KK / 16, ["ONK"]); ms(T.ON16[:], 0.0625, ["ON16"]); ms(T.one[:], 1.0, ["one"])
-    ms(T.wc[:, 8:9], -20.5 * 256, ["wc8"]); ms(T.wc[:, 9:10], 128.0, ["wc9"]); ms(T.nl3[:, 8:9], 1.0, ["nl3b"])
-    ms(T.wc[:, 10:11], -14.5 * 256, ["wc10"]); ms(T.wc[:, 11:12], -BIG, ["wc11"])
-    ms(T.lt[:, 0:GH], 0.0, ["lty"]); ms(T.lt[:, 16 * LATE[0]:16 * LATE[1]], 0.0, ["ltz"], ["lty"])
-    for nm, k in (("I1", 1.0), ("I16", 16.0), ("IN", -1.0)):
-        ts(T[nm][:], T.v1[:], 0.0, Op.is_equal, ["v1"], [nm], k, Op.mult)
-    sc(T.tc1[:], T.v1[:], ["v1", "wc9"], ["tc1"], AF.Sigmoid, bias=T.wc[:, 9:10], scale=256.0)
-    for nm, k in (("IK", KK), ("IB", BIG), ("INB", -BIG), ("I128", 128.0), ("I1920", 1920.0), ("I256", 256.0), ("IN15", -15.0)):
-        sc(T[nm][:], I1, ["I1"], [nm], scale=k)
-    ts(T.M1[:], T.vi[:], 1.0, Op.is_ge, ["vi"], ["M1"])
-    mm([(T.PC[:, 0:1], T.vi[:], T.I1[:, 0:1], True, True)], ["vi", "I1"], ["PC"])
-    ts(T.LE[:], T.v2[:], 0.0, Op.is_le, ["v2"], ["LE"])
-    ts(T.GE[:], T.v2[:], -15.0, Op.is_ge, ["v2"], ["GE"])
-    ts(T.PRE3[:], T.v2[:], -15.0, Op.is_ge, ["v2"], ["PRE3"], 2 * KK, Op.mult)
-    ts(T.EK[:], T.vi[:, 0:16], T.PC[:, 0:1], Op.is_equal, ["vi", "PC"], ["EK"])
-    ts(T.wc[:, 0:1], T.PC[:, 0:1], float(TB_), Op.is_ge, ["PC"], ["wc0"], 0.0625, Op.mult)
-    cp(T.oa1[:], T.adi[:], ["adi"], ["oa1"])
-    ts(T.adt[:, 0:128], T.adi[:], 4, Op.arith_shift_right, ["adi"], ["adt0"])
-    ts(T.adt[:, 128:256], T.adi[:], 15, Op.bitwise_and, ["adi"], ["adt1"])
-    tt(T.BLK[:], T.LE[:], T.GE[:], Op.mult, ["LE", "GE"], ["BLK"])
-    cp(T.WD[:, 0:256], T.adt[:], ["adt0", "adt1"], ["WD0", "WD1"])
-    cp(T.slb[0:8, 0:137], T.sl[0:8, 0:137], ["sl"], ["slb0"])
-    cp(T.slb[0:8, 144:281], T.sl[0:8, 144:281], ["sl"], ["slb1"])
-    mm([(T.PM[:, 0:128], wd(0), I1, True, True), (T.PM[:, 128:256], wd(1), I1, True, True)], ["WD0", "WD1", "I1"], ["PM"])
-    mm([(T.PN[:, 0:8], T.slb[0:8, 0:128], T.I1[0:8, 0:8], True, True), (T.PN[:, 24:32], T.slb[0:8, 144:272], T.I1[0:8, 0:8], True, True),
-        (T.PN[0:9, 64:72], T.slb[0:8, 128:137], T.I1[0:8, 0:8], True, True), (T.PN[0:9, 72:80], T.slb[0:8, 272:281], T.I1[0:8, 0:8], True, True)],
-       ["slb0", "slb1", "I1"], ["PN"])
-    sc(T.A0[:], T.PM[:, 0:256], ["PM"], ["A0"])
-    ts(T.E2[:], T.v3[:], 0.0, Op.is_equal, ["v3"], ["E2"])
-    ts(T.E3[:], T.vk[:], 8.0, Op.is_equal, ["vk"], ["E3"])
-    cp(T.tu[0:9, :], T.PN[0:9, 64:80], ["PN"], ["tu"])
-    mm([(T.PN[:, 8:16], T.E2[0:9, :], T.tu[0:9, 0:8], True, True), (T.PN[:, 16:24], T.E3[0:9, :], T.tu[0:9, 0:8], True, True),
-        (T.PN[:, 32:40], T.E2[0:9, :], T.tu[0:9, 8:16], True, True), (T.PN[:, 40:48], T.E3[0:9, :], T.tu[0:9, 8:16], True, True)],
-       ["tu", "E2", "E3"], ["PN"])
-    ts(T.xm[:, c2:V], T.W0[:, c2:V], -20.0, Op.add, okeys(0), ["xm2", "xm3"])
-    tt(T.TRI[:], T.LE[:], T.tc1[:], Op.mult, ["LE", "tc1"], ["TRI"])
-    ts(T.SELC[:], T.BLK[:, 0::16], 0.15625, Op.mult, ["BLK"], ["SELC"])
-    ts(T.ne[:, 0:16], T.PN[:, 24:40], 2.0, Op.not_equal, ["PN"], ["ne"])
-    ts(T.ne[:, 16:24], T.PN[:, 40:48], 2.0, Op.not_equal, ["PN"], ["ne3"], -1.0, Op.mult)
-    ts(T.ne[:, 24:32], T.PN[:, 40:48], 0.0, Op.is_equal, ["PN"], ["z3"], 99.0, Op.mult)
-    ts(T.LIM[:, 40:48], T.PN[:, 32:40], 0.0, Op.is_equal, ["PN"], ["LIM5"], 99.0, Op.mult)
-    ts(T.mul[:], T.PN[:, 24:32], 0.0, Op.is_equal, ["PN"], ["mul"], -0.5, Op.mult)
-    ts(T.nl3[:, 0:8], T.PN[:, 16:24], -1.0, Op.mult, ["PN"], ["nl3"], -0.5, Op.add)
-    tt(T.LIM[:, 8:16], T.PN[:, 0:8], T.ne[:, 0:8], Op.mult, ["PN", "ne"], ["LIM1"])
-    tt(T.LIM[:, 32:40], T.PN[:, 8:16], T.ne[:, 8:16], Op.mult, ["PN", "ne"], ["LIM4"])
-    tt(T.nL3[:], T.PN[:, 16:24], T.ne[:, 16:24], Op.mult, ["PN", "ne3"], ["nL3"])
-    tt(T.LIM[:, 24:32], T.PN[:, 8:16], T.ne[:, 24:32], Op.add, ["PN", "z3"], ["LIM3"])
-    for a, b, k in ((0, 0, 0), (16, 8, 2)):
-        sc(T.LIM[:, a:a + 8], T.PN[:, b:b + 8], ["PN"], ["LIM%d" % k])
-    for b in range(8):
-        sc(T.M2[:, 16 * b + 1:16 * b + 16], T.M1[:, 1:16], ["M1", "mul"], ["M2c%d" % b], bias=1.0, scale=T.mul[:, b:b + 1])
-    sc(T.M2[:, 0::16], T.M1[:, 0::16], ["M1"], ["M2"])
-    for k in range(4):
-        a, b = CUTS[k] // 16, CUTS[k + 1] // 16
-        sc(T.IS[:, a:b], T.I1[:, a:b], ["I1"], ["IS%d" % k], scale=float(CUTS[k + 1] - CUTS[k]))
-    for k in range(1, 4):
-        ts(T.tc2[:], T.vk[:], float(CUTS[k] // 16), Op.is_ge, ["vk"], ["tc2"], float(CUTS[k - 1] // 16 - CUTS[k] // 16), Op.mult)
-        tt(T.sr[:], T.vk[:] if k == 1 else T.sr[:], T.tc2[:], Op.add, ["vk", "sr", "tc2"], ["sr"])
-    ek = lambda k: T.EK[:, k:k + 1]
-    ts(wd(2), wd(0), 128.0, Op.is_ge, ["WD0"], ["WD2a"], 14.0, Op.mult)
-    ts(T.TB[:, 0:V], T.W0[:, 0:V], 0.0, Op.mult, okeys(0) + ["EK"], ["TBi"], ek(TO), Op.add)
-    sc(wd(2), wd(2), ["WD2a"], ["WD2"], bias=1.0)
-    rows([(TH, 0), (TL, 1), (TW, 2)])
-    ts(T.wc[:, 6:7], ek(TO), 14.0, Op.mult, ["EK"], ["wc6"], ek(TB_), Op.add)
-    ts(T.wc[:, 4:5], ek(TB_), BIG, Op.mult, ["EK"], ["wc4"])
-    ts(T.wc[:, 3:4], ek(TW), 0.0625, Op.mult, ["EK"], ["wc3"], ek(TB_), Op.add)
-    ts(T.gh[:], T.A0[:, 0:128], 128.0, Op.is_ge, ["A0"], ["gh"])
-    ts(T.wc[:, 1:3], T.EK[:, TH:TL + 1], T.wc[:, 4:5], Op.subtract, ["EK", "wc4"], ["wc1", "wc2"])
-    ts(T.TB[:, V:V + 16], T.one[:, 0:16], T.wc[:, 6:7], Op.mult, ["one", "wc6"], ["TBg"])
-    for j in range(4):
-        sc(T.SELM[:, 8 * j:8 * j + 8], T.BLK[:, 0::16], ["BLK", "wc%d" % j], ["SELM%d" % j], scale=T.wc[:, j:j + 1])
-    ts(T.a0w[:], T.adi[:], 16.0, Op.mult, ["adi"], ["a0w"])
-    M2K = ["M2"] + ["M2c%d" % b for b in range(8)]
-    SELK = ["SELM%d" % j for j in range(4)]
-    F0, FU, F3, FB, X = T.PM[:, 0:128], T.PM[:, 128:384], T.PM[:, 384:512], T.PN[:, 0:256], T.PN[:, 256:512]
-    PL, N3, UP, BT, Z = T.PC[:, 128:160], T.PC[:, 160:169], T.P1[:, 384:392], T.P1[:, 256:384], T.P0[:, 0:256]
-    PU, PI = T.P0[:, 0:128], T.PA[:, 384:512]
-    PD = [(T.PA[:, 0:CUTS[1]], "PA"), (T.PB[:, 0:CUTS[2] - CUTS[1]], "PB")]
+    dma("y", rot("xc", GH, A, T.x0, GH), SENT)
+    dma("y", rot("MX", GH, V, T.xi, GH), SENT)
+    ms(col("wc", 1), 128.0); ms(col("wc", 0), -20.5 * 256); ms(col("wc", 2), -256.0); ms(col("wc", 3), -4.0 * 64); ms(col("wc", 5), 16.5 * 256)
+    sc(R("tc1"), R("v1"), AF.Sigmoid, col("wc", 1), 256.0)
+    ms(R("TB"), 0.0)
+    eye("I1", 1); eye("IN", -1)
+    each([(R("PC", 0, 1), R("vi"), col("I1", 0))])
+    ts(R("LE"), R("v2"), 0.0, Op.is_le, 17.0, Op.mult)
+    ts(R("GE"), R("v2"), -15.0, Op.is_ge)
+    ts(R("M1"), R("vi"), 1.0, Op.is_ge)
+    ts(R("E2", p=g8), R("v3", p=g8), 0.0, Op.is_equal)
+    tt(R("BLK"), R("LE"), R("GE"), Op.min)
+    cp(pm, R("PC", 0, 1))
+    cp(R("of1", 0, 128), R("adi"))
+    sc(R("slb", 0, 137, 1, g8), R("sl", 0, 137, 1, g8))
+    sc(R("slb", 144, 281, 1, g8), R("sl", 144, 281, 1, g8))
+    ms(R("lt", MID, END), 0.0)
+    tt(R("EM", p=g8), R("E2", p=g8), R("M1", p=g8), Op.mult)
+    ts(R("pk", 0, 16), R("vi", 0, 16), 16.0, Op.mult, pm, Op.add)
+    ts(R("ne", 0, 137, 1, g8), R("slb", 144, 281, 1, g8), 2.0, Op.not_equal)
+    ts(R("e1", 0, 137, 1, g8), R("slb", 144, 281, 1, g8), 1.0, Op.is_equal)
+    ms(R("one"), 1.0); ms(R("MG"), MAGIC); ms(R("ON9", p=g8), 9 / 64)
+    tt(R("lp", 0, 137, 1, g8), R("slb", 0, 137, 1, g8), R("ne", 0, 137, 1, g8), Op.mult)
+    sc(R("SELC"), R("BLK", 0, 128, 16), scale=0.15625)
+    sc(R("B0"), R("pk", 0, 16), scale=2.0)
+    for j in (2 * GH, 2 * GH + 1, 1): sc(R("M0", j, j - j % 2 + 2 * GH, 2), R("MX", 0, GH))
+    ts(R("xm"), R("W0", 0, A), -20.0, Op.add)
+    each([(R("PN", 8 * j, 8 * j + 8, 1, g8), R(nm, 128, 136, 1, g8), I8) for j, nm in enumerate(("lp", "slb", "e1"))])
+    each([(R("PM", 0, 128), R("e1", 0, 128, 1, g8), R("EM", p=g8))])
+    ts(R("tu", 0, 16, 1, g8), R("PN", 0, 16, 1, g8), -1.0, Op.mult, -0.5, Op.add)
+    ts(R("tu", 16, 24, 1, g8), R("PN", 16, 24, 1, g8), -99.0, Op.mult, 99.0, Op.add)
+    sc(R("MQ"), R("PM", 0, 128))
+    cp(R("xc", 0, GH), R("W0", 0, GH))
+    ts(R("J512"), R("v1", 0, 16), 0.0, Op.is_equal, 512.0, Op.mult)
+    mm([(R("PC", 0, 8), R("slb", 0, 128, 1, g8), I8), (R("PC", 8, 16), R("slb", 0, 128, 1, g8), I8), (R("PC", 8, 16), R("E2", p=g8), R("tu", 16, 24, 1, g8)),
+        (R("PC", 16, 24), R("lp", 0, 128, 1, g8), I8)])
+    opens("W0")
+    tt(R("TRI"), R("LE"), R("tc1"), Op.mult)
+    eye("IB", BIG)
+    sc(R("LIM"), R("PC", 0, 24))
+    sc(R("BC", p=g8), R("E2", p=g8), scale=512.0)
+    ts(col("T3", 0, g8), col("lp", 136, g8), 32.0, Op.mult, -128.0, Op.add)
+    ts(col("T3", 1, g8), col("slb", 136, g8), 32.0, Op.mult, -128.0, Op.add)
+    ts(R("BCS", p=g8), R("E2", p=g8), col("e1", 136, g8), Op.mult)
+    ts(R("EK"), R("vi", 0, 16), pm, Op.is_equal)
+    cp(R("wc", 8, 16), R("BLK", 0, 128, 16))
+    eye("ITS", TS)
+    tt(R("CO", 0, 24, 4), R("EK", TB0, TB0 + 6), R("EK", TB0 - 1, TB0 + 5), Op.add)
+    scan(R("CO", 24, 31), R("one", 0, 7), R("EK", TO, TO + 7), Op.add)
+    ts(R("pk", 16, 22), R("EK", TB0, TB0 + 6), 16.0, Op.mult)
+    for j in (1, 2): ts(R("CO", j, 8, 4), R("one", 0, 2), col("EK", j - 1), Op.mult)
+    ts(col("pk", 24), col("EK", TL), 16.0, Op.mult, col("EK", TW), Op.add)
+    tt(R("CO", 3, 24, 4), R("CO", 25, 31), R("pk", 16, 22), Op.add)
+    for j in (1, 2):
+        ts(R("CO", 8 + j, 24 - j, 4), R("EK", TB0 + 1, TB0 + 6 - j), 256.0, Op.mult, col("EK", j - 1), Op.add)
+    ts(col("CO", 22), col("EK", TB0 + 4), 4096.0, Op.mult, col("pk", 24), Op.add)
+    for j in range(8): sc(R("SELM", j, 32 * (RO - 1), 8), R("CO", 0, 24), scale=col("wc", 8 + j))
+    for k in (2, 3): cp(R("M0", 2 * GH * k, 2 * GH * (k + 1)), R("M0", 2 * GH, 4 * GH))
+    ts(half("adt", 0), R("adi"), 4, Op.arith_shift_right)
+    ts(half("adt", 1), R("adi"), 15, Op.bitwise_and)
+    for j in range(2):
+        ms(pad("A0", j), 0.0)
+        cp(dig("A0", j), half("adt", j))
+    ms(R("OW", 0, 128), 1.0); ms(R("OW", 128, TS), 16.0)
+    rows([(TH, dig("A0", 0, TS)), (TL, dig("A0", 1, TS)), (TO, R("OW"))])
 
-    def offsets(hb, hk, oa, oak):
-        h, l = hb[:, 0:128], hb[:, 128:256]
-        mm(group(T.PO[:, 256:384], [(h, I1), (l, T.I128[:]), (T.gh[:], T.I1920[:])])
-           + (group(T.PO[:, 128:256], [(h, I16), (l, I1)]) if oak else []), [hk, "gh", "I128", "I1920", "I16"], ["PO"])
-        ts(T.ot[:], T.PO[:, 256:384], float(V), Op.min, ["PO"], ["ot"])
-        if oak: cp(oa[:], T.PO[:, 128:256], ["PO"], [oak])
-
-    def base():
-        mm([(T.PO[:, 0:128], T.sr[:], I16, True, False), (T.PO[:, 0:128], T.vi[:], I1, False, False)], ["sr", "vi", "I16", "I1"], ["PO"])
-
-    def own(W, t):
-        for k in (1, 0):
-            mm([(PD[k][0], T.IN[:], W[:, CUTS[k]:CUTS[k + 1]], True, False)], okeys(t, [k]) + ["IN"], [PD[k][1]])
-
-    offsets(T.A0, "A0", None, None)
-    base()
+    def spare(t, k):
+        eyes = lambda *ks: [sc(R(nm), I1, scale=float(c)) for nm, c in ks]
+        zero = lambda nm, j: sc(pad(nm, j), R("one", 0, TS - 128), scale=0.0)
+        if k == 1 and t < RO - 1: zero("bn", t)
+        if (t, k) == (0, 0): eyes(("I16", 16), ("INO", -MO), ("IN16", -16), ("INB", -BIG))
+        if (t, k) == (0, 1): sc(R("t0"), R("adt"), bias=col("wc", 2))
+        if (t, k) == (1, 0): eyes(("IT2", 256 * (TS + 1)), ("I17", 256 * 17), ("IN256", -256), ("I256", 256))
+        if (t, k) == (1, 1): zero("HB", 0), zero("HB", 1)
+        if (t, k) == (2, 0): eyes(("INK", -4096), ("IK17", 4096 * 17))
+        if (t, k) == (3, 0): zero("WR", 0), sc(R("a0w"), R("adi"), scale=16.0)
 
     for t in range(RO):
         last = t == RO - 1
-        Wt, Wn = T["W%d" % (t % 3)], T["W%d" % ((t + 1) % 3)]
-        wn = "W%d." % ((t + 1) % 3)
-        oak, onk = "oa%d" % (t % 2 if t else 1), "oa%d" % ((t + 1) % 2)
-        oa = T[oak]
-        hb, hk = (T.HB, "HB") if t > 1 else (T.A0, "A0")
-        cc, ck = (T.cc, "cc") if t > 1 else (T.one, "one")
-        born, bk = T.bn[:, 128 * t:128 * t + 128], "bn%d" % t
-        wb = 3 + t % 2
+        Wt, Wn = "W%d" % (t % 3), "W%d" % ((t + 1) % 3)
+        of, on_ = "of%d" % (t % 2 if t else 1), "of%d" % ((t + 1) % 2 if t else 1)
+        hb, hn = "HB" if t > 1 else "A0", "HB" if t else "A0"
+        bt = born(t)
+        called = lambda a, b: pick(R(Wt), R(of, a // 16, b // 16))
 
-        def maxg(k, a=None, b=None, j=0):
-            a, b = a or CUTS[k], b or CUTS[k + 1]
-            if a < b:
-                tt(T.MX[:, CUTS[k] + a:CUTS[k] + b], Wt[:, 0:WW].indirect(oa[:, a // 16:b // 16]), T.xc[:, a:b], Op.max,
-                   wkeys(t) + [oak, "xc%d" % k], ["m%d.%d" % (k, j)])
+        def maxg(a, b): tt(R("MX", MO + a, MO + b) if a else R("M0", 0, 2 * GH, 2), called(a, b), R("xc", a, b), Op.max)
+        def select(eng, a, b): move(eng, R(Wn, a, b), pick(R("MX", 0, MO + b) if b > GH else R("M0"), R("osel", a // 16, b // 16)))
+        def count(a, b, lt): each([(R("PC", i, 128, 16, (a // 16, b // 16)), R(lt, a + i, b, 16), R("SELC")) for i in range(16)])
 
-        def select(eng, k, a=None, b=None, key=None):
-            a, b = a or CUTS[k], b or CUTS[k + 1]
-            src = T.MX[:, 2 * CUTS[k]:2 * CUTS[k + 1]].indirect(T.osel[:, a // 16:b // 16])
-            move(eng, Wn[:, a:b], src, ["m%d.%d" % (k, j) for j in range(3)] + ["xi%d" % k, "os%d" % min(k, 1)], [key or wn + str(k)])
-
-        def minus(k):
-            a, b = CUTS[k], CUTS[k + 1]
-            ts(T.xm[:, a:b], Wn[:, a:b], -20.0, Op.add, [wn + str(k)], ["xm%d" % k])
-
-        def count(a, b, r_, lt=T.lt):
-            mm([(T.PC[a:b, i:128:16], lt[:, 16 * a + i:16 * b:16], T.SELC[:], True, True) for i in range(16)], r_ + ["SELC"], ["PC"])
-
-        def low(a, b, key, lt=T.lt):
-            tt(lt[:, 16 * a:16 * b], Wt[:, 0:WW].indirect(oa[:, a:b]), T.xm[:, 16 * a:16 * b], Op.is_lt, wkeys(t) + [oak, "xm2", "xm3"], [key])
-
-        def table(pieces):
-            for e, a, b in pieces:
-                move(e, T.G[:, 16 * a:16 * b], T.TB[:, 0:V + 16].indirect(T.ot[:, a:b]), TBK + ["ot"], ["G%d" % a])
-
-        def fields(a, b):
-            gk = ["G%d" % c for e, c, d in GT if c < b and d > a] + SELK
-            mm([(T.PM[a:b, i:512:16], T.G[:, 16 * a + i:16 * b:16], T.SELM[:], True, True) for i in range(16)], gk, ["PM"])
-
-        def pair(out, a, flag, scale, r_, w):
-            if a is not None: mm([(out, I1, a[:], True, False)], r_, w)
-            else: mm([(out[:, 0:128], scale, flag, False, False), (out[:, 128:256], scale, flag, False, True)], r_, w)
-
-        new = [(TH, hb[:, 0:128]), (TL, hb[:, 128:256]), (TW, T.wl[:])][0 if t > 1 else 2:]
-
-        def digits():
-            a = 128 * new[0][0]
-            mm([(T.P0[:, 128 * k:128 * k + 128], d, I1, True, True) for k, d in new], [hk, "wl"], ["P0"])
-            sc(T.WD[:, a:384], T.P0[:, a:384], ["P0"], ["WD%d" % k for k, _ in new])
-            rows([(k, k) for k, _ in new] + [(TS + t - 1, 7 - wb)])
-
-        most = lambda k: mm(group(PD[k][0], [(I1, Wt[:, CUTS[k]:CUTS[k + 1]]), (I1, T.rl[:, CUTS[k]:CUTS[k + 1]])]), okeys(t, [k]) + ["rl%d" % k], [PD[k][1]])
-        keep1 = lambda: sc(T.MX[:, 2 * CUTS[1]:CUTS[1] + CUTS[2]], PD[1][0], ["PB"], ["m1.0"])
-
-        if t == 0: own(Wt, t)
-        else: pair(FB, hb, None, None, [hk], ["PN"])
-        for k in (1, 0):
-            a, b = CUTS[k], CUTS[k + 1]
-            sc(T.ys[:, a:b], Wt[:, 0:WW].indirect(oa[:, a // 16:b // 16]), wkeys(t) + [oak], ["ys%d" % k])
-            mm([(PD[k][0], I1, T.ys[:, a:b], False, True)], ["ys%d" % k], [PD[k][1]])
-        low(SQ, LATE[0], "ltv")
-        low(LATE[1], 128, "ltw")
-        low(LATE[0], LATE[1], "ltb", T.ltb)
-        for k in (1, 0):
-            sc(T.lt[:, CUTS[1]:c2] if k else T.ltb[:, 0:GH], PD[k][0], [PD[k][1], "wc8"], ["lt%d" % k], AF.Sigmoid, bias=T.wc[:, 8:9], scale=-256.0)
-        count(0, 128, ["ltz", "lt1", "ltv", "ltw"])
-        count(LATE[0], LATE[1], ["ltb"], T.ltb)
-        count(0, GH // 16, ["lt0"], T.ltb)
+        for a, b, bank, lt in SCA:
+            sc(R("ys", a, b), called(a, b))
+            mm([(R(bank, 0, b - a), I1, R("ys", a, b))], start=False)
+        tt(R("lt", 0, A), called(0, A), R("xm"), Op.is_lt)
+        for a, b, bank, lt in SCA: sc(R(lt, a, b), R(bank, 0, b - a), AF.Sigmoid, col("wc", 0), -256.0)
+        count(0, V, "lt")
+        count(MID, END, "ltb")
+        if t > 1: sc(R("ok"), F0, AF.Sigmoid, col("wc", 5), -256.0)
+        maxg(0, GH)
+        maxg(GH, GM)
+        for a, b, bank, lt in SCA[::-1]: sc(R("MX", MO + a, MO + b), R(bank, 0, b - a), AF.Relu)
+        dma("g", [(R("MX", MO + A, MO + V), R(Wt, A, V))], accum_op=Op.add)
+        if t > 0: sc(R("got"), FQ, AF.Sigmoid, col("wc", 3), -64.0)
+        spare(t, 0)
+        if 1 < t and not last: rows([(TH, dig(hb, 0, TS)), (TL, dig(hb, 1, TS))])
+        tt(R("jb"), R("PC", 0, 128), R("ok" if t > 1 else "one"), Op.is_ge)
+        if last: mm([(X[0], R("I256"), dig(hb, 0)), (X[0], R("I16"), dig(hb, 1)), (X[0], R("IK17"), born(t - 1))], stop=False)
+        elif t: mm([(X[j], I1, dig(hb, j)) for j in range(2)] + [(X[j], R("I256"), born(t - 1)) for j in range(2) if t > 1], stop=False)
+        scan(R("nb"), R("M1"), R("jb"), Op.add)
+        for j in range(3): tt(R("d1", 8 * j, 8 * j + 8), R("nb", 15, 128, 16), R("LIM", 8 * j, 8 * j + 8), Op.is_gt)
+        scan(R("qb"), R("MQ"), R("jb"), Op.max)
         if t > 0:
-            ts(T.fb[:], F3, 1.0, Op.is_ge, ["PM"], ["fb"])
-            tt(T.ok[:], F0, cc[:], Op.is_le, ["PM", ck], ["ok"])
-            ts(T.wl[:], F0, 16.0, Op.mult, ["PM"], ["wl"])
-            if last: ts(T.cz[:], F3, 16.0, Op.mult, ["PM"], ["cz"], 15.0, Op.min)
-            pair(FB, None, T.fb[:], T.IB[:], ["fb"], ["PN"])
-        for k in (0, 1):
-            a, b = CUTS[k], CUTS[k + 1]
-            sc(T.rl[:, a:b], PD[k][0], [PD[k][1]], ["rl%d" % k], AF.Relu)
-        most(0)
-        if t > 0: sc(T.t1[:], FB, ["PN", "wc11"], ["t1"], AF.Relu, bias=T.wc[:, 11:12])
-        sc(T.MX[:, 0:CUTS[1]], PD[0][0], ["PA"], ["m0.0"])
-        if 0 < t and not last: digits()
-        tt(T.jb[:], T.PC[:, 0:128], (T.ok if t else T.one)[:], Op.is_ge, ["PC", "ok", "one"], ["cr"])
-        scan(T.nb[:], T.M1[:], T.jb[:], 0.0, Op.mult, Op.add, ["M1", "cr"], ["nb"])
-        tt(T.d1[:], T.nb[:, 15::16], T.LIM[:, 0:8], Op.is_gt, ["nb", "LIM0"], ["d1"])
-        mm([(PL[:, 8 * k:8 * k + 8], (T.TRI if k == 3 else T.BLK)[:], T.d1[:], True, True) for k in range(4)]
-           + [(N3, I1, T.nl3[:, 0:9], True, False)], ["d1", "BLK", "TRI", "nl3", "nl3b"], ["PC"])
-        tt(T.f1[:], T.nb[:, 15::16], T.LIM[:, 8:16], Op.is_gt, ["nb", "LIM1"], ["f1"])
-        mm([(UP, T.IK[:], T.nL3[:], True, False), (UP, T.IB[:], T.f1[:], False, False)], ["IK", "IB", "nL3", "f1"], ["P1"])
-        if last:
-            sc(T.tc2[:], F3, ["PM", "wc10"], ["tc2"], AF.Sigmoid, bias=T.wc[:, 10:11], scale=4096.0)
-        tt(T.l2[:], PL, T.LIM[:, 16:48], Op.is_gt, ["PC", "LIM2", "LIM3", "LIM4", "LIM5"], ["l2"])
-        mm([(N3[:, 0:8], T.ON16[:], T.l2[:, 0:8], False, True)], ["l2", "ON16"], ["PC"])
-        mm([(UP, T.ONK[:], T.l2[:, 0:8], False, False), (UP, T.PRE3[:], T.l2[:, 8:16], False, False),
-            (UP, T.IB[:], T.l2[:, 16:24], False, False), (UP, T.IB[:], T.l2[:, 24:32], False, True)], ["l2", "ONK", "PRE3"], ["P1"])
-        most(1)
-        sc(T.sgn[:, 0:9], N3, ["PC"], ["rk"], AF.Sign, accum_out=T.rk[:, 0:1])
-        if t > 0: tt(T.nA[:], FU, T.t1[:], Op.max, ["PM", "t1"], ["nA"])
-        else: maxg(2, c2, EM)
-        if last: keep1()
-        tt(T.jb[:, 0::16], UP, T.jb[:, 0::16], Op.max, ["P1", "cr"], ["cr"])
-        scan(T.qb[:], T.M2[:], T.jb[:], 0.0, Op.mult, Op.max, M2K + ["cr"], ["qb"])
-        ts(born, T.qb[:], T.rk[:, 0:1], Op.max, ["qb", "rk"], [bk], 0.75, Op.is_ge)
-        mm([(T.PO[:, 0:128], born, T.IS[:], False, True)], [bk] + ["IS%d" % k for k in range(4)], ["PO"])
+            for j, f in enumerate((FH, FL)): tt(half("pr", j), f, R("got"), Op.mult)
+        mm([(P3, R("d1", 0, 8), R("BLK"))], start=False)
+        sc(R("sgn", p=g8), P3, AF.Sign, acc=col("acc", 0, g8))
+        mm([(P2, R("d1", 8 * j, 8 * j + 8), R(nm)) for j, nm in enumerate(("BLK", "TRI", "IB"))], start=False)
+        sc(R("b12", p=g8), P2, AF.Sigmoid, scale=256.0)
+        spare(t, 1)
+        if t >= RO - 2: sc(R("wq"), FQ)
+        mm([(PF, R("qb", p=s16), R("J512", p=s16))], start=False, stop=False)
+        mm([(PX, R("qb"), I1)], stop=False)
+        ts(R("r3", 0, 2, 1, g8), R("T3", 0, 2, 1, g8), col("acc", 0, g8), Op.is_lt)
+        scan(R("pre", p=g8), R("one", p=g8), R("sgn", p=g8), Op.max)
+        maxg(GM, G2)
+        mm([(PK, R("BC", p=g8), col("r3", 0, g8)), (PK, R("ON9", p=g8), col("r3", 1, g8))], start=False, stop=False)
+        mm([(PF, R("BC", p=g8), R("b12", 0, 16, 1, g8))], start=False)
+        mm([(PX, R("BCS", p=g8), R("pre", p=g8)), (PX, R("E2", p=g8), R("b12", p=g8))], start=False)
+        mm([(PS, R("I16"), R("vc", 16, 128))], stop=False)
+        if 0 < t and not last: mm([(X[j], half("pr", j), I1) for j in range(2)], start=False, stop=False)
+        ts(R("osel", 0, 16), PF, PK, Op.add, -MAGIC, Op.add)
+        ts(bt, PX, PK, Op.add, 0.45, Op.is_ge)
         if not last:
-            mm([(BT, born, I1, True, True)], [bk], ["P1"])
-            cp(T.osel[:, 0:16], T.PO[:, 0:16], ["PO"], ["os0"])
-            sc(wd(wb), BT, ["P1"], ["WD%d" % wb])
-            rows([(TB_, wb)])
-            select("v", 0, 0, GH // 2, wn + "a")
-            select("s", 0, GH // 2, GH)
+            rows([(TB0 + t, born(t, TS))])
+            select("v", 0, S0)
+            select("s", S0, GH)
             send(t + 1)
-            cp(T.osel[:, 16:128], T.PO[:, 16:128], ["PO"], ["os1"])
+        mm([(PS, R("INO"), R("bn", TS * t + 16, TS * t + 128))], start=False)
+        if not last:
             if t > 0:
-                pair(Z, T.A0, None, None, ["A0"], ["P0"])
-                pair(Z, None, born, T.IB[:], [bk], ["P0"])
-                pair(X, T.nA, None, None, ["nA"], ["PN"])
-                pair(X, None, born, T.INB[:], [bk, "INB"], ["PN"])
-                if T0S: sc(T.t0[:], Z, ["P0", "wc11"], ["t0"], AF.Relu, bias=T.wc[:, 11:12])
-                else: ts(T.t0[:], Z, -BIG, Op.add, ["P0"], ["t0"], 0.0, Op.max)
-            keep1()
-            select("s", 1)
-            first = FIRST if t else c2
-            maxg(2, EM if t == 0 else c2, first, 1)
+                mm([(X[j], R("INB"), bt) for j in range(2)], start=False)
+                mm([(half("PC", 1), R("IT2"), bt), (half("PC", 0), R("I17"), bt)], stop=False)
+            ts(R("osel", 16, 128), PS, pm, Op.add, float(MO), Op.add)
+            select("s", GH, C1)
             if t > 0:
-                tt(T.HB[:], X, T.t0[:], Op.max, ["PN", "t0"], ["HB"])
-                ts(T.gh[:], T.HB[:, 0:128], 128.0, Op.is_ge, ["HB"], ["gh"])
-            maxg(2, max(first, EM if t == 0 else c2), None, 2)
-            select("s", 2)
-            maxg(3, None, SECOND)
-            if t > 0: offsets(T.HB, "HB", T[onk], onk)
-            base()
-            own(Wn, t + 1)
-            table([p for p in GT[:1] if p[0] == "s"])
-            maxg(3, SECOND, None, 1)
-            select("s", 3)
-            dma("y", [(T.xc[:, c2:V], Wn[:, c2:V])], ["sent", wn + "2", wn + "3"], ["xc2", "xc3"])
-            if t > 0: tt(T.cc[:], F3, born, Op.max, ["PM", bk], ["cc"])
-            table([p for j, p in enumerate(GT) if j or p[0] != "s"])
-            minus(2)
-            minus(3)
-            for a, b in FR: fields(a, b)
+                for j in range(2): tt(dig("HB", j), X[j], half("t0", j), Op.max)
+            h, l = dig(hn, 0), dig(hn, 1)
+            mm([(half("PC", 1), I1, h), (half("PC", 1), R("ITS"), l)] + ([(half("PC", 0), R("I16"), h), (half("PC", 0), I1, l)] if t else []), start=not t)
+            maxg(G2, A)
+            select("v", C1, A)
+            cp(R(on_, 0 if t else 128, 256), R("PC", 0 if t else 128, 256))
+            dma("y", [(R("xc", GH, A), R(Wn, GH, A))], SENT)
+            select("s", A, V)
+            if t == RO - 2:
+                mm([(half("P0", 0), R("wq"), I1), (half("P0", 0), R("got"), R("I16"))])
+                sc(R("WR", 0, 128), half("P0", 0))
+                rows([(TW, R("WR"))])
+            mm([(FQ, R("IN16"), R("one")), (FH, h, R("IN")), (FL, l, R("IN16" if t == RO - 2 else "IN")), (F0, bt, R("IN16"))]
+               + ([(F0, R("I16"), R("got")), (FH, bt, R("IN256")), (FL, bt, R("INK" if t == RO - 2 else "IN256"))] if t else []), stop=False)
+            opens(Wn)
+            ts(R("xm"), R(Wn, 0, A), -20.0, Op.add)
+            cp(R("xc", 0, GH), R(Wn, 0, GH))
+            for e, a, b in (("v", 0, GT), ("s", GT, 128)): move(e, R("G", 16 * a, 16 * b), pick(R("TB"), R(on_, 128 + a, 128 + b)))
+            mm([(R("PM", i, 512, 16), R("G", i, V, 16), R("SELM", 32 * t, 32 * t + 32)) for i in range(16)], start=False)
         else:
-            out = lambda a, b, r_: dma("y", rot(Wn, T.yx, slice(a, b), slice(a, b), load=False), r_=r_)
-            mm([(BT, born, T.IB[:], True, True)], [bk], ["P1"])
-            mm(group(PU, [(hb[:, 0:128], T.I256[:]), (hb[:, 128:256], I16), (T.wl[:], I1), (T.gh[:], T.IN15[:]), (born, T.INB[:])]),
-               [hk, "wl", "gh", "I256", "IN15", "INB"], ["P0"])
-            mm(group(X[:, 0:128], [(T.nA[:, 0:128], T.I256[:]), (T.nA[:, 128:256], I16), (T.cz[:], I1), (T.tc2[:], T.IN15[:]), (born, T.INB[:])]),
-               ["nA", "cz", "tc2", bk], ["PN"])
-            mm(group(PI, [(T.bn[:, 128 * s:128 * s + 128], I1) for s in range(RO)]), [], ["PA"])
-            cp(T.osel[:], T.PO[:, 0:128], ["PO"], ["os0", "os1"])
-            select("s", 0)
-            select("s", 1)
-            out(0, c2, okeys(t + 1, [0, 1]))
-            maxg(2)
-            select("s", 2)
-            sc(T.YI[:], PI, ["PA"], ["YI"], bias=1.0)
-            out(c2, CUTS[3], okeys(t + 1, [2]))
-            maxg(3)
-            select("s", 3, LS, V)
-            tt(T.tw[:], BT, T.a0w[:], Op.min, ["P1", "a0w"], ["tw"])
-            ts(T.YO[:, 128:256], PU, -1.0, Op.max, ["P0"], ["YU"])
-            tt(T.YO[:, 0:128], X[:, 0:128], T.tw[:], Op.max, ["PN", "tw"], ["YA"])
-            dma("y", rot(T.YI, T.yi, full, full, load=False) + rot(T.YO, T.ya, slice(0, 128), full, load=False)
-                + rot(T.YO, T.yu, slice(128, 256), full, load=False), r_=["YI", "YA", "YU"])
-            select("v", 3, CUTS[3], LS, wn + "b")
-            out(CUTS[3], V, okeys(t + 1, [3, "b"]))
+            out = lambda a, b: dma("y", rot(Wn, a, b, T.yx, a, load=False))
+            h, l = dig(hb, 0), dig(hb, 1)
+            PU, PI = half("P0", 0), half("PM", 0)
+            mm([(X[0], half("pr", 0), R("I256")), (X[0], half("pr", 1), I1), (X[0], R("INB"), bt)], start=False)
+            mm([(PU, R("I256"), h), (PU, R("I16"), l), (PU, R("wq"), I1), (PU, R("IK17"), born(t - 1)), (PU, R("got"), R("I16")), (PU, R("INB"), bt)])
+            mm([(PI, I1, born(s)) for s in range(RO)])
+            select("s", 0, GH)
+            ts(R("osel", 16, 128), PS, pm, Op.add, float(MO), Op.add)
+            maxg(G2, A)
+            select("s", GH, C1)
+            out(0, C1)
+            select("v", C1, A)
+            out(C1, A)
+            select("s", A, SL)
+            select("v", SL, V)
+            out(A, V)
+            sc(half("YO", 2), PI, bias=1.0)
+            tt(R("tw"), R("a0w"), bt, Op.mult)
+            ts(half("YO", 1), PU, -1.0, Op.max)
+            tt(half("YO", 0), X[0], R("tw"), Op.max)
+            dma("s", rot("YO", 0, 128, T.ya, 0, load=False) + rot("YO", 128, 256, T.yu, 0, load=False) + rot("YO", 256, 384, T.yi, 0, load=False))
     emit(g, T, ops)

@@ -5,7 +5,7 @@ N, V, GH, RO = 8, 2048, 256, 7
 WW = V + (N - 1) * GH
 TS = WW // 16
 MO = V - GH
-ROUTE = [(True, 1, 1)]
+ROUTE = [(True, 1, 1), (False, 0, 1)]
 A = 1280
 MID = 1536
 END = 1792
@@ -13,7 +13,9 @@ GM = 800
 G2 = 1024
 S0 = 96
 C1 = 896
-SL = 1792
+G3 = 1152
+CL = 896
+SL = 1728
 GT = 62
 SCA = [(A, MID, "PA", "lt"), (END, V, "PB", "lt"), (MID, END, "PN", "ltb")]
 BIG = 1048576.0
@@ -22,7 +24,7 @@ TH, TL, TW, TO, TB0 = 0, 1, 2, 3, 4
 
 B, F, U = "bfloat16", "float32", "uint16"
 SQUARE = ("v1", "v2", "v3", "vi", "vc", "I1", "IN", "I16", "IN16", "ITS", "IB", "INB", "I256", "INO", "IT2", "I17", "IN256", "INK", "IK17",
-          "BLK", "TRI", "LE", "GE", "tc1", "E2", "EM", "BC", "BCS", "ON9", "M1", "MQ", "jb", "nb", "qb", "ok", "got", "wq", "one", "b12", "pre", "sgn")
+          "BLK", "TRI", "LE", "GE", "tc1", "E2", "EM", "BC", "ON9", "M1", "MQ", "jb", "nb", "qb", "ok", "got", "wq", "one", "b12", "sgn", "Z")
 SCRATCH = {
     "W0": ("sbuf", [128, WW], B), "W1": ("sbuf", [128, WW], B), "W2": ("sbuf", [128, WW], B),
     "M0": ("sbuf", [128, 8 * GH], B), "MX": ("sbuf", [128, MO + V], B), "xm": ("sbuf", [128, A], B), "xc": ("sbuf", [128, A], B),
@@ -44,7 +46,7 @@ for _n in SQUARE:
 PSUMS = ("PA", "PB", "P0", "P1", "PC", "PM", "PN", "PO")
 for _p in PSUMS:
     SCRATCH[_p] = ("psum", [128, 512], F)
-SEMAPHORES = (["qv", "qs", "qt", "qg"] + ["dm%d" % k for k in range(48)]
+SEMAPHORES = (["qv", "qs", "qt", "qg"] + ["dm%d" % k for k in range(56)]
               + [a + str(t) for a in ("ar", "ls", "ha") for t in range(RO)])
 
 
@@ -209,11 +211,11 @@ def rank_program(g, core, T, topo):
     def send(t):
         direct, hands = routes(r, T, topo)
         src = R("W%d" % (t % 3), 0, GH)
-        on = topo.mask(core, hands[0][0]) & ~off
+        on = topo.mask(core, hands[0][0]) & ~off if hands else 0
         trs = [RemoteDMATransfer(dst_ids=dst_ids([T.cores[q] for q in direct], core, topo), dma_engine_mask=off,
-                                 remote_sem=T.sem["ar%d" % t], srcs=[src[0]], dsts=[ghost_slot(T, t, r, q) for q in direct]),
-               RemoteDMATransfer(dst_ids=dst_ids([c for c, via in hands], core, topo), dma_engine_mask=on, remote_sem=T.sem["ha%d" % t],
-                                 srcs=[src[0]], dsts=[T.hl[:, t * GH:(t + 1) * GH] for c in hands])]
+                                 remote_sem=T.sem["ar%d" % t], srcs=[src[0]], dsts=[ghost_slot(T, t, r, q) for q in direct])]
+        if hands: trs.append(RemoteDMATransfer(dst_ids=dst_ids([c for c, via in hands], core, topo), dma_engine_mask=on, remote_sem=T.sem["ha%d" % t],
+                                 srcs=[src[0]], dsts=[T.hl[:, t * GH:(t + 1) * GH] for c in hands]))
         ops.append({"eng": "g", "fn": [lambda: g.remote_dma_fused(trs, local_sem=T.sem["ls%d" % t])],
                     "r": src[1], "w": SENT, "ev": ("ls%d" % t, bits(off) + bits(on)), "dma": False})
         ops.append({"eng": None, "r": [], "w": R("W%d" % (t % 3), V, WW)[1], "ev": ("ar%d" % t, (N - 1) * bits(off))})
@@ -221,7 +223,7 @@ def rank_program(g, core, T, topo):
     def rows(pairs):
         dma("y", [(R("TB", 0, WW, 1, (k, 128, 16)), src) for k, src in pairs])
 
-    g8, s16 = (0, 8), (0, 16)
+    g8, r8, k40, s16 = (0, 8), (32, 40), (0, 40), (0, 16)
     I1, I8, pm = R("I1"), R("I1", 0, 8, 1, g8), R("wc", 4, 5)
     dig = lambda nm, j, n=128: R(nm, TS * j, TS * j + n)
     pad = lambda nm, j: R(nm, TS * j + 128, TS * j + TS)
@@ -231,7 +233,7 @@ def rank_program(g, core, T, topo):
     eye = lambda nm, k: ts(R(nm), R("v1"), 0.0, Op.is_equal, float(k), Op.mult)
     F0, FH, FL, FQ = [half("PM", j) for j in range(4)]
     PF, PK, PS, PX = R("PO", 0, 16), R("PO", 16, 17), R("P1", 16, 128), R("PC", 0, 128)
-    P2, P3 = R("P1", 0, 128, 1, g8), R("P0", 0, 128, 1, g8)
+    P2, P3 = R("P1", 0, 128, 1, g8), R("P0", 0, 128, 1, r8)
     X = [half("PN", 0), half("PN", 1)]
 
     def opens(W):
@@ -248,11 +250,16 @@ def rank_program(g, core, T, topo):
     io_("v1", [[1, 128]], -1)
     io_("vi", [[0, 8], [1, 16]], 0)
     io_("v2", [[16, 8], [0, 16]], -1)
-    io_("v3", [[1, 8], [0, 16]], -1)
-    io_("vc", [[1, 128]], 0)
     send(0)
-    dma("y", rot("xc", GH, A, T.x0, GH), SENT)
+    io_("vc", [[1, 128]], 0)
+    dma("y", rot("xc", 0, A, T.x0, 0), SENT)
     dma("y", rot("MX", GH, V, T.xi, GH), SENT)
+    eyes = lambda *ks: [op("g", [lambda nm=nm, c=c: g.affine_select(T[nm][:], T.Z[:], [[-1, 128]], Op.not_equal, float(c), 0, 1)], [R("Z")], [R(nm)]) for nm, c in ks]
+    zero = lambda nm, j: op("g", [lambda: g.iota(pad(nm, j)[0], [[0, TS - 128]], 0, 0, allow_small_or_imprecise_dtypes=True)], [], [pad(nm, j)])
+    ms(R("Z"), 0.0)
+    eyes(("IB", BIG), ("I16", 16), ("INO", -MO))
+    zero("bn", 0)
+    eyes(("ITS", TS), ("IN16", -16))
     ms(col("wc", 1), 128.0); ms(col("wc", 0), -20.5 * 256); ms(col("wc", 2), -256.0); ms(col("wc", 3), -4.0 * 64); ms(col("wc", 5), 16.5 * 256)
     sc(R("tc1"), R("v1"), AF.Sigmoid, col("wc", 1), 256.0)
     ms(R("TB"), 0.0)
@@ -261,9 +268,12 @@ def rank_program(g, core, T, topo):
     ts(R("LE"), R("v2"), 0.0, Op.is_le, 17.0, Op.mult)
     ts(R("GE"), R("v2"), -15.0, Op.is_ge)
     ts(R("M1"), R("vi"), 1.0, Op.is_ge)
-    ts(R("E2", p=g8), R("v3", p=g8), 0.0, Op.is_equal)
     tt(R("BLK"), R("LE"), R("GE"), Op.min)
     cp(pm, R("PC", 0, 1))
+    ts(col("wc", 6), R("PC", 0, 1), 15.0, Op.mult)
+    for nm in ("E2", "b12", "BC", "r3"): ms(R(nm, p=k40), 0.0)
+    ts(R("GE", p=r8), R("v2", p=r8), col("wc", 6, r8), Op.subtract, -32.0, Op.is_equal)
+    ts(R("E2", p=g8), R("v2", p=g8), col("wc", 6, g8), Op.is_equal)
     cp(R("of1", 0, 128), R("adi"))
     sc(R("slb", 0, 137, 1, g8), R("sl", 0, 137, 1, g8))
     sc(R("slb", 144, 281, 1, g8), R("sl", 144, 281, 1, g8))
@@ -272,7 +282,7 @@ def rank_program(g, core, T, topo):
     ts(R("pk", 0, 16), R("vi", 0, 16), 16.0, Op.mult, pm, Op.add)
     ts(R("ne", 0, 137, 1, g8), R("slb", 144, 281, 1, g8), 2.0, Op.not_equal)
     ts(R("e1", 0, 137, 1, g8), R("slb", 144, 281, 1, g8), 1.0, Op.is_equal)
-    ms(R("one"), 1.0); ms(R("MG"), MAGIC); ms(R("ON9", p=g8), 9 / 64)
+    ms(R("one"), 1.0); ms(R("MG"), MAGIC); ms(R("ON9", p=k40), 9 / 64)
     tt(R("lp", 0, 137, 1, g8), R("slb", 0, 137, 1, g8), R("ne", 0, 137, 1, g8), Op.mult)
     sc(R("SELC"), R("BLK", 0, 128, 16), scale=0.15625)
     sc(R("B0"), R("pk", 0, 16), scale=2.0)
@@ -283,21 +293,19 @@ def rank_program(g, core, T, topo):
     ts(R("tu", 0, 16, 1, g8), R("PN", 0, 16, 1, g8), -1.0, Op.mult, -0.5, Op.add)
     ts(R("tu", 16, 24, 1, g8), R("PN", 16, 24, 1, g8), -99.0, Op.mult, 99.0, Op.add)
     sc(R("MQ"), R("PM", 0, 128))
-    cp(R("xc", 0, GH), R("W0", 0, GH))
     ts(R("J512"), R("v1", 0, 16), 0.0, Op.is_equal, 512.0, Op.mult)
     mm([(R("PC", 0, 8), R("slb", 0, 128, 1, g8), I8), (R("PC", 8, 16), R("slb", 0, 128, 1, g8), I8), (R("PC", 8, 16), R("E2", p=g8), R("tu", 16, 24, 1, g8)),
         (R("PC", 16, 24), R("lp", 0, 128, 1, g8), I8)])
     opens("W0")
     tt(R("TRI"), R("LE"), R("tc1"), Op.mult)
-    eye("IB", BIG)
     sc(R("LIM"), R("PC", 0, 24))
+    each([(R("PC", j, j + 1, 1, r8), I8, col(nm, 136, g8)) for j, nm in enumerate(("lp", "slb", "e1"))])
     sc(R("BC", p=g8), R("E2", p=g8), scale=512.0)
-    ts(col("T3", 0, g8), col("lp", 136, g8), 32.0, Op.mult, -128.0, Op.add)
-    ts(col("T3", 1, g8), col("slb", 136, g8), 32.0, Op.mult, -128.0, Op.add)
-    ts(R("BCS", p=g8), R("E2", p=g8), col("e1", 136, g8), Op.mult)
+    sc(R("BC", p=r8), R("GE", p=r8), scale=512.0)
+    ts(R("T3", 0, 2, 1, r8), R("PC", 0, 2, 1, r8), 32.0, Op.mult, -128.0, Op.add)
+    ts(R("E2", p=r8), R("GE", p=r8), R("PC", 2, 3, 1, r8), Op.mult)
     ts(R("EK"), R("vi", 0, 16), pm, Op.is_equal)
     cp(R("wc", 8, 16), R("BLK", 0, 128, 16))
-    eye("ITS", TS)
     tt(R("CO", 0, 24, 4), R("EK", TB0, TB0 + 6), R("EK", TB0 - 1, TB0 + 5), Op.add)
     scan(R("CO", 24, 31), R("one", 0, 7), R("EK", TO, TO + 7), Op.add)
     ts(R("pk", 16, 22), R("EK", TB0, TB0 + 6), 16.0, Op.mult)
@@ -317,16 +325,11 @@ def rank_program(g, core, T, topo):
     ms(R("OW", 0, 128), 1.0); ms(R("OW", 128, TS), 16.0)
     rows([(TH, dig("A0", 0, TS)), (TL, dig("A0", 1, TS)), (TO, R("OW"))])
 
-    def spare(t, k):
-        eyes = lambda *ks: [sc(R(nm), I1, scale=float(c)) for nm, c in ks]
-        zero = lambda nm, j: sc(pad(nm, j), R("one", 0, TS - 128), scale=0.0)
-        if k == 1 and t < RO - 1: zero("bn", t)
-        if (t, k) == (0, 0): eyes(("I16", 16), ("INO", -MO), ("IN16", -16), ("INB", -BIG))
-        if (t, k) == (0, 1): sc(R("t0"), R("adt"), bias=col("wc", 2))
-        if (t, k) == (1, 0): eyes(("IT2", 256 * (TS + 1)), ("I17", 256 * 17), ("IN256", -256), ("I256", 256))
-        if (t, k) == (1, 1): zero("HB", 0), zero("HB", 1)
-        if (t, k) == (2, 0): eyes(("INK", -4096), ("IK17", 4096 * 17))
-        if (t, k) == (3, 0): zero("WR", 0), sc(R("a0w"), R("adi"), scale=16.0)
+    def spare(t):
+        if t < RO - 2: zero("bn", t + 1)
+        if t == 0: eyes(("INB", -BIG), ("IT2", 256 * (TS + 1)), ("I17", 256 * 17), ("IN256", -256), ("I256", 256))
+        if t == 1: zero("HB", 0), zero("HB", 1)
+        if t == 2: eyes(("INK", -4096), ("IK17", 4096 * 17)), zero("WR", 0)
 
     for t in range(RO):
         last = t == RO - 1
@@ -353,7 +356,9 @@ def rank_program(g, core, T, topo):
         for a, b, bank, lt in SCA[::-1]: sc(R("MX", MO + a, MO + b), R(bank, 0, b - a), AF.Relu)
         dma("g", [(R("MX", MO + A, MO + V), R(Wt, A, V))], accum_op=Op.add)
         if t > 0: sc(R("got"), FQ, AF.Sigmoid, col("wc", 3), -64.0)
-        spare(t, 0)
+        if t == 0: sc(R("t0"), R("adt"), bias=col("wc", 2))
+        if t == 2: sc(R("a0w"), R("adi"), scale=16.0)
+        if t == RO - 2: sc(R("wq"), FQ)
         if 1 < t and not last: rows([(TH, dig(hb, 0, TS)), (TL, dig(hb, 1, TS))])
         tt(R("jb"), R("PC", 0, 128), R("ok" if t > 1 else "one"), Op.is_ge)
         if last: mm([(X[0], R("I256"), dig(hb, 0)), (X[0], R("I16"), dig(hb, 1)), (X[0], R("IK17"), born(t - 1))], stop=False)
@@ -364,19 +369,22 @@ def rank_program(g, core, T, topo):
         if t > 0:
             for j, f in enumerate((FH, FL)): tt(half("pr", j), f, R("got"), Op.mult)
         mm([(P3, R("d1", 0, 8), R("BLK"))], start=False)
-        sc(R("sgn", p=g8), P3, AF.Sign, acc=col("acc", 0, g8))
-        mm([(P2, R("d1", 8 * j, 8 * j + 8), R(nm)) for j, nm in enumerate(("BLK", "TRI", "IB"))], start=False)
+        sc(R("sgn", p=r8), P3, AF.Sign, acc=col("acc", 0, r8))
+        for j, nm in enumerate(("BLK", "TRI", "IB")): mm([(P2, R("d1", 8 * j, 8 * j + 8), R(nm))], start=False, stop=j == 2)
         sc(R("b12", p=g8), P2, AF.Sigmoid, scale=256.0)
-        spare(t, 1)
-        if t >= RO - 2: sc(R("wq"), FQ)
+        if t == RO - 2:
+            mm([(half("PA", 0), R("wq"), I1), (half("PA", 0), R("got"), R("I16"))])
+            sc(R("WR", 0, 128), half("PA", 0))
+            rows([(TW, R("WR"))])
+        if last: sc(R("wq"), FQ)
         mm([(PF, R("qb", p=s16), R("J512", p=s16))], start=False, stop=False)
         mm([(PX, R("qb"), I1)], stop=False)
-        ts(R("r3", 0, 2, 1, g8), R("T3", 0, 2, 1, g8), col("acc", 0, g8), Op.is_lt)
-        scan(R("pre", p=g8), R("one", p=g8), R("sgn", p=g8), Op.max)
+        ts(R("r3", 0, 2, 1, r8), R("T3", 0, 2, 1, r8), col("acc", 0, r8), Op.is_lt)
+        scan(R("b12", p=r8), R("one", p=r8), R("sgn", p=r8), Op.max)
         maxg(GM, G2)
-        mm([(PK, R("BC", p=g8), col("r3", 0, g8)), (PK, R("ON9", p=g8), col("r3", 1, g8))], start=False, stop=False)
+        mm([(PK, R("BC", p=k40), col("r3", 0, k40)), (PK, R("ON9", p=k40), col("r3", 1, k40))], start=False, stop=False)
         mm([(PF, R("BC", p=g8), R("b12", 0, 16, 1, g8))], start=False)
-        mm([(PX, R("BCS", p=g8), R("pre", p=g8)), (PX, R("E2", p=g8), R("b12", p=g8))], start=False)
+        mm([(PX, R("E2", p=k40), R("b12", p=k40))], start=False)
         mm([(PS, R("I16"), R("vc", 16, 128))], stop=False)
         if 0 < t and not last: mm([(X[j], half("pr", j), I1) for j in range(2)], start=False, stop=False)
         ts(R("osel", 0, 16), PF, PK, Op.add, -MAGIC, Op.add)
@@ -386,6 +394,7 @@ def rank_program(g, core, T, topo):
             select("v", 0, S0)
             select("s", S0, GH)
             send(t + 1)
+            spare(t)
         mm([(PS, R("INO"), R("bn", TS * t + 16, TS * t + 128))], start=False)
         if not last:
             if t > 0:
@@ -400,17 +409,12 @@ def rank_program(g, core, T, topo):
             maxg(G2, A)
             select("v", C1, A)
             cp(R(on_, 0 if t else 128, 256), R("PC", 0 if t else 128, 256))
-            dma("y", [(R("xc", GH, A), R(Wn, GH, A))], SENT)
+            dma("y", [(R("xc"), R(Wn, 0, A))], SENT)
             select("s", A, V)
-            if t == RO - 2:
-                mm([(half("P0", 0), R("wq"), I1), (half("P0", 0), R("got"), R("I16"))])
-                sc(R("WR", 0, 128), half("P0", 0))
-                rows([(TW, R("WR"))])
             mm([(FQ, R("IN16"), R("one")), (FH, h, R("IN")), (FL, l, R("IN16" if t == RO - 2 else "IN")), (F0, bt, R("IN16"))]
                + ([(F0, R("I16"), R("got")), (FH, bt, R("IN256")), (FL, bt, R("INK" if t == RO - 2 else "IN256"))] if t else []), stop=False)
             opens(Wn)
             ts(R("xm"), R(Wn, 0, A), -20.0, Op.add)
-            cp(R("xc", 0, GH), R(Wn, 0, GH))
             for e, a, b in (("v", 0, GT), ("s", GT, 128)): move(e, R("G", 16 * a, 16 * b), pick(R("TB"), R(on_, 128 + a, 128 + b)))
             mm([(R("PM", i, 512, 16), R("G", i, V, 16), R("SELM", 32 * t, 32 * t + 32)) for i in range(16)], start=False)
         else:
@@ -420,19 +424,23 @@ def rank_program(g, core, T, topo):
             mm([(X[0], half("pr", 0), R("I256")), (X[0], half("pr", 1), I1), (X[0], R("INB"), bt)], start=False)
             mm([(PU, R("I256"), h), (PU, R("I16"), l), (PU, R("wq"), I1), (PU, R("IK17"), born(t - 1)), (PU, R("got"), R("I16")), (PU, R("INB"), bt)])
             mm([(PI, I1, born(s)) for s in range(RO)])
+            names = lambda j, y: dma("y", rot("YO", 128 * j, 128 * j + 128, y, 0, load=False))
             select("s", 0, GH)
+            maxg(G2, G3)
             ts(R("osel", 16, 128), PS, pm, Op.add, float(MO), Op.add)
-            maxg(G2, A)
-            select("s", GH, C1)
-            out(0, C1)
-            select("v", C1, A)
-            out(C1, A)
-            select("s", A, SL)
-            select("v", SL, V)
-            out(A, V)
-            sc(half("YO", 2), PI, bias=1.0)
+            select("s", GH, CL)
             tt(R("tw"), R("a0w"), bt, Op.mult)
-            ts(half("YO", 1), PU, -1.0, Op.max)
             tt(half("YO", 0), X[0], R("tw"), Op.max)
-            dma("s", rot("YO", 0, 128, T.ya, 0, load=False) + rot("YO", 128, 256, T.yu, 0, load=False) + rot("YO", 256, 384, T.yi, 0, load=False))
+            ts(half("YO", 1), PU, -1.0, Op.max)
+            names(0, T.ya), names(1, T.yu)
+            out(0, CL)
+            sc(half("YO", 2), PI, bias=1.0)
+            names(2, T.yi)
+            maxg(G3, A)
+            select("v", CL, A)
+            select("s", A, MID)
+            out(CL, MID)
+            select("s", MID, SL)
+            select("v", SL, V)
+            out(MID, V)
     emit(g, T, ops)

from concourse.bass import DstId, RemoteDMATransfer
from concourse.mybir import AluOpType, ActivationFunctionType

N, V, GH, RO = 8, 2048, 256, 7
WW = V + (N - 1) * GH
TS = WW // 16
MO = V - GH
ROUTE = [(True, 1, 1), (False, 0, 1)]
A = 1280
MID = 1536
END = 1792
GM = 800
G2 = 1024
S0 = 96
C1 = 896
G3 = 1152
CL = 896
SL = 1728
GT = 62
SCA = [(A, MID, "PA", "lt"), (END, V, "PB", "lt"), (MID, END, "PN", "ltb")]
BIG = 1048576.0
MAGIC = 12582912.0
TH, TL, TW, TO, TB0 = 0, 1, 2, 3, 4

B, F, U = "bfloat16", "float32", "uint16"
SQUARE = ("v1", "v2", "v3", "vi", "vc", "I1", "IN", "I16", "IN16", "ITS", "IB", "INB", "I256", "INO", "IT2", "I17", "IN256", "INK", "IK17",
          "BLK", "TRI", "LE", "GE", "tc1", "E2", "EM", "BC", "ON9", "M1", "MQ", "jb", "nb", "qb", "ok", "got", "wq", "one", "b12", "sgn", "Z")
SCRATCH = {
    "W0": ("sbuf", [128, WW], B), "W1": ("sbuf", [128, WW], B), "W2": ("sbuf", [128, WW], B),
    "M0": ("sbuf", [128, 8 * GH], B), "MX": ("sbuf", [128, MO + V], B), "xm": ("sbuf", [128, A], B), "xc": ("sbuf", [128, A], B),
    "lt": ("sbuf", [128, V], B), "ltb": ("sbuf", [128, V], B), "ys": ("sbuf", [128, V], B), "G": ("sbuf", [128, V], B),
    "TB": ("sbuf", [128, WW], B), "bn": ("sbuf", [128, RO * TS], B), "HB": ("sbuf", [128, 2 * TS], B), "A0": ("sbuf", [128, 2 * TS], B),
    "WR": ("sbuf", [128, TS], B), "OW": ("sbuf", [128, TS], B), "t0": ("sbuf", [128, 256], B), "pr": ("sbuf", [128, 256], B),
    "adi": ("sbuf", [128, 128], "int32"), "adt": ("sbuf", [128, 256], "int32"),
    "of0": ("sbuf", [128, 256], U), "of1": ("sbuf", [128, 256], U), "osel": ("sbuf", [128, 128], U),
    "sl": ("sbuf", [128, 288], "int32"), "slb": ("sbuf", [128, 288], B), "lp": ("sbuf", [128, 144], B), "ne": ("sbuf", [128, 144], B),
    "e1": ("sbuf", [128, 144], B), "tu": ("sbuf", [128, 32], B), "T3": ("sbuf", [128, 8], F), "r3": ("sbuf", [128, 8], B),
    "SELC": ("sbuf", [128, 8], B), "SELM": ("sbuf", [128, 32 * (RO - 1)], B), "CO": ("sbuf", [128, 32], F),
    "wc": ("sbuf", [128, 16], F), "EK": ("sbuf", [128, 16], F), "pk": ("sbuf", [128, 32], F), "LIM": ("sbuf", [128, 24], F),
    "d1": ("sbuf", [128, 24], B), "B0": ("sbuf", [128, 16], B), "MG": ("sbuf", [128, 16], B), "J512": ("sbuf", [128, 16], B),
    "acc": ("sbuf", [128, 8], F), "YO": ("sbuf", [128, 384], F), "a0w": ("sbuf", [128, 128], F), "tw": ("sbuf", [128, 128], F),
    "hl": ("sbuf", [128, RO * GH], B),
}
for _n in SQUARE:
    SCRATCH[_n] = ("sbuf", [128, 128], B)
PSUMS = ("PA", "PB", "P0", "P1", "PC", "PM", "PN", "PO")
for _p in PSUMS:
    SCRATCH[_p] = ("psum", [128, 512], F)
SEMAPHORES = (["qv", "qs", "qt", "qg"] + ["dm%d" % k for k in range(56)]
              + [a + str(t) for a in ("ar", "ls", "ha") for t in range(RO)])


def bits(m):
    return bin(m).count("1")


def routes(r, T, topo):
    me = T.cores[r]
    others = [(r + d) % N for d in range(1, N)]
    plane = [q for q in others if topo.same_plane(me, T.cores[q])]
    far = [q for q in others if q not in plane and not topo.mates(me, T.cores[q])]
    free = [c for c in topo.cores_of(me) if T.rank_of(c) is None]
    hands = []
    for other_die, nf, np_ in ROUTE:
        via, far, plane = far[:nf] + plane[:np_], far[nf:], plane[np_:]
        c = [c for c in free if (topo.die(c) != topo.die(me)) == other_die and all(topo.may_write(c, T.cores[q]) for q in via)][0]
        free.remove(c)
        hands.append((c, via))
    mate = [q for q in others if topo.mates(me, T.cores[q])]
    return far + plane + mate, hands


def ghost_slot(T, t, src, dst):
    d = (dst - src) % N
    return T["W%d" % (t % 3)][:, V + (d - 1) * GH:V + d * GH]


def dst_ids(cores, src, topo):
    return [DstId(rid=a[0], pnc=a[1]) for a in [topo.addr(c, src) for c in cores]]


def helper_program(g, core, r, via, T, topo):
    off = topo.mask(core, T.cores[via[0]])
    on = topo.mask(T.cores[r], core) & ~off
    for t in range(RO):
        g.wait_ge(T.sem["ha%d" % t], bits(on))
        g.remote_dma_fused([RemoteDMATransfer(dst_ids=dst_ids([T.cores[q] for q in via], core, topo), dma_engine_mask=off,
                                              remote_sem=T.sem["ar%d" % t], srcs=[T.hl[:, t * GH:(t + 1) * GH]],
                                              dsts=[ghost_slot(T, t, r, q) for q in via])], local_sem=T.sem["ls%d" % t])
    for t in range(RO):
        g.wait_ge(T.sem["ls%d" % t], bits(off))


def emit(g, T, ops):
    queue = {"v": g.vector, "s": g.scalar, "t": g.tensor, "g": g, "y": g.sync}
    clock = {e: {} for e in queue}
    seq = {e: 0 for e in queue}
    wrote, read, need = {}, {}, set()
    meets = lambda a, b: a[0] & b[0] and a[1] < b[2] and b[1] < a[2] and (a[3] != b[3] or (a[1] - b[1]) % a[3] == 0)
    inside = lambda a, b: not a[0] & ~b[0] and b[1] <= a[1] and a[2] <= b[2] and (b[3] == 1 or a[1:] == b[1:])
    for o in ops:
        e = o["eng"]
        deps = []
        for k, reg in o["r"]:
            deps += [ev for x, ev in wrote.get(k, []) if meets(x, reg)]
        for k, reg in o["w"]:
            deps += [ev for x, ev in wrote.get(k, []) + read.get(k, []) if meets(x, reg) and (ev[0] != e or k not in PSUMS)]
        if e is not None:
            best = {}
            for ev in deps:
                if ev[1] > best.get(ev[0], (0, 0))[1]: best[ev[0]] = ev
            evs = list(best.values())
            o["waits"] = [(ev[0], ev[1]) for ev in evs if clock[e].get(ev[0], 0) < ev[1]
                          and not any(x is not ev and x[2].get(ev[0], 0) >= ev[1] for x in evs)]
            for ev in evs:
                for s, n in list(ev[2].items()) + [(ev[0], ev[1])]:
                    if clock[e].get(s, 0) < n: clock[e][s] = n
            need.update(o["waits"])
        if o["ev"] is None:
            seq[e] += 1
            o["seq"] = seq[e]
            ev = (e, seq[e], dict(clock[e]))
        else:
            ev = (o["ev"][0], o["ev"][1], dict(clock[e]) if e else {})
        for k, reg in o["r"]: read.setdefault(k, []).append((reg, ev))
        for k, reg in o["w"]:
            wrote[k] = [x for x in wrote.get(k, []) if not inside(x[0], reg)] + [(reg, ev)]
            read[k] = [x for x in read.get(k, []) if not inside(x[0], reg)]
    count, value = {e: 0 for e in queue}, {}
    for o in ops:
        if o["ev"] is None and (o["eng"], o["seq"]) in need:
            count[o["eng"]] += 1
            value[(o["eng"], o["seq"])] = count[o["eng"]]
    left = {}
    for o in ops:
        e = o["eng"]
        if o["ev"] is not None: left[o["ev"][0]] = (o["ev"][1], e if e in ("s", "y") else "g")
        if e is None: continue
        for s, n in o["waits"]:
            if s in queue: queue[e].wait_ge(T.sem["q" + s], value[(s, n)])
            else: queue[e].wait_ge(T.sem[s], n)
        for j, f in enumerate(o["fn"]):
            ins = f()
            if o["ev"] is None:
                if (e, o["seq"]) in need and j == len(o["fn"]) - 1: ins.then_inc(T.sem["q" + e], 1)
            elif o["dma"]:
                ins.then_inc(T.sem[o["ev"][0]], 16)
    for s, (n, e) in left.items():
        if (s, n) not in need: queue[e].wait_ge(T.sem[s], n)


def rank_program(g, core, T, topo):
    r = T.rank_of(core)
    if r is None:
        for q in range(N):
            for c, via in routes(q, T, topo)[1]:
                if c == core: helper_program(g, core, q, via, T, topo)
        return
    Op, AF = AluOpType, ActivationFunctionType
    vec, act, pe = g.vector, g.scalar, g.tensor
    ops, ndma = [], [0]
    ALL = (1 << 128) - 1

    def R(name, a=0, b=None, step=1, p=(0, 128, 1)):
        b = SCRATCH[name][1][1] if b is None else b
        p = p if len(p) == 3 else (p[0], p[1], 1)
        reg = (ALL, 0, 512, 1) if name in PSUMS else (sum(1 << k for k in range(*p)), a, b, step)
        return T[name][p[0]:p[1]:p[2], a:b:step], [(name, reg)]

    def pick(win, off): return win[0].indirect(off[0]), win[1] + off[1]
    ap = lambda x: x[0] if isinstance(x, tuple) else x
    SENT = [("sent", (1, 0, 1, 1))]

    def op(eng, fn, ins, outs):
        rd = sum([x[1] for x in ins if isinstance(x, tuple)], [])
        wr = sum([x[1] for x in outs], []) + [k for k in rd if k[0] in PSUMS]
        ops.append({"eng": eng, "fn": fn, "r": [k for k in rd if k[0] not in PSUMS], "w": wr, "ev": None, "dma": False})

    def dma(eng, pairs, after=(), **kw):
        q = {"s": act, "y": g.sync, "g": g}[eng]
        ndma[0] += 1
        ops.append({"eng": eng, "fn": [(lambda o=o, i=i: q.dma_start(o[0], i[0], **kw)) for o, i in pairs], "r": sum([i[1] for o, i in pairs], list(after)),
                    "w": sum([o[1] for o, i in pairs], []), "ev": ("dm%d" % (ndma[0] - 1), 16 * len(pairs)), "dma": True})

    def rot(sb, a, b, dr, c, unit=16, load=True):
        n, k = 8 * unit, r * unit
        parts = [((0, n - k), slice(k, n))] + ([((n - k, n), slice(0, k))] if k else [])
        pairs = [(R(sb, a, b, 1, p), (dr[q, c:c + b - a], [])) for p, q in parts]
        return pairs if load else [(y, x) for x, y in pairs]

    def tt(out, a, b, o): op("v", [lambda: vec.tensor_tensor(out[0], a[0], b[0], o)], [a, b], [out])
    def ts(out, a, s1, o1, s2=None, o2=None):
        if o2 is None: op("v", [lambda: vec.tensor_scalar(out[0], a[0], ap(s1), None, o1)], [a, s1], [out])
        else: op("v", [lambda: vec.tensor_scalar(out[0], a[0], ap(s1), ap(s2), o1, o2)], [a, s1, s2], [out])
    def cp(out, a): op("v", [lambda: vec.tensor_copy(out[0], a[0])], [a], [out])
    def ms(out, c): op("v", [lambda: vec.memset(out[0], c)], [], [out])
    def sc(out, a, f=AF.Identity, bias=0.0, scale=1.0, acc=None):
        if acc: op("s", [lambda: act.activation(out[0], a[0], f, accum_out=acc[0])], [a], [out, acc])
        else: op("s", [lambda: act.activation(out[0], a[0], f, bias=ap(bias), scale=ap(scale))], [a, bias, scale], [out])
    def move(eng, out, a): (cp if eng == "v" else sc)(out, a)
    def scan(out, a, b, o1): op("v", [lambda: vec.tensor_tensor_scan(out[0], a[0], b[0], 0.0, Op.mult, o1)], [a, b], [out])
    def mm(terms, start=True, stop=True):
        n = len(terms) - 1
        op("t", [(lambda x=x, j=j: pe.matmul(x[0][0], x[1][0], x[2][0], start and j == 0, stop and j == n)) for j, x in enumerate(terms)],
           [y for x in terms for y in x[1:]], [terms[0][0]])
    def each(terms):
        op("t", [(lambda x=x: pe.matmul(x[0][0], x[1][0], x[2][0], True, True)) for x in terms], [y for x in terms for y in x[1:]], [terms[0][0]])

    off = topo.mask(core, T.cores[(r + 1) % N])

    def send(t):
        direct, hands = routes(r, T, topo)
        src = R("W%d" % (t % 3), 0, GH)
        on = topo.mask(core, hands[0][0]) & ~off if hands else 0
        trs = [RemoteDMATransfer(dst_ids=dst_ids([T.cores[q] for q in direct], core, topo), dma_engine_mask=off,
                                 remote_sem=T.sem["ar%d" % t], srcs=[src[0]], dsts=[ghost_slot(T, t, r, q) for q in direct])]
        if hands: trs.append(RemoteDMATransfer(dst_ids=dst_ids([c for c, via in hands], core, topo), dma_engine_mask=on, remote_sem=T.sem["ha%d" % t],
                                 srcs=[src[0]], dsts=[T.hl[:, t * GH:(t + 1) * GH] for c in hands]))
        ops.append({"eng": "g", "fn": [lambda: g.remote_dma_fused(trs, local_sem=T.sem["ls%d" % t])],
                    "r": src[1], "w": SENT, "ev": ("ls%d" % t, bits(off) + bits(on)), "dma": False})
        ops.append({"eng": None, "r": [], "w": R("W%d" % (t % 3), V, WW)[1], "ev": ("ar%d" % t, (N - 1) * bits(off))})

    def rows(pairs):
        dma("y", [(R("TB", 0, WW, 1, (k, 128, 16)), src) for k, src in pairs])

    g8, r8, k40, s16 = (0, 8), (32, 40), (0, 40), (0, 16)
    I1, I8, pm = R("I1"), R("I1", 0, 8, 1, g8), R("wc", 4, 5)
    dig = lambda nm, j, n=128: R(nm, TS * j, TS * j + n)
    pad = lambda nm, j: R(nm, TS * j + 128, TS * j + TS)
    half = lambda nm, j: R(nm, 128 * j, 128 * j + 128)
    born = lambda t, n=128: dig("bn", t, n)
    col = lambda nm, k, p=(0, 128): R(nm, k, k + 1, 1, p)
    eye = lambda nm, k: ts(R(nm), R("v1"), 0.0, Op.is_equal, float(k), Op.mult)
    F0, FH, FL, FQ = [half("PM", j) for j in range(4)]
    PF, PK, PS, PX = R("PO", 0, 16), R("PO", 16, 17), R("P1", 16, 128), R("PC", 0, 128)
    P2, P3 = R("P1", 0, 128, 1, g8), R("P0", 0, 128, 1, r8)
    X = [half("PN", 0), half("PN", 1)]

    def opens(W):
        for a, b, bank, lt in SCA: mm([(R(bank, 0, b - a), R("IN"), R(W, a, b))], stop=False)
        mm([(PF, I1, R("B0")), (PF, I1, R("MG"))], stop=False)
        for j, out in enumerate((P2, P3)): mm([(out, R("tu", 8 * j, 8 * j + 8, 1, g8), R("E2", p=g8))], stop=False)

    dma("y", rot("W0", 0, GH, T.x0, 0))
    dma("s", rot("adi", 0, 128, T.ad, 0))
    dma("y", rot("W0", GH, V, T.x0, GH))
    dma("s", rot("sl", 0, 137, T.lm, 0, 1) + rot("sl", 144, 281, T.sg, 0, 1))
    dma("s", rot("MX", 0, GH, T.xi, 0))
    io_ = lambda nm, pat, cm: op("g", [lambda: g.iota(T[nm][:], pat, 0, cm, allow_small_or_imprecise_dtypes=True)], [], [R(nm)])
    io_("v1", [[1, 128]], -1)
    io_("vi", [[0, 8], [1, 16]], 0)
    io_("v2", [[16, 8], [0, 16]], -1)
    send(0)
    io_("vc", [[1, 128]], 0)
    dma("y", rot("xc", 0, A, T.x0, 0), SENT)
    dma("y", rot("MX", GH, V, T.xi, GH), SENT)
    eyes = lambda *ks: [op("g", [lambda nm=nm, c=c: g.affine_select(T[nm][:], T.Z[:], [[-1, 128]], Op.not_equal, float(c), 0, 1)], [R("Z")], [R(nm)]) for nm, c in ks]
    zero = lambda nm, j: op("g", [lambda: g.iota(pad(nm, j)[0], [[0, TS - 128]], 0, 0, allow_small_or_imprecise_dtypes=True)], [], [pad(nm, j)])
    ms(R("Z"), 0.0)
    eyes(("IB", BIG), ("I16", 16), ("INO", -MO))
    zero("bn", 0)
    eyes(("ITS", TS), ("IN16", -16))
    ms(col("wc", 1), 128.0); ms(col("wc", 0), -20.5 * 256); ms(col("wc", 2), -256.0); ms(col("wc", 3), -4.0 * 64); ms(col("wc", 5), 16.5 * 256)
    sc(R("tc1"), R("v1"), AF.Sigmoid, col("wc", 1), 256.0)
    ms(R("TB"), 0.0)
    eye("I1", 1); eye("IN", -1)
    each([(R("PC", 0, 1), R("vi"), col("I1", 0))])
    ts(R("LE"), R("v2"), 0.0, Op.is_le, 17.0, Op.mult)
    ts(R("GE"), R("v2"), -15.0, Op.is_ge)
    ts(R("M1"), R("vi"), 1.0, Op.is_ge)
    tt(R("BLK"), R("LE"), R("GE"), Op.min)
    cp(pm, R("PC", 0, 1))
    ts(col("wc", 6), R("PC", 0, 1), 15.0, Op.mult)
    for nm in ("E2", "b12", "BC", "r3"): ms(R(nm, p=k40), 0.0)
    ts(R("GE", p=r8), R("v2", p=r8), col("wc", 6, r8), Op.subtract, -32.0, Op.is_equal)
    ts(R("E2", p=g8), R("v2", p=g8), col("wc", 6, g8), Op.is_equal)
    cp(R("of1", 0, 128), R("adi"))
    sc(R("slb", 0, 137, 1, g8), R("sl", 0, 137, 1, g8))
    sc(R("slb", 144, 281, 1, g8), R("sl", 144, 281, 1, g8))
    ms(R("lt", MID, END), 0.0)
    tt(R("EM", p=g8), R("E2", p=g8), R("M1", p=g8), Op.mult)
    ts(R("pk", 0, 16), R("vi", 0, 16), 16.0, Op.mult, pm, Op.add)
    ts(R("ne", 0, 137, 1, g8), R("slb", 144, 281, 1, g8), 2.0, Op.not_equal)
    ts(R("e1", 0, 137, 1, g8), R("slb", 144, 281, 1, g8), 1.0, Op.is_equal)
    ms(R("one"), 1.0); ms(R("MG"), MAGIC); ms(R("ON9", p=k40), 9 / 64)
    tt(R("lp", 0, 137, 1, g8), R("slb", 0, 137, 1, g8), R("ne", 0, 137, 1, g8), Op.mult)
    sc(R("SELC"), R("BLK", 0, 128, 16), scale=0.15625)
    sc(R("B0"), R("pk", 0, 16), scale=2.0)
    for j in (2 * GH, 2 * GH + 1, 1): sc(R("M0", j, j - j % 2 + 2 * GH, 2), R("MX", 0, GH))
    ts(R("xm"), R("W0", 0, A), -20.0, Op.add)
    each([(R("PN", 8 * j, 8 * j + 8, 1, g8), R(nm, 128, 136, 1, g8), I8) for j, nm in enumerate(("lp", "slb", "e1"))])
    each([(R("PM", 0, 128), R("e1", 0, 128, 1, g8), R("EM", p=g8))])
    ts(R("tu", 0, 16, 1, g8), R("PN", 0, 16, 1, g8), -1.0, Op.mult, -0.5, Op.add)
    ts(R("tu", 16, 24, 1, g8), R("PN", 16, 24, 1, g8), -99.0, Op.mult, 99.0, Op.add)
    sc(R("MQ"), R("PM", 0, 128))
    ts(R("J512"), R("v1", 0, 16), 0.0, Op.is_equal, 512.0, Op.mult)
    mm([(R("PC", 0, 8), R("slb", 0, 128, 1, g8), I8), (R("PC", 8, 16), R("slb", 0, 128, 1, g8), I8), (R("PC", 8, 16), R("E2", p=g8), R("tu", 16, 24, 1, g8)),
        (R("PC", 16, 24), R("lp", 0, 128, 1, g8), I8)])
    opens("W0")
    tt(R("TRI"), R("LE"), R("tc1"), Op.mult)
    sc(R("LIM"), R("PC", 0, 24))
    each([(R("PC", j, j + 1, 1, r8), I8, col(nm, 136, g8)) for j, nm in enumerate(("lp", "slb", "e1"))])
    sc(R("BC", p=g8), R("E2", p=g8), scale=512.0)
    sc(R("BC", p=r8), R("GE", p=r8), scale=512.0)
    ts(R("T3", 0, 2, 1, r8), R("PC", 0, 2, 1, r8), 32.0, Op.mult, -128.0, Op.add)
    ts(R("E2", p=r8), R("GE", p=r8), R("PC", 2, 3, 1, r8), Op.mult)
    ts(R("EK"), R("vi", 0, 16), pm, Op.is_equal)
    cp(R("wc", 8, 16), R("BLK", 0, 128, 16))
    tt(R("CO", 0, 24, 4), R("EK", TB0, TB0 + 6), R("EK", TB0 - 1, TB0 + 5), Op.add)
    scan(R("CO", 24, 31), R("one", 0, 7), R("EK", TO, TO + 7), Op.add)
    ts(R("pk", 16, 22), R("EK", TB0, TB0 + 6), 16.0, Op.mult)
    for j in (1, 2): ts(R("CO", j, 8, 4), R("one", 0, 2), col("EK", j - 1), Op.mult)
    ts(col("pk", 24), col("EK", TL), 16.0, Op.mult, col("EK", TW), Op.add)
    tt(R("CO", 3, 24, 4), R("CO", 25, 31), R("pk", 16, 22), Op.add)
    for j in (1, 2):
        ts(R("CO", 8 + j, 24 - j, 4), R("EK", TB0 + 1, TB0 + 6 - j), 256.0, Op.mult, col("EK", j - 1), Op.add)
    ts(col("CO", 22), col("EK", TB0 + 4), 4096.0, Op.mult, col("pk", 24), Op.add)
    for j in range(8): sc(R("SELM", j, 32 * (RO - 1), 8), R("CO", 0, 24), scale=col("wc", 8 + j))
    for k in (2, 3): cp(R("M0", 2 * GH * k, 2 * GH * (k + 1)), R("M0", 2 * GH, 4 * GH))
    ts(half("adt", 0), R("adi"), 4, Op.arith_shift_right)
    ts(half("adt", 1), R("adi"), 15, Op.bitwise_and)
    for j in range(2):
        ms(pad("A0", j), 0.0)
        cp(dig("A0", j), half("adt", j))
    ms(R("OW", 0, 128), 1.0); ms(R("OW", 128, TS), 16.0)
    rows([(TH, dig("A0", 0, TS)), (TL, dig("A0", 1, TS)), (TO, R("OW"))])

    def spare(t):
        if t < RO - 2: zero("bn", t + 1)
        if t == 0: eyes(("INB", -BIG), ("IT2", 256 * (TS + 1)), ("I17", 256 * 17), ("IN256", -256), ("I256", 256))
        if t == 1: zero("HB", 0), zero("HB", 1)
        if t == 2: eyes(("INK", -4096), ("IK17", 4096 * 17)), zero("WR", 0)

    for t in range(RO):
        last = t == RO - 1
        Wt, Wn = "W%d" % (t % 3), "W%d" % ((t + 1) % 3)
        of, on_ = "of%d" % (t % 2 if t else 1), "of%d" % ((t + 1) % 2 if t else 1)
        hb, hn = "HB" if t > 1 else "A0", "HB" if t else "A0"
        bt = born(t)
        called = lambda a, b: pick(R(Wt), R(of, a // 16, b // 16))

        def maxg(a, b): tt(R("MX", MO + a, MO + b) if a else R("M0", 0, 2 * GH, 2), called(a, b), R("xc", a, b), Op.max)
        def select(eng, a, b): move(eng, R(Wn, a, b), pick(R("MX", 0, MO + b) if b > GH else R("M0"), R("osel", a // 16, b // 16)))
        def count(a, b, lt): each([(R("PC", i, 128, 16, (a // 16, b // 16)), R(lt, a + i, b, 16), R("SELC")) for i in range(16)])

        for a, b, bank, lt in SCA:
            sc(R("ys", a, b), called(a, b))
            mm([(R(bank, 0, b - a), I1, R("ys", a, b))], start=False)
        tt(R("lt", 0, A), called(0, A), R("xm"), Op.is_lt)
        for a, b, bank, lt in SCA: sc(R(lt, a, b), R(bank, 0, b - a), AF.Sigmoid, col("wc", 0), -256.0)
        count(0, V, "lt")
        count(MID, END, "ltb")
        if t > 1: sc(R("ok"), F0, AF.Sigmoid, col("wc", 5), -256.0)
        maxg(0, GH)
        maxg(GH, GM)
        for a, b, bank, lt in SCA[::-1]: sc(R("MX", MO + a, MO + b), R(bank, 0, b - a), AF.Relu)
        dma("g", [(R("MX", MO + A, MO + V), R(Wt, A, V))], accum_op=Op.add)
        if t > 0: sc(R("got"), FQ, AF.Sigmoid, col("wc", 3), -64.0)
        if t == 0: sc(R("t0"), R("adt"), bias=col("wc", 2))
        if t == 2: sc(R("a0w"), R("adi"), scale=16.0)
        if t == RO - 2: sc(R("wq"), FQ)
        if 1 < t and not last: rows([(TH, dig(hb, 0, TS)), (TL, dig(hb, 1, TS))])
        tt(R("jb"), R("PC", 0, 128), R("ok" if t > 1 else "one"), Op.is_ge)
        if last: mm([(X[0], R("I256"), dig(hb, 0)), (X[0], R("I16"), dig(hb, 1)), (X[0], R("IK17"), born(t - 1))], stop=False)
        elif t: mm([(X[j], I1, dig(hb, j)) for j in range(2)] + [(X[j], R("I256"), born(t - 1)) for j in range(2) if t > 1], stop=False)
        scan(R("nb"), R("M1"), R("jb"), Op.add)
        for j in range(3): tt(R("d1", 8 * j, 8 * j + 8), R("nb", 15, 128, 16), R("LIM", 8 * j, 8 * j + 8), Op.is_gt)
        scan(R("qb"), R("MQ"), R("jb"), Op.max)
        if t > 0:
            for j, f in enumerate((FH, FL)): tt(half("pr", j), f, R("got"), Op.mult)
        mm([(P3, R("d1", 0, 8), R("BLK"))], start=False)
        sc(R("sgn", p=r8), P3, AF.Sign, acc=col("acc", 0, r8))
        for j, nm in enumerate(("BLK", "TRI", "IB")): mm([(P2, R("d1", 8 * j, 8 * j + 8), R(nm))], start=False, stop=j == 2)
        sc(R("b12", p=g8), P2, AF.Sigmoid, scale=256.0)
        if t == RO - 2:
            mm([(half("PA", 0), R("wq"), I1), (half("PA", 0), R("got"), R("I16"))])
            sc(R("WR", 0, 128), half("PA", 0))
            rows([(TW, R("WR"))])
        if last: sc(R("wq"), FQ)
        mm([(PF, R("qb", p=s16), R("J512", p=s16))], start=False, stop=False)
        mm([(PX, R("qb"), I1)], stop=False)
        ts(R("r3", 0, 2, 1, r8), R("T3", 0, 2, 1, r8), col("acc", 0, r8), Op.is_lt)
        scan(R("b12", p=r8), R("one", p=r8), R("sgn", p=r8), Op.max)
        maxg(GM, G2)
        mm([(PK, R("BC", p=k40), col("r3", 0, k40)), (PK, R("ON9", p=k40), col("r3", 1, k40))], start=False, stop=False)
        mm([(PF, R("BC", p=g8), R("b12", 0, 16, 1, g8))], start=False)
        mm([(PX, R("E2", p=k40), R("b12", p=k40))], start=False)
        mm([(PS, R("I16"), R("vc", 16, 128))], stop=False)
        if 0 < t and not last: mm([(X[j], half("pr", j), I1) for j in range(2)], start=False, stop=False)
        ts(R("osel", 0, 16), PF, PK, Op.add, -MAGIC, Op.add)
        ts(bt, PX, PK, Op.add, 0.45, Op.is_ge)
        if not last:
            rows([(TB0 + t, born(t, TS))])
            select("v", 0, S0)
            select("s", S0, GH)
            send(t + 1)
            spare(t)
        mm([(PS, R("INO"), R("bn", TS * t + 16, TS * t + 128))], start=False)
        if not last:
            if t > 0:
                mm([(X[j], R("INB"), bt) for j in range(2)], start=False)
                mm([(half("PC", 1), R("IT2"), bt), (half("PC", 0), R("I17"), bt)], stop=False)
            ts(R("osel", 16, 128), PS, pm, Op.add, float(MO), Op.add)
            select("s", GH, C1)
            if t > 0:
                for j in range(2): tt(dig("HB", j), X[j], half("t0", j), Op.max)
            h, l = dig(hn, 0), dig(hn, 1)
            mm([(half("PC", 1), I1, h), (half("PC", 1), R("ITS"), l)] + ([(half("PC", 0), R("I16"), h), (half("PC", 0), I1, l)] if t else []), start=not t)
            maxg(G2, A)
            select("v", C1, A)
            cp(R(on_, 0 if t else 128, 256), R("PC", 0 if t else 128, 256))
            dma("y", [(R("xc"), R(Wn, 0, A))], SENT)
            select("s", A, V)
            mm([(FQ, R("IN16"), R("one")), (FH, h, R("IN")), (FL, l, R("IN16" if t == RO - 2 else "IN")), (F0, bt, R("IN16"))]
               + ([(F0, R("I16"), R("got")), (FH, bt, R("IN256")), (FL, bt, R("INK" if t == RO - 2 else "IN256"))] if t else []), stop=False)
            opens(Wn)
            ts(R("xm"), R(Wn, 0, A), -20.0, Op.add)
            for e, a, b in (("v", 0, GT), ("s", GT, 128)): move(e, R("G", 16 * a, 16 * b), pick(R("TB"), R(on_, 128 + a, 128 + b)))
            mm([(R("PM", i, 512, 16), R("G", i, V, 16), R("SELM", 32 * t, 32 * t + 32)) for i in range(16)], start=False)
        else:
            out = lambda a, b: dma("y", rot(Wn, a, b, T.yx, a, load=False))
            h, l = dig(hb, 0), dig(hb, 1)
            PU, PI = half("P0", 0), half("PM", 0)
            mm([(X[0], half("pr", 0), R("I256")), (X[0], half("pr", 1), I1), (X[0], R("INB"), bt)], start=False)
            mm([(PU, R("I256"), h), (PU, R("I16"), l), (PU, R("wq"), I1), (PU, R("IK17"), born(t - 1)), (PU, R("got"), R("I16")), (PU, R("INB"), bt)])
            mm([(PI, I1, born(s)) for s in range(RO)])
            names = lambda j, y: dma("y", rot("YO", 128 * j, 128 * j + 128, y, 0, load=False))
            select("s", 0, GH)
            maxg(G2, G3)
            ts(R("osel", 16, 128), PS, pm, Op.add, float(MO), Op.add)
            select("s", GH, CL)
            tt(R("tw"), R("a0w"), bt, Op.mult)
            tt(half("YO", 0), X[0], R("tw"), Op.max)
            ts(half("YO", 1), PU, -1.0, Op.max)
            names(0, T.ya), names(1, T.yu)
            out(0, CL)
            sc(half("YO", 2), PI, bias=1.0)
            names(2, T.yi)
            maxg(G3, A)
            select("v", CL, A)
            select("s", A, MID)
            out(CL, MID)
            select("s", MID, SL)
            select("v", SL, V)
            out(MID, V)
    emit(g, T, ops)
